import numpy as np, ml_dtypes
CORES = [9,25,41,57]
N = 4
import mx_ref
BF = ml_dtypes.bfloat16
def gentries(a):
    return np.ascontiguousarray(a.reshape(8, 16, -1).transpose(0, 2, 1)).reshape(8, -1)
def gtable(e):
    e = np.asarray(e); return np.ascontiguousarray(e.reshape(8, -1, 16).transpose(0, 2, 1)).reshape(128, -1).astype(np.int32)
def gcols(t, e):
    v = np.concatenate([t.reshape(8, 16, -1, 4), np.zeros((8, 16, 1, 4), BF)], axis=2)
    return np.ascontiguousarray(np.stack([v[g][:, e[g]] for g in range(8)])).reshape(128, -1)
def gpick(z, e):
    return np.concatenate([z[16 * g:16 * g + 16][:, e[g]] for g in range(8)])
def tile(rs):
    return np.stack(rs, axis=2).reshape(128, -1).astype(BF)
def pick(q, e):
    c = np.concatenate([q[0].reshape(128, -1, 4), np.zeros((128, 1, 4), np.uint8)], axis=1); s = np.concatenate([q[1], np.ones((16, 1), np.uint8)], axis=1)
    return (np.ascontiguousarray(c[:, e].reshape(128, -1)), np.ascontiguousarray(s[:, e]))
def join(*qs):
    return (np.concatenate([q[0] for q in qs], axis=1), np.concatenate([q[1] for q in qs], axis=1))
def put(q, e, v):
    c, s = q[0].reshape(128, -1, 4).copy(), q[1].copy(); c[:, e] = v[0].reshape(128, -1, 4); s[:, e] = v[1]
    return (c.reshape(128, -1), s)
def pk(c, s):
    return (np.ascontiguousarray(c), mx_ref.live(s))
def emit(q):
    return q[0], q[1]
def packed(v, rng):
    q = [mx_ref.quantize(np.ascontiguousarray(v[r])) for r in range(N)]
    return np.stack([a for a, b in q]), np.stack([mx_ref.plane(b, rng) for a, b in q])
def values_of_codes():
    e, c = np.zeros((128, 128, 4), np.float32), np.zeros((128, 2, 4), np.uint8)
    e[np.arange(128), np.arange(128), 0] = 1
    c[:127, :, 0] = np.arange(256).reshape(2, 128).T[:127]
    return mx_ref.matmul(mx_ref.quantize(e.reshape(128, 512).astype(BF)), (c.reshape(128, 8), np.full((16, 2), 127, np.uint8))).T.reshape(-1).astype(np.float64)
CODE_VALUE, SCALE_VALUE = values_of_codes(), 2.0 ** (np.arange(256) - 127.0)
def decode(q):
    return (CODE_VALUE[q[0]].reshape(16, 8, -1, 4) * SCALE_VALUE[q[1]][:, None, :, None] + 0.0).reshape(128, -1).astype(np.float32)
def f(rng, *shape):
    return mx_ref.flush((rng.standard_normal(shape, dtype=np.float32) * np.exp2(rng.integers(-2, 3, shape[:-1] + (1,)))).astype(BF))
def wide(rng, *shape, cols=0):
    v = rng.standard_normal(shape, dtype=np.float32) * np.exp2(rng.integers(-12, 13, shape)).astype(np.float32)
    if cols: v *= np.repeat(np.exp2(rng.integers(-cols, cols + 1, shape[:-2] + (1, shape[-1] // 4))) * (rng.random(shape[:-2] + (1, shape[-1] // 4)) > 0.0625), 4, axis=-1).astype(np.float32)
    return mx_ref.flush(v.astype(BF))
C, H = 448, 224
STEP = [1, 2, 3]
G, OWN = np.arange(8)[:, None], np.tile(np.arange(C), (8, 1))
def numbers_of(rng):
    return {"x": np.array(f(rng, N, 128, 4 * C)), "u": np.array(f(rng, N, 128, 512)), "v": np.array(f(rng, N, 128, 512))}
def stored(a, m):
    return {"fl": np.stack([gtable(a[r]) for r in range(N)]), "ml": np.stack([gtable(m[r]) for r in range(N)])}
def pairs(o):
    m = np.zeros(o.shape, np.int64)
    np.put_along_axis(m, o[..., ::2], o[..., 1::2], axis=-1)
    np.put_along_axis(m, o[..., 1::2], o[..., ::2], axis=-1)
    return m
def ring(o):
    a = np.zeros(C, np.int64)
    a[o] = np.roll(o, -1)
    return a
def lists(rng):
    e = np.tile(np.arange(C), (N, 8, 1))
    return rng.permuted(e, axis=2), pairs(rng.permuted(e, axis=2))
def layers(rng, still=[]):
    w = np.array(f(rng, N, 128, 2048)).reshape(N, 8, 16, 4, 8, 16, 4)
    for i in still:
        w[:, :, i] = 0
        w[:, :, :, :, :, i] = 0
    return w
def weights(rng, w):
    c, s = packed(np.ascontiguousarray(w).reshape(N, 128, 2048), rng)
    return {"wc": c, "ws": s}
def parity():
    i = np.arange(N)
    return (i ^ (i >> 1) ^ (i >> 2)) % 2
def setup_inputs(rng):
    return {**numbers_of(rng), **stored(*lists(rng)), **weights(rng, layers(rng))}
def setup_inputs_ties(rng):
    d = numbers_of(rng)
    o = rng.permutation(N)
    k = rng.integers(0, 4, (N, 8, C))
    k[o[1]] += 1
    k[o[2], rng.permutation(8)[:4]] = 1
    a, m = lists(rng)
    g = int(rng.integers(8))
    a[:, g] = np.arange(C)
    m[:, g] = (np.arange(C) + H) % C
    k[o[3], g] = np.arange(C) >= H
    x = d["x"].reshape(N, 8, 16, C, 4)
    x[:, :, 0] = 0
    x[:, :, 0, :, 0] = k.astype(np.float32).astype(BF)
    u = d["u"].reshape(N, 128, 128, 4)
    u[:, :, ::16] = 0
    for r in range(N):
        for h in range(0, 128, 16): u[r, h, h, 0] = 0.0 if r == o[0] else -1.0 if r == o[1] else 1.0
    return {"x": x.reshape(N, 128, 4 * C), "u": u.reshape(N, 128, 512), "v": d["v"], **stored(a, m), **weights(rng, layers(rng, [0]))}
def setup_inputs_near(rng):
    d = numbers_of(rng)
    x = d["x"].astype(np.float32).reshape(N, 8, 16, C, 4)
    x[:, :, 0] = 0
    x[:, :, 8:] = 0
    x[:, :, 15, :, 0] = 2.0 ** -26
    u = d["u"].reshape(N, 128, 128, 4)
    u[:, :, ::16] = 0
    o = rng.permutation(N) % 4
    for r in range(N):
        c = rng.choice([-1.0, 1.0], (8, 1))
        s = rng.integers(0, 16, (8, C))
        digits = ((s[:, :, None] >> np.arange(4)) & 1) * np.exp2(np.arange(4) - 23.0)
        if o[r] < 2:
            x[r, :, 0, :, 0] = c
            x[r, :, 8] = digits
            x[r, :, 11, :, 0] = 2.0 ** -10
        elif o[r] == 2: x[r, :, 8] = digits * rng.choice([-1.0, 1.0], (8, C, 1))
        else:
            x[r, :, 8, :, 0] = np.where(s < 8, 1.25, 0.0) * 2.0 ** -30 * c
            x[r, :, 9, :, 0] = np.where(s < 8, 0.0, 1.125) * 2.0 ** -30 * c
            for g in rng.permutation(8)[:4]:
                e = rng.choice([-1.0, 1.0], C) * 2.0 ** -30
                x[r, g, 8, :, 0] = 1.25 * e
                x[r, g, 9, :, 0] = -1.125 * e
            x[r, :, 13, :, 0] = rng.choice([-1.0, 1.0], (8, C)) * 2.0 ** -30
        at = [0, C - 1, int(rng.integers(C)), int(rng.integers(C))]
        for g, j in zip(rng.permutation(8)[:4], at): x[r, g, 0, j, 0] = 2.0 ** 29 * rng.choice([-1.0, 1.0])
        k = 1.0 if o[r] == 0 else 2.0 ** -30
        for h in range(0, 128, 16):
            u[r, h, h, 0] = k if o[r] < 2 else 1.0
            if o[r] < 2: u[r, h + 11, h, 0] = k
            if o[r] < 3: u[r, h + 8, h] = k
            else:
                u[r, h + 8, h, 0] = k
                u[r, h + 9, h, 0] = 1.125 * k
                u[r, h + 14, h, 0] = k
    w = layers(rng, [0, 8, 9, 10, 11, 12, 13, 14, 15])
    for g in range(8): w[:, g, 13, 0, g, 14, 0] = 2.0 ** -5
    return {"x": x.reshape(N, 128, 4 * C).astype(BF), "u": u.reshape(N, 128, 512), "v": d["v"], **stored(*lists(rng)), **weights(rng, w)}
def setup_inputs_odd(rng):
    d = numbers_of(rng)
    x = (1.0 + (2 * rng.integers(0, 64, (N, 16, 8, C, 4)) + 1) * 2.0 ** -7) * np.exp2(-rng.integers(0, 7, (N, 16, 8, C, 4)).astype(np.float64)) * rng.choice([-1.0, 1.0], (N, 16, 8, C, 4))
    x[:, :, 0, :, 0] = (np.where((parity()[:, None] + np.arange(16)) % 2 == 0, 1.96875, 1.875) * 2.0 ** 8)[:, :, None]
    x[:, :, 1, :, 0] = rng.integers(8, 16, (N, 16, C)) * 2.0 ** -8
    u = d["u"].reshape(N, 16, 8, 128, 4)
    u[:, :, 0, ::16] = 0
    for r in range(N):
        for g in rng.permutation(8)[:2]:
            u[r, :, :, 16 * g] = 0
            u[r, 2 * g + parity()[r], 1, 16 * g, 0] = 1.0
    w = layers(rng, [0, 1, 8, 9])
    for g in range(8):
        for i in (0, 8): w[:, g, i, 0, g, i, 0] = -0.5
    return {"x": x.astype(np.float32).reshape(N, 128, 4 * C).astype(BF), "u": u.reshape(N, 128, 512), "v": d["v"], **stored(*lists(rng)), **weights(rng, w)}
def setup_inputs_ends(rng):
    d = numbers_of(rng)
    r0 = int(rng.integers(N))
    a = rng.permutation(np.array([r0, r0 ^ STEP[0], r0 ^ STEP[1], r0 ^ STEP[0] ^ STEP[1]]))
    z = rng.permutation(np.setdiff1d(np.arange(N), a))
    x = np.where(rng.random((N, 128, C, 4)) < 0.5, -1.0, -0.9375) * 2.0 ** 30
    x[:, 5] *= 2.0 ** -10
    c = rng.choice([-1.0, 1.0], (128, 1, 4))
    for r in z[:2]: x[r] = c * (1.0 + 0.125 * rng.integers(0, 8, (128, C, 4))) * 2.0 ** -30
    for r in z[2:]: x[r] = x[r] * rng.choice([-1.0, 1.0], (1, C, 1))
    size = np.full(N, 2.0 ** 30)
    size[a[2:]] = 2.0 ** -30
    size[z[1::2]] = 2.0 ** -30
    u = d["u"].astype(np.float32).reshape(N, 128, 128, 4)
    w = np.zeros((N, 128, 4, 128, 4), np.float32)
    i = np.arange(128)
    for b in range(4): w[:, i, b, i, b] = 32.0
    w[a[2], 5, 0, 5, 0] = 2.0 ** 8
    w[a[2], 6, 0, 6, 0] = 2.0 ** -8
    k = np.array([[0, 0, 2, 2, 1, 1, 3, 3], [2, 1, 0, 3, 0, 3, 2, 1]])[parity()][:, rng.permutation(8)]
    e, m = lists(rng)
    j = np.arange(C)
    for r in range(N):
        h = rng.permutation(8)
        u[r, :, ::16] = (np.where(h < 2, 0.0, h % 2 * 2.0 - 1.0) * size[r])[None, :, None]
        for g in range(8):
            t = int(rng.integers(4))
            if t: m[r, g] = [C - 1 - j, j ^ 1, (j + H) % C][t - 1]
            e[r, g] = [ring(rng.permutation(C)), j, ring(j), m[r, g]][k[r, g]]
    u[:, 5, ::16] = 0
    v = rng.choice([-1.0, 1.0], (N, 128, 512)) * size[:, None, None]
    return {"x": x.astype(np.float32).reshape(N, 128, 4 * C).astype(BF), "u": u.reshape(N, 128, 512).astype(BF), "v": v.astype(np.float32).astype(BF), **stored(e, m), **weights(rng, w.astype(BF))}
def setup_inputs_spread(rng):
    d = setup_inputs(rng)
    d["x"] = wide(rng, N, 128, 4 * C, cols=6)
    return d
def check_inputs(d):
    b = []
    for k in ("x", "u", "v"):
        a = np.abs(d[k].astype(np.float32))
        if not (np.isfinite(a).all() and ((a == 0) | (a >= 2.0 ** -30) & (a <= 2.0 ** 30)).all()): b.append("a value of " + k)
    none, least, most = [emit(mx_ref.quantize(np.full((128, 16), k, np.float32).astype(BF)))[1][0, 0] for k in (0.0, 2.0 ** -8, 2.0 ** 8)]
    for r in range(N):
        if (np.sort(gentries(d["fl"][r]), axis=1) != OWN).any(): b.append("fl: a group that doesn't name every column once")
        m = gentries(d["ml"][r])
        if ((m < 0) | (m >= C)).any() or (m == OWN).any() or (m[G, m] != OWN).any(): b.append("ml: columns that aren't each other's mates")
        if ((d["wc"][r] == 0x7F) | (d["wc"][r] == 0xFF)).any(): b.append("wc: a code that is no number")
        s = mx_ref.live(d["ws"][r])
        if ((s != none) & ((s < least) | (s > most))).any(): b.append("ws: a scale out of range")
    return b
def leaders(a, s):
    best, w = OWN, a
    for _ in range(C - 1):
        p, o = s[G, w], s[G, best]
        best = np.where((p > o) | (p == o) & (w < best), w, best)
        w = a[G, w]
    return best
def hops(a, best):
    n, w = np.zeros((8, C), np.int64), best
    for _ in range(C - 1):
        go = w != OWN
        n, w = n + go, np.where(go, a[G, w], w)
    return n
def walk(a, at, n):
    for i in range(C - 1): at = np.where(i < n, a[G, at], at)
    return at
def reference(x, u, v, fl, ml, wc, ws):
    qu = [mx_ref.quantize(u[r]) for r in range(N)]
    lay = [pk(wc[r], ws[r]) for r in range(N)]
    cyc, mate = [gentries(fl[r]) for r in range(N)], [gentries(ml[r]) for r in range(N)]
    now = [x[r] for r in range(N)]
    for step in STEP:
        q = [mx_ref.quantize(now[r]) for r in range(N)]
        t = [decode(q[r]).astype(BF) for r in range(N)]
        made, after = [], []
        for r in range(N):
            p = r ^ step
            s = mx_ref.matmul(qu[r], q[r])[::16] + np.float32(0.0)
            lead = leaders(cyc[r], s)
            far = walk(cyc[p], lead, hops(cyc[r], lead))
            mine = s[G, far]
            other = mine[G, mate[r]]
            swap = np.where(OWN < mate[r], mine < other, other < mine)
            new = cyc[r][G, np.where(swap, mate[r], OWN)]
            back = np.argsort(new, axis=1)
            z = mx_ref.quantize(((gcols(t[r], new).astype(np.float32) + gcols(t[p], far).astype(np.float32)) * np.float32(0.5)).astype(BF))
            res = [mx_ref.matmul(pick(lay[r], np.arange(128 * b, 128 * b + 128)), z) * np.float32(0.03125) for b in range(4)]
            made.append(tile([(t[r][:, b::4].astype(np.float32) + gpick(res[b], back)) * np.float32(0.5) for b in range(4)]))
            after.append(new)
        now, cyc = made, after
    y, nl = np.zeros((N, 128, C), np.float32), np.zeros((N, 8, C), np.float32)
    oc, osc = np.zeros((N, 128, 4 * C), np.uint8), np.zeros((N, 16, C), np.uint8)
    for r in range(N):
        q = mx_ref.quantize(now[r])
        y[r] = mx_ref.matmul(mx_ref.quantize(v[r]), q)
        nl[r] = cyc[r]
        oc[r], osc[r] = emit(q)
    return {"y": y, "nl": nl, "oc": oc, "osc": osc}

@@ -1,0 +1,492 @@
+from concourse.mybir import dt, AluOpType, ActivationFunctionType
+
+C = 448
+TW = 28
+STEP = [1, 2, 3]
+NP = 1
+SCRATCH = {}
+
+
+def _decl():
+    f32, bf, f16 = "float32", "bfloat16", "float16"
+    for n in ["k0", "k0m", "kc", "cpr", "ka", "kb", "kma", "kmb", "kd", "yk", "yr", "cs", "sr", "sa", "cand", "mu", "nu", "sgn", "ck", "lck", "nlr", "ysb"]:
+        SCRATCH[n] = ("sbuf", [128, C], f32)
+    for n in ["cp", "rst", "pm", "cm"]:
+        SCRATCH[n] = ("sbuf", [128, C + 8], f32)
+    for n in ["eq", "lrow", "plr", "tplr", "tcsr", "tlenr", "trow", "sw", "srow", "brow", "lc", "fmr"]:
+        SCRATCH[n] = ("sbuf", [128, C], bf)
+    SCRATCH["ar"] = ("sbuf", [128, C + 16], bf)
+    for b in range(4 - NP, 4):
+        SCRATCH["pp%d" % b] = ("sbuf", [128, C], f32)
+    SCRATCH["ramp"] = ("sbuf", [128, C + 16], bf)
+    SCRATCH["ro"] = ("sbuf", [128, 9 * C], bf)
+    SCRATCH["cc"] = ("sbuf", [128, 6 * C], f16)
+    SCRATCH["drow"] = SCRATCH["plg"] = ("sbuf", [128, C], bf)
+    SCRATCH["cl"] = SCRATCH["nsgn"] = ("sbuf", [128, C], f32)
+    SCRATCH["c4s"] = ("sbuf", [128, 4 * C], f16)
+    SCRATCH["gr"] = ("sbuf", [128, 4 * C], bf)
+    for b in range(4):
+        for n in ["fh", "ft", "fs"]:
+            SCRATCH[n + str(b)] = ("sbuf", [128, C], bf)
+        SCRATCH["r2" + str(b)] = ("sbuf", [128, C], f32)
+    for n in ["xin", "xt", "zt"]:
+        SCRATCH[n] = ("sbuf", [128, 4 * C], bf)
+    for n in ["uin", "vin"]:
+        SCRATCH[n] = ("sbuf", [128, 512], bf)
+    SCRATCH["et"] = ("sbuf", [128, 2048], bf)
+    for n, w in [("wq", 512), ("qe", 512), ("qu", 128), ("qur", 128), ("qv", 128), ("qz", C)] + [("qx%d" % i, C) for i in range(4)] + [("lq%d" % i, C) for i in range(3)]:
+        SCRATCH[n] = ("sbuf", [128, w], "float8_e4m3fn_x4")
+        SCRATCH[n + "s"] = ("sbuf", [128, w], "uint8")
+    for n, w, t in [("fl_s", TW, "int32"), ("ml_s", TW, "int32"), ("pq", TW, "int32"), ("pqm", TW, "int32"), ("ofq", TW, "uint16"), ("ofi", 8, "int32"), ("ofu", 8, "uint16"),
+                    ("col", 12, f32), ("tf", TW * 50, f32), ("ti", TW * 4, "int32"), ("tu", TW * 20, "uint16"), ("t16", 16, bf), ("la16", 16, bf), ("lb16", 16, bf), ("lc16", 16, bf)]:
+        SCRATCH[n] = ("sbuf", [128, w], t)
+    for i in range(3):
+        SCRATCH["sp%d" % i] = ("sbuf", [128, 3 * TW], "uint16")
+        SCRATCH["sl%d" % i] = ("sbuf", [128, TW], "uint16")
+        SCRATCH["lp%d" % i] = ("sbuf", [128, 3 * TW], "uint16")
+        SCRATCH["la%d" % i] = ("sbuf", [128, TW], "uint16")
+    SCRATCH["pa"] = ("psum", [128, 2048], f32)
+    SCRATCH["pb"] = ("psum", [128, 2048], f32)
+
+
+_decl()
+LOADS = ["dfl", "dml", "dx", "du", "dv", "dwc", "dws"]
+SEMAPHORES = ["cv", "cs_", "ct", "cg", "snt", "outs"] + LOADS + ["%s%d" % (n, i) for n in ("aq", "al", "aa") for i in range(3)]
+TF = {n: i for i, n in enumerate(["jt", "f", "m", "hf", "fm", "cf", "hm", "cm", "ln", "cs", "pl", "g0", "g1", "g2", "g3", "i0", "ng", "t1", "p0", "pi", "u", "inv", "bq",
+                                  "t2", "tp", "sw", "sg", "si", "sn", "e1", "wr", "wl", "pb", "kmd", "lx", "ple", "ple2", "c2", "pre0", "pre", "vv", "vp", "w", "l3"])}
+TU = {n: i for i, n in enumerate(["tab%d" % k for k in range(9)] + ["m", "root", "l", "tp", "T", "sig", "b"] + ["end"])}
+TI = {"k": 0, "root": 1, "d": 2, "n": 3}
+BIAS = {"pp": 1.0, "lq": -2.0, "qz": 4.0, "tu.sig": 1.0}
+H, HW = 192, 12
+GAT, HALF, TINY, WAKE = 0.62, 0.32, 0.06, 0.15
+
+
+def rank_program(g, core, T, topo):
+    rank = T.rank_of(core)
+    if rank is None:
+        return
+    A = AluOpType
+    AF = ActivationFunctionType
+    Q = {"v": g.vector, "s": g.scalar, "t": g.tensor, "g": g, "y": g.sync}
+    CS = {"v": "cv", "s": "cs_", "t": "ct", "g": "cg"}
+    prog = []
+
+    def op(eng, fn, reads, writes, cost=TINY, sem=None, inc=1, lat=0.0, remote=None):
+        prog.append({"eng": eng, "fn": fn, "r": reads, "w": writes, "c": cost, "sem": sem, "inc": inc, "lat": lat, "remote": remote})
+
+    tf = lambda n: T.tf[:, TW * TF[n]:TW * TF[n] + TW]
+    tu = lambda n, a=0, b=TW: T.tu[:, TW * TU[n] + a:TW * TU[n] + b]
+    ti = lambda n: T.ti[:, TW * TI[n]:TW * TI[n] + TW]
+    cl = lambda i: T.col[:, i:i + 1]
+    SLOT = {"%s%d" % (n, k): (m, C * k) for n, m, z in (("ro", "ro", 9), ("c", "cc", 6)) for k in range(z)}
+
+    def row(n):
+        n, a = SLOT.get(n, (n, 0))
+        return T[n][:, a:a + C]
+
+    def sampled(n):
+        n, a = SLOT.get(n, (n, 0))
+        return T[n][:, a + 15:a + C:16]
+
+    row1 = lambda n: T[n][:, 1:C + 1]
+    win1 = lambda n: T[n][:, 0:C + 1]
+
+    def tt(out, wk, a, b, o, rk, c=TINY):
+        op("v", lambda: g.vector.tensor_tensor(out, a, b, o), rk, wk, c)
+
+    def ts(out, wk, a, s1, s2, o0, o1, rk, c=TINY):
+        if o1 is None:
+            op("v", lambda: g.vector.tensor_scalar(out, a, s1, None, o0), rk, wk, c)
+        else:
+            op("v", lambda: g.vector.tensor_scalar(out, a, s1, s2, o0, o1), rk, wk, c)
+
+    def cp(out, wk, a, rk, c=TINY):
+        op("v", lambda: g.vector.tensor_copy(out, a), rk, wk, c)
+
+    def act(out, wk, a, rk, c=GAT, func=None, **kw):
+        op("s", lambda: g.scalar.activation(out, a, func or AF.Copy, **kw), rk, wk, c)
+
+    def scan(out, wk, d0, d1, init, o0, o1, rk, c=0.43):
+        op("v", lambda: g.vector.tensor_tensor_scan(out, d0, d1, init, o0, o1), rk, wk, c)
+
+    def latch(ap, rk, cap, wk):
+        scan(cap, [wk], ap, row("lc"), -1024.0, A.max, A.add, (rk if isinstance(rk, list) else [rk]) + ["lc"], 0.26)
+
+    def tabs(cname, out, wk, col):
+        ts(out, wk, sampled(cname), cl(col), None, A.add, None, [cname, "col%d" % col])
+
+    def tabm(cname, out, wk, col):
+        ts(out, wk, sampled(cname), -1.0, cl(col), A.mult, A.add, [cname, "col%d" % col])
+
+    def load(eng, sem, out, src, key):
+        op(eng, lambda: Q[eng].dma_start(out, src), [], [key], 0.07, sem=sem, inc=16, lat=2.0)
+    load("y", "dfl", T.fl_s[:], T.fl[:], "fl_s")
+    load("s", "dx", T.xin[:], T.x[:], "xin")
+    load("y", "dml", T.ml_s[:], T.ml[:], "ml_s")
+    load("y", "du", T.uin[:], T.u[:], "uin")
+    load("y", "dwc", T.wq[:, 0:512].bitcast(dt.uint8), T.wc[:], "wq")
+    load("y", "dws", T.wqs[:, 0:512], T.ws[:], "wqs")
+    load("y", "dv", T.vin[:], T.v[:], "vin")
+
+    def iota(out, wk, pattern, base, cm, n, flag=True):
+        c = 0.15 + 0.00166 * n
+        if flag:
+            op("g", lambda: g.iota(out, pattern, base, cm, allow_small_or_imprecise_dtypes=True), [], wk, c)
+        else:
+            op("g", lambda: g.iota(out, pattern, base, cm), [], wk, c)
+    iota(T.pq[:], ["pq"], [[0, TW]], 0, 1, TW, False)
+    iota(T.t16[:], ["t16"], [[1, 16]], 0, 0, 16)
+    iota(T.ramp[:], ["ramp"], [[1, C + 16]], -224, 0, C + 16)
+    iota(row("k0"), ["k0"], [[1024, C]], 0, 0, C)
+    iota(row("k0m"), ["k0m"], [[1024, C]], -1, 0, C)
+    iota(tf("jt"), ["jt0"], [[16, TW]], 0, 0, TW)
+    iota(T.ofi[:], ["ofi"], [[16, 8]], 0, 0, 8, False)
+    iota(row("cpr"), ["cpr"], [[-1, C]], 449, 0, C)
+    iota(row("kd"), ["kd"], [[1024, C]], -1536, 0, C)
+    iota(row("kc"), ["kc"], [[1024, C]], -512, 0, C)
+    ts(T.pqm[:], ["pqm"], T.pq[:], 15, None, A.bitwise_and, None, ["pq"])
+    cp(cl(0), ["col0"], T.pqm[:, 0:1], ["pqm"])
+    cp(T.ofq[:], ["ofq"], T.pqm[:], ["pqm"])
+    ts(T.t16[:], ["t16"], T.t16[:], cl(0), None, A.subtract, None, ["t16", "col0"])
+    ts(T.la16[:], ["la16"], T.t16[:], 0.0, -1024.0, A.is_lt, A.mult, ["t16"])
+    ts(T.lb16[:], ["lb16"], T.t16[:], 0.0, 512.0, A.is_equal, A.mult, ["t16"])
+    tt(T.la16[:], ["la16"], T.la16[:], T.lb16[:], A.add, ["la16", "lb16"])
+    ts(T.lb16[:], ["lb16"], T.t16[:], 15.0, -1024.0, A.is_equal, A.mult, ["t16"])
+    tt(T.lc16[:], ["lc16"], T.la16[:], T.lb16[:], A.add, ["la16", "lb16"])
+    act(row("lc"), ["lc"], T.lc16[:].indirect(T.ofq[:]), ["lc16", "ofq"])
+    act(row("lck"), ["lck"], row("lc"), ["lc"], 0.43, scale=1024.0)
+    ts(cl(1), ["col1"], cl(0), 0.0, 1024.0, A.is_equal, A.mult, ["col0"])
+    ts(cl(1), ["col1"], cl(1), -512.0, None, A.add, None, ["col1"])
+    ts(cl(2), ["col2"], cl(1), 224.0, None, A.add, None, ["col1"])
+    ts(cl(3), ["col3"], cl(1), 1024.0, 511.0, A.mult, A.add, ["col1"])
+    ts(cl(8), ["col8"], cl(1), 1024.0, 512.0, A.mult, A.add, ["col1"])
+    ts(cl(7), ["col7"], cl(1), -2.0, 1.0, A.mult, A.add, ["col1"])
+    ts(cl(6), ["col6"], cl(1), 511.0 / 1024 + 0.01, None, A.add, None, ["col1"])
+    ts(cl(4), ["col4"], cl(1), -1.0, 449.0, A.mult, A.add, ["col1"])
+    ts(cl(5), ["col5"], cl(1), -1.0, 224.0, A.mult, A.add, ["col1"])
+    for n in ["cp", "rst", "pm", "cm"]:
+        op("v", lambda n=n: g.vector.memset(T[n][:, 0:1], 0.0), [], [n + "0"])
+    op("v", lambda: g.vector.memset(T.ar[:, 0:1], 0.0), [], ["ar0"])
+    op("v", lambda: g.vector.memset(T.et[:], 0.5), [], ["et1"], 0.5)
+    op("g", lambda: g.affine_select(T.et[:], T.et[:], [[-1, 4], [1, 512]], A.is_equal, 0.0, 0, -4), ["et1"], ["et"], 3.6)
+    cp(tu("tab0"), ["tu.tab0"], T.fl_s[:], ["fl_s"])
+
+    KS, KM = ["ka", "kb"], ["kma", "kmb"]
+
+    def frow():
+        act(row("ro0"), ["ro0"], T.ramp[:].indirect(tu("tab0")), ["ramp", "tu.tab0"])
+
+    def levels():
+        for k in range(9):
+            if k < 8:
+                a, b = "ro%d" % k, "ro%d" % (k + 1)
+                act(row(b), [b], row(a).indirect(tu("tab%d" % k)), [a, "tu.tab%d" % k])
+            src = "k0" if k == 0 else KS[k % 2]
+            sm = "k0m" if k == 0 else KM[k % 2]
+            dst, dm = KS[(k + 1) % 2], KM[(k + 1) % 2]
+            tt(row(dst), [dst], row(src).indirect(tu("tab%d" % k)), row(sm), A.min, [src, sm, "tu.tab%d" % k], GAT)
+            if k < 8:
+                c = "c%d" % (k % 2)
+                latch(row(b), b, row(c), c)
+                tabs(c, tu("tab%d" % (k + 1)), ["tu.tab%d" % (k + 1)], 2)
+                act(row(dm), [dm], row(dst), [dst], 0.43, bias=-float(2 ** (k + 1)))
+
+    KF = KS[1]
+
+    def send(r, dst_name, src_name, rk, sem, code=False, w=C):
+        dst = T.cores[rank ^ STEP[r]]
+        rid, pid = topo.addr(dst)[0:2]
+        m = topo.mask(core, dst)
+        n = len(topo.engines(core, dst))
+        if code:
+            o, i = T[dst_name][:, 0:w].bitcast(dt.uint8), T[src_name][:, 0:w].bitcast(dt.uint8)
+        else:
+            o, i = T[dst_name][:, 0:w], T[src_name][:, 0:w]
+        op("g", lambda: g.remote_dma(out_ap=o, in_ap=i, remote_sem=T.sem[sem], local_sem=T.sem.snt, pid=pid, routing_id=rid, dma_engine_mask=m),
+           rk, [dst_name], 0.5, lat=4.0 + (6.0 if code else 0.0), remote=(sem, n))
+
+    def finish(r):
+        sp, sl = "sp%d" % r, "sl%d" % r
+        tt(row("yk"), ["yk"], row(KF).indirect(tu("tab0")), row("kc"), A.max, [KF, "tu.tab0", "kc"], GAT)
+        scan(row("ck"), ["ck"], row(KF), row("lck"), -1048576.0, A.max, A.add, [KF, "lck"])
+        ts(tu("root"), ["tu.root"], T.ck[:, 15:C:16], 2.0 ** -10, cl(6), A.mult, A.add, ["ck", "col6"])
+        ts(ti("k"), ["ti.k"], T.ck[:, 15:C:16], cl(3), None, A.add, None, ["ck", "col3"])
+        ts(ti("d"), ["ti.d"], ti("k"), 511, None, A.bitwise_and, None, ["ti.k"])
+        cp(T[sp][:, 2 * TW:3 * TW], [sp + "d"], ti("d"), ["ti.d"])
+        tt(tf("kmd"), ["tf.kmd"], ti("k"), ti("d"), A.subtract, ["ti.k", "ti.d"])
+        act(row("yr"), ["yr"], row("yk").indirect(tu("root")), ["yk", "tu.root"])
+        act(row("drow"), ["drow"], T.ramp[:].indirect(T[sp][:, 2 * TW:3 * TW]), ["ramp", sp + "d"])
+        scan(row("cs"), ["cs"], row("yk"), row("kd"), -1024.0 - 224.0 - 511.0, A.add, A.subtract, ["yk", "kd"])
+        tt(row("plg"), ["plg"], row("cs").indirect(tu("root")), row(KF), A.subtract, ["cs", "tu.root", KF], GAT)
+        latch(row("plg"), "plg", row("c2"), "c2")
+        tabs("c2", T[sp][:, 0:TW], [sp + "a"], 2)
+        op("v", lambda: g.vector.tensor_copy(win1("cp").indirect(T[sp][:, 0:TW]), row("cpr")), ["cpr", sp + "a", "cp0"], ["cp"], 1.4)
+        scan(row("cl"), ["cl"], row("yr"), row("lck"), -1048576.0, A.max, A.add, ["yr", "lck"])
+        ts(tf("lx"), ["tf.lx"], T["cl"][:, 15:C:16], cl(8), None, A.add, None, ["cl", "col8"])
+        tt(tf("ln"), ["tf.ln"], tf("lx"), tf("kmd"), A.subtract, ["tf.lx", "tf.kmd"])
+        cp(T[sp][:, TW:2 * TW], [sp + "b"], tf("ln"), ["tf.ln"])
+        tabs("c2", tf("pl"), ["tf.pl"], 2)
+        ts(tf("ple"), ["tf.ple"], tf("pl"), cl(2), None, A.subtract, None, ["tf.pl", "col2"])
+        ts(tf("ple2"), ["tf.ple2"], tf("ple"), cl(2), None, A.subtract, None, ["tf.ple", "col2"])
+        tt(tf("cs"), ["tf.cs"], tf("pl"), ti("d"), A.add, ["tf.pl", "ti.d"])
+        cp(tu("end"), ["tu.end"], tf("cs"), ["tf.cs"])
+        ts(tf("c2"), ["tf.c2"], tf("cf"), -2.0, None, A.mult, None, ["tf.cf"])
+        ts(tf("pre0"), ["tf.pre0"], tf("cf"), cl(7), None, A.mult, None, ["tf.cf", "col7"])
+        tt(tf("pre"), ["tf.pre"], tf("pre0"), tf("hf"), A.add, ["tf.pre0", "tf.hf"])
+        send(r, "lp%d" % r, sp, [sp + "a", sp + "b", sp + "d"], "al%d" % r, w=3 * TW)
+        latch(row1("cp"), "cp", row("c4"), "c4")
+        tabm("c4", T[sl][:], [sl], 4)
+        send(r, "la%d" % r, sl, [sl], "aa%d" % r, w=TW)
+
+    def mm(dst, b, st, so, mv):
+        op("t", lambda: g.tensor.matmul_mx(T[dst][:, 512 * b:512 * b + C], T[st][:, so:so + 128], T[st + "s"][:, so:so + 128], T[mv][:, 0:C], T[mv + "s"][:, 0:C], True, True),
+           [st, st + "s", mv, mv + "s"], [dst + str(b)], 0.4)
+
+    def quant(tile, keys, w, q):
+        op("v", lambda: g.vector.quantize_mx(T[q][:, 0:w], T[q + "s"][:, 0:w], T[tile][:, 0:4 * w]), keys, [q, q + "s"], 0.08 + 0.00088 * w)
+
+    def state_made(r):
+        send(r, "lq%d" % r, "qx%d" % r, ["qx%d" % r], "aq%d" % r, code=True)
+        send(r, "lq%ds" % r, "qx%ds" % r, ["qx%ds" % r], "aq%d" % r)
+        mm("pb", 0, "qur", 0, "qx%d" % r)
+        act(row("sr"), ["sr"], T.pb[:, 0:C], ["pb0", "ro8"], 0.43)
+        for b in range(4):
+            mm("pa", b, "qe", 128 * b, "qx%d" % r)
+        for b in range(4):
+            mm("pb", b, "qe", 128 * b, "lq%d" % r)
+
+    frow()
+    levels()
+    cp(tu("m"), ["tu.m"], T.ml_s[:], ["ml_s"])
+    cp(tf("f"), ["tf.f"], T.fl_s[:], ["fl_s"])
+    cp(tf("m"), ["tf.m"], T.ml_s[:], ["ml_s"])
+    act(row("fmr"), ["fmr"], row("ro0").indirect(tu("m")), ["ro0", "tu.m", "ro8"])
+    latch(row("fmr"), "fmr", row("c2"), "c2")
+    tabs("c2", tf("fm"), ["tf.fm"], 2)
+    tt(tf("hf"), ["tf.hf"], tf("fm"), tf("f"), A.add, ["tf.fm", "tf.f"])
+    ts(tf("hf"), ["tf.hf"], tf("hf"), 0.5, None, A.mult, None, ["tf.hf"])
+    tt(tf("cf"), ["tf.cf"], tf("f"), tf("hf"), A.subtract, ["tf.f", "tf.hf"])
+    ts(tf("jt"), ["tf.jt"], tf("jt"), cl(0), None, A.add, None, ["jt0", "col0"])
+    tt(tf("hm"), ["tf.hm"], tf("m"), tf("jt"), A.add, ["tf.m", "tf.jt"])
+    ts(tf("hm"), ["tf.hm"], tf("hm"), 0.5, None, A.mult, None, ["tf.hm"])
+    tt(tf("cm"), ["tf.cm"], tf("jt"), tf("hm"), A.subtract, ["tf.jt", "tf.hm"])
+    ts(tf("sn"), ["tf.sn"], tf("cm"), 0.0, 2.0, A.is_lt, A.mult, ["tf.cm"])
+    ts(tu("sig"), ["tu.sig"], tf("sn"), 223.0, None, A.add, None, ["tf.sn"])
+    act(row("sgn"), ["sgn"], T.ramp[:].indirect(tu("sig")), ["ramp", "tu.sig", "ro8"])
+    quant("xin", ["xin", "tu.tab2"], C, "qx0")
+    quant("uin", ["uin"], 128, "qu")
+    cp(T.ofu[:], ["ofu"], T.ofi[:], ["ofi"])
+    op("v", lambda: g.vector.tensor_copy(T.qur[:, 0:128].bitcast(dt.uint32), T.qu[:, 0:128].bitcast(dt.uint32).indirect(T.ofu[:, 0:8])), ["qu", "ofu"], ["qur"], 0.27)
+    op("s", lambda: g.scalar.activation(T.qurs[:, 0:128], T.qus[:, 0:128].indirect(T.ofu[:, 0:8]), AF.Copy), ["qus", "ofu"], ["qurs"], 0.27)
+    quant("et", ["et"], 512, "qe")
+    state_made(0)
+    finish(0)
+    act(row("nsgn"), ["nsgn"], row("sgn"), ["sgn", "yr"], 0.43, scale=-1.0)
+    ts(tf("e1"), ["tf.e1"], ti("d"), 1.0, None, A.add, None, ["ti.d"])
+    tt(tf("wr"), ["tf.wr"], tf("e1"), tf("ln"), A.is_equal, ["tf.e1", "tf.ln"])
+    tt(tf("wl"), ["tf.wl"], tf("wr"), tf("ln"), A.mult, ["tf.wr", "tf.ln"])
+    tt(tf("pb"), ["tf.pb"], tf("pl"), tf("wl"), A.add, ["tf.pl", "tf.wl"])
+    ts(tu("b"), ["tu.b"], tf("pb"), -1.0, None, A.add, None, ["tf.pb"])
+    act(row("brow"), ["brow"], win1("cp").indirect(tu("b")), ["cp", "tu.b"], scale=-1.0, bias=225.0)
+    latch(row("brow"), "brow", row("c3"), "c3")
+    tabs("c3", tu("b"), ["tu.b"], 2)
+
+    grs = lambda i: T.gr[:, C * i:C * i + C]
+    for r in range(3):
+        sl, lp, la, sp = "sl%d" % r, "lp%d" % r, "la%d" % r, "sp%d" % r
+        last = r == 2
+        act(row1("rst"), ["rst"], row("drow").indirect(T[sl][:]), ["drow", sl, "rst0"], scale=float(2 ** 90), bias=223.5 * float(2 ** 90))
+        cp(row("sa"), ["sa"], row("sr").indirect(T[sl][:]), ["sr", sl], GAT)
+        scan(row1("pm"), ["pm"], row("rst"), row("sa"), -float(2 ** 90), A.min, A.max, ["rst", "rst0", "sa", "pm0"])
+        tt(row("eq"), ["eq"], win1("pm").indirect(tu("end")), row("sr"), A.is_equal, ["pm", "tu.end", "sr"], GAT)
+        tt(row("cand"), ["cand"], row("eq").indirect(T[sl][:]), row1("cp"), A.mult, ["eq", sl, "cp"], GAT)
+        scan(row1("cm"), ["cm"], row("rst"), row("cand"), 0.0, A.min, A.max, ["rst", "cand", "cm0"])
+        act(T.lrow[:, 0:H], ["lrowa"], win1("cm").indirect(tu("end", 0, HW)), ["cm", "tu.end"], HALF, bias=-225.0)
+        ts(T.lrow[:, H:C], ["lrowb"], win1("cm").indirect(tu("end", HW)), -225.0, None, A.add, None, ["cm", "tu.end"], HALF)
+        latch(row("lrow"), ["lrowa", "lrowb"], row("c5"), "c5")
+        tabm("c5", tu("l"), ["tu.l"], 5)
+        act(row("plr"), ["plr"], T.ramp[:].indirect(T[sp][:, 0:TW]), ["ramp", sp + "a"])
+        for b in range(4):
+            act(row("fh%d" % b), ["fh%d" % b], T.pa[:, 512 * b:512 * b + C], ["pa%d" % b, "yr"], 0.43)
+        act(row("tcsr"), ["tcsr"], T.ramp[:].indirect(T[lp][:, 2 * TW:3 * TW]), ["ramp", lp])
+        act(row("tlenr"), ["tlenr"], T.ramp[:].indirect(T[lp][:, TW:2 * TW]), ["ramp", lp])
+        act(row("tplr"), ["tplr"], T.ramp[:].indirect(T[lp][:, 0:TW]), ["ramp", lp])
+        cp(grs(3), ["gr3"], row("tlenr").indirect(tu("l")), ["tlenr", "tu.l"], GAT)
+        act(grs(1), ["gr1"], row("plr").indirect(tu("l")), ["plr", "tu.l"])
+        cp(grs(2), ["gr2"], row("tcsr").indirect(tu("l")), ["tcsr", "tu.l"], GAT)
+        act(grs(0), ["gr0"], row("tplr").indirect(tu("l")), ["tplr", "tu.l"])
+        act(row1("ar"), ["ar"], T.ramp[:].indirect(T[la][:]), ["ramp", la, "ar0"])
+        for i in (3, 1, 2, 0):
+            latch(grs(i), "gr%d" % i, T.c4s[:, C * i:C * i + C], "c4s%d" % i)
+        x = lambda i: T.c4s[:, C * i + 15:C * i + C:16]
+        for b in range(4):
+            act(row("ft%d" % b), ["ft%d" % b], T.pb[:, 512 * b:512 * b + C], ["pb%d" % b, "gr0"], 0.43)
+        ts(tf("l3"), ["tf.l3"], x(3), cl(2), None, A.add, None, ["c4s3", "col2"])
+        tt(tf("ng"), ["tf.ng"], tf("ple"), x(1), A.is_lt, ["c4s1", "tf.ple"])
+        tt(tf("vv"), ["tf.vv"], tf("ple2"), x(1), A.subtract, ["c4s1", "tf.ple2"])
+        tt(tf("vp"), ["tf.vp"], tf("pl"), x(1), A.subtract, ["c4s1", "tf.pl"])
+        op("v", lambda: g.vector.reciprocal(tf("inv"), tf("l3")), ["tf.l3"], ["tf.inv"], 0.33)
+        tt(tf("t1"), ["tf.t1"], tf("ng"), tf("ln"), A.mult, ["tf.ng", "tf.ln"])
+        tt(tf("w"), ["tf.w"], x(2), tf("vv"), A.subtract, ["c4s2", "tf.vv"])
+        tt(tf("u"), ["tf.u"], tf("w"), tf("t1"), A.subtract, ["tf.w", "tf.t1"])
+        tt(tf("p0"), ["tf.p0"], x(0), tf("vp"), A.add, ["c4s0", "tf.vp"])
+        tt(tf("pi"), ["tf.pi"], tf("p0"), tf("t1"), A.add, ["tf.p0", "tf.t1"])
+        tt(tf("bq"), ["tf.bq"], tf("u"), tf("inv"), A.mult, ["tf.u", "tf.inv"])
+        ts(ti("n"), ["ti.n"], tf("bq"), -0.4989, None, A.add, None, ["tf.bq"])
+        tt(tf("t2"), ["tf.t2"], ti("n"), tf("l3"), A.mult, ["ti.n", "tf.l3"])
+        tt(tf("tp"), ["tf.tp"], tf("pi"), tf("t2"), A.add, ["tf.pi", "tf.t2"])
+        cp(tu("tp"), ["tu.tp"], tf("tp"), ["tf.tp"])
+        act(T.trow[:, 0:H], ["trowa"], win1("ar").indirect(tu("tp", 0, HW)), ["ar", "tu.tp"], HALF)
+        cp(T.trow[:, H:C], ["trowb"], win1("ar").indirect(tu("tp", HW)), ["ar", "tu.tp"], HALF)
+        latch(row("trow"), ["trowa", "trowb"], row("c5"), "c5")
+        tabs("c5", tu("T"), ["tu.T"], 2)
+        tt(row("mu"), ["mu"], row("sr").indirect(tu("T")), row("sgn"), A.mult, ["sr", "tu.T", "sgn"], GAT)
+        for b in range(4):
+            act(row("fs%d" % b), ["fs%d" % b], row("ft%d" % b).indirect(tu("T")), ["ft%d" % b, "tu.T"])
+        tt(row("nu"), ["nu"], row("sr").indirect(tu("T")), row("nsgn"), A.mult, ["sr", "tu.T", "nsgn"], GAT)
+        tt(row("sw"), ["sw"], row("mu").indirect(tu("m")), row("nu"), A.is_lt, ["mu", "nu", "tu.m"], GAT)
+        latch(row("sw"), "sw", row("c5"), "c5")
+        ts(tf("sw"), ["tf.sw"], sampled("c5"), -2.0, cl(7), A.mult, A.add, ["c5", "col7"])
+        tt(tf("si"), ["tf.si"], sampled("c5"), tf("c2"), A.mult, ["c5", "tf.c2"])
+        tt(tf("f"), ["tf.f"], tf("si"), tf("pre"), A.add, ["tf.si", "tf.pre"])
+        tt(tf("cf"), ["tf.cf"], tf("sw"), tf("cf"), A.mult, ["tf.sw", "tf.cf"])
+        cp(tu("tab0"), ["tu.tab0"], tf("f"), ["tf.f"])
+        for b in range(4):
+            tt(T.zt[:, b:4 * C:4], ["zt%d" % b], row("fh%d" % b).indirect(tu("tab0")), row("fs%d" % b), A.add, ["fh%d" % b, "fs%d" % b, "tu.tab0"], GAT)
+        quant("zt", ["zt0", "zt1", "zt2", "zt3"], C, "qz")
+        for b in range(4):
+            mm("pb", b, "wq", 128 * b, "qz")
+        tt(tf("sg"), ["tf.sg"], tf("sw"), tf("cm"), A.mult, ["tf.sw", "tf.cm"])
+        tt(tf("si"), ["tf.si"], tf("sg"), tf("hm"), A.add, ["tf.sg", "tf.hm"])
+        cp(tu("sig"), ["tu.sig"], tf("si"), ["tf.si"])
+        act(row("srow"), ["srow"], T.ramp[:].indirect(tu("sig")), ["ramp", "tu.sig"])
+        act(row("brow"), ["brow"], row("srow").indirect(tu("b")), ["srow", "tu.b"])
+        latch(row("brow"), "brow", row("c3"), "c3")
+        tabs("c3", tu("b"), ["tu.b"], 2)
+        for b in range(4):
+            act(row("r2%d" % b), ["r2%d" % b], T.pb[:, 512 * b:512 * b + C], ["pb%d" % b], 0.43, scale=0.015625)
+        for b in range(4):
+            if b >= 4 - NP and not last:
+                act(row("pp%d" % b), ["pp%d" % b], row("r2%d" % b).indirect(tu("b")), ["r2%d" % b, "tu.b"])
+                tt(T.xt[:, b:4 * C:4], ["xt%d" % b], row("pp%d" % b), T.pa[:, 512 * b:512 * b + C], A.add, ["pp%d" % b, "pa%d" % b], 0.43)
+                continue
+            tt(T.xt[:, b:4 * C:4], ["xt%d" % b], row("r2%d" % b).indirect(tu("b")), row("fh%d" % b), A.add, ["r2%d" % b, "fh%d" % b, "tu.b"], GAT)
+        quant("xt", ["xt0", "xt1", "xt2", "xt3"], C, "qx%d" % (r + 1))
+        if last:
+            break
+        frow()
+        levels()
+        state_made(r + 1)
+        if r == 0:
+            quant("vin", ["vin"], 128, "qv")
+        finish(r + 1)
+    def store(eng, out, src, keys):
+        op(eng, lambda: Q[eng].dma_start(out, src), keys, [], 0.07, sem="outs", inc=16, lat=2.0)
+    act(row("nlr"), ["nlr"], T.ramp[:].indirect(tu("tab0")), ["ramp", "tu.tab0"], bias=224.0)
+    store("y", T.nl[:], T.nlr[0:128:16, :], ["nlr"])
+    mm("pb", 0, "qv", 0, "qx3")
+    store("y", T.oc[:], T.qx3[:, 0:C].bitcast(dt.uint8), ["qx3"])
+    act(row("ysb"), ["ysb"], T.pb[:, 0:C], ["pb0"], 0.43)
+    for k in range(4):
+        store("y", T.osc[4 * k:4 * k + 4, :], T.qx3s[32 * k:32 * k + 4, 0:C], ["qx3s"])
+    store("s", T.y[:], row("ysb"), ["ysb"])
+
+    n = len(prog)
+    deps, kids = [set() for _ in range(n)], [[] for _ in range(n)]
+    lw, rd = {}, {}
+    for i, p in enumerate(prog):
+        for k in p["r"]:
+            if k in lw:
+                deps[i].add(lw[k])
+        for k in p["w"]:
+            if k in lw:
+                deps[i].add(lw[k])
+            deps[i].update(rd.get(k, []))
+        for k in p["r"]:
+            rd.setdefault(k, []).append(i)
+        for k in p["w"]:
+            lw[k], rd[k] = i, []
+        deps[i].discard(i)
+        for d in deps[i]:
+            kids[d].append(i)
+    prio = [0.0] * n
+    for i in range(n - 1, -1, -1):
+        prio[i] = prog[i]["c"] + prog[i]["lat"] + max([prio[k] + WAKE for k in kids[i]] + [0.0])
+    for i in range(n):
+        prio[i] += BIAS.get(prog[i]["w"][0].rstrip("0123456789") if prog[i]["w"] else "", 0.0)
+    done, left, tq, order = {}, [len(d) for d in deps], {e: 0.0 for e in Q}, []
+    ready = {e: [] for e in Q}
+    for i in range(n):
+        if not left[i]:
+            ready[prog[i]["eng"]].append((0.0, i))
+    while len(order) < n:
+        pick = None
+        for e in Q:
+            if not ready[e]:
+                continue
+            t0 = max(tq[e], min(a for a, i in ready[e]))
+            a, i = max((x for x in ready[e] if x[0] <= t0 + 1e-9), key=lambda x: (prio[x[1]], -x[1]))
+            if pick is None or t0 < pick[0]:
+                pick = (t0, e, a, i)
+        t0, e, a, i = pick
+        ready[e].remove((a, i))
+        order.append(i)
+        tq[e] = t0 + prog[i]["c"]
+        done[i] = tq[e] + prog[i]["lat"] + WAKE
+        for k in kids[i]:
+            left[k] -= 1
+            if not left[k]:
+                ready[prog[k]["eng"]].append((max(done[d] for d in deps[k]), k))
+
+    cnt = {s: 0 for s in SEMAPHORES}
+    known = {e: {} for e in Q}
+    clock, lastw, readers = {}, {}, {}
+
+    def need(eng, ds):
+        best = {}
+        for s, v in ds:
+            best[s] = max(best.get(s, 0), v)
+        own = CS.get(eng)
+        for s in sorted(best, key=lambda x: (x == own, x)):
+            if known[eng].get(s, 0) >= best[s]:
+                continue
+            Q[eng].wait_ge(T.sem[s], best[s])
+            for x, y in clock[(s, best[s])].items():
+                known[eng][x] = max(known[eng].get(x, 0), y)
+
+    landed = {"aq%d" % i: 2 for i in range(3)}
+    for i in order:
+        p = prog[i]
+        ds = []
+        for k in p["r"]:
+            if k in lastw:
+                ds.append(lastw[k])
+        if p["remote"]:
+            need("g", ds)
+            p["fn"]()
+            sem, m = p["remote"]
+            cnt["snt"] += m
+            cnt[sem] += m
+            me = (sem, m * landed.get(sem, 1))
+            clock[me] = {sem: me[1]}
+            lastw[p["w"][0]] = me
+            continue
+        for k in p["w"]:
+            if k in lastw:
+                ds.append(lastw[k])
+            ds += readers.get(k, [])
+        need(p["eng"], ds)
+        s = p["sem"] or CS[p["eng"]]
+        cnt[s] += p["inc"]
+        p["fn"]().then_inc(T.sem[s], p["inc"])
+        me = (s, cnt[s])
+        clock[me] = dict(known[p["eng"]])
+        clock[me][s] = cnt[s]
+        for k in p["r"]:
+            readers.setdefault(k, []).append(me)
+        for k in p["w"]:
+            lastw[k] = me
+            readers[k] = []
+    for s in SEMAPHORES:
+        if cnt[s] and known["g"].get(s, 0) < cnt[s]:
+            g.wait_ge(T.sem[s], cnt[s])

@@ -3,46 +3,41 @@ from concourse.mybir import dt, AluOpType, ActivationFunctionType
 C = 448
 TW = 28
 STEP = [1, 2, 3]
-NP = 1
+OPT = {"NP": [1, 1, 0], "SA": True, "K2": True, "NU": False, "ZD": 0, "TAIL": True, "HE": 12, "HA": 0, "HL": 12, "HT": 12, "BYL": "vsss",
+       "WAKE": 0.15, "REM": 2.5, "RW": 0.9, "LOOK": 0.08, "KAP": 0.6, "BIAS": {"tf.swb": 5.0}, "DADD": 4.0}
 SCRATCH = {}
 
 
 def _decl():
     f32, bf, f16 = "float32", "bfloat16", "float16"
-    for n in ["k0", "k0m", "kc", "cpr", "ka", "kb", "kma", "kmb", "kd", "yk", "yr", "cs", "sr", "sa", "cand", "mu", "nu", "sgn", "ck", "lck", "nlr", "ysb"]:
+    for n in ["k0m", "kc", "ka", "kb", "kma", "kmb", "yk", "sr", "sa", "pm", "mu", "nu", "ck", "nlr"]:
         SCRATCH[n] = ("sbuf", [128, C], f32)
-    for n in ["cp", "rst", "pm", "cm"]:
-        SCRATCH[n] = ("sbuf", [128, C + 8], f32)
-    for n in ["eq", "lrow", "plr", "tplr", "tcsr", "tlenr", "trow", "sw", "srow", "brow", "lc", "fmr"]:
+    SCRATCH["sfa"] = ("sbuf", [128, 2 * C], f32)
+    for n in ["cum", "rst", "ramp"]:
+        SCRATCH[n] = ("sbuf", [128, C + 16], bf)
+    for n in ["neq", "cand", "cm", "cp", "code9", "lrow", "plr", "orow", "strow", "lenrow", "trow", "dif", "sw", "swb", "brow", "mrow", "mbr", "lc", "lc9", "fmr",
+              "erow", "srow", "drow", "ar", "sgn"]:
         SCRATCH[n] = ("sbuf", [128, C], bf)
-    SCRATCH["ar"] = ("sbuf", [128, C + 16], bf)
-    for b in range(4 - NP, 4):
-        SCRATCH["pp%d" % b] = ("sbuf", [128, C], f32)
-    SCRATCH["ramp"] = ("sbuf", [128, C + 16], bf)
     SCRATCH["ro"] = ("sbuf", [128, 9 * C], bf)
-    SCRATCH["cc"] = ("sbuf", [128, 6 * C], f16)
-    SCRATCH["drow"] = SCRATCH["plg"] = ("sbuf", [128, C], bf)
-    SCRATCH["cl"] = SCRATCH["nsgn"] = ("sbuf", [128, C], f32)
+    SCRATCH["cc"] = ("sbuf", [128, 10 * C], f16)
     SCRATCH["c4s"] = ("sbuf", [128, 4 * C], f16)
-    SCRATCH["gr"] = ("sbuf", [128, 4 * C], bf)
-    for b in range(4):
-        for n in ["fh", "ft", "fs"]:
-            SCRATCH[n + str(b)] = ("sbuf", [128, C], bf)
-        SCRATCH["r2" + str(b)] = ("sbuf", [128, C], f32)
-    for n in ["xin", "xt", "zt"]:
+    for n in ["gr", "fh", "ft", "fs", "xin", "xt", "zt", "za"]:
         SCRATCH[n] = ("sbuf", [128, 4 * C], bf)
+    for n in ["pp", "r2", "kw"]:
+        SCRATCH[n] = ("sbuf", [128, 4 * C], f32)
     for n in ["uin", "vin"]:
         SCRATCH[n] = ("sbuf", [128, 512], bf)
     SCRATCH["et"] = ("sbuf", [128, 2048], bf)
+    SCRATCH["half"] = ("sbuf", [128, 128], bf)
     for n, w in [("wq", 512), ("qe", 512), ("qu", 128), ("qur", 128), ("qv", 128), ("qz", C)] + [("qx%d" % i, C) for i in range(4)] + [("lq%d" % i, C) for i in range(3)]:
         SCRATCH[n] = ("sbuf", [128, w], "float8_e4m3fn_x4")
         SCRATCH[n + "s"] = ("sbuf", [128, w], "uint8")
     for n, w, t in [("fl_s", TW, "int32"), ("ml_s", TW, "int32"), ("pq", TW, "int32"), ("pqm", TW, "int32"), ("ofq", TW, "uint16"), ("ofi", 8, "int32"), ("ofu", 8, "uint16"),
-                    ("col", 12, f32), ("tf", TW * 50, f32), ("ti", TW * 4, "int32"), ("tu", TW * 20, "uint16"), ("t16", 16, bf), ("la16", 16, bf), ("lb16", 16, bf), ("lc16", 16, bf)]:
+                    ("col", 12, f32), ("tf", TW * 50, f32), ("ti", TW * 4, "int32"), ("tu", TW * 24, "uint16"), ("t16", 16, bf), ("la16", 16, bf), ("lb16", 16, bf), ("lc16", 16, bf)]:
         SCRATCH[n] = ("sbuf", [128, w], t)
+    SCRATCH["sp"] = ("sbuf", [128, 3 * 3 * TW], "uint16")
+    SCRATCH["sl"] = ("sbuf", [128, 3 * TW], "uint16")
     for i in range(3):
-        SCRATCH["sp%d" % i] = ("sbuf", [128, 3 * TW], "uint16")
-        SCRATCH["sl%d" % i] = ("sbuf", [128, TW], "uint16")
         SCRATCH["lp%d" % i] = ("sbuf", [128, 3 * TW], "uint16")
         SCRATCH["la%d" % i] = ("sbuf", [128, TW], "uint16")
     SCRATCH["pa"] = ("psum", [128, 2048], f32)
@@ -51,14 +46,14 @@ def _decl():
 
 _decl()
 LOADS = ["dfl", "dml", "dx", "du", "dv", "dwc", "dws"]
-SEMAPHORES = ["cv", "cs_", "ct", "cg", "snt", "outs"] + LOADS + ["%s%d" % (n, i) for n in ("aq", "al", "aa") for i in range(3)]
-TF = {n: i for i, n in enumerate(["jt", "f", "m", "hf", "fm", "cf", "hm", "cm", "ln", "cs", "pl", "g0", "g1", "g2", "g3", "i0", "ng", "t1", "p0", "pi", "u", "inv", "bq",
-                                  "t2", "tp", "sw", "sg", "si", "sn", "e1", "wr", "wl", "pb", "kmd", "lx", "ple", "ple2", "c2", "pre0", "pre", "vv", "vp", "w", "l3"])}
-TU = {n: i for i, n in enumerate(["tab%d" % k for k in range(9)] + ["m", "root", "l", "tp", "T", "sig", "b"] + ["end"])}
-TI = {"k": 0, "root": 1, "d": 2, "n": 3}
-BIAS = {"pp": 1.0, "lq": -2.0, "qz": 4.0, "tu.sig": 1.0}
-H, HW = 192, 12
-GAT, HALF, TINY, WAKE = 0.62, 0.32, 0.06, 0.15
+SEMAPHORES = ["cv", "cs_", "ct", "cg", "snt", "outs", "zadd"] + LOADS + ["%s%d" % (n, i) for n in ("aq", "al", "aa") for i in range(3)]
+TF = {n: i for i, n in enumerate(["jt", "f", "m", "hf", "fm", "cf", "hb", "cb", "b", "mb", "sn", "dq", "pl", "ple", "o", "ln", "st", "l3", "inv", "ng", "t1", "w", "a1", "hl", "a2",
+                                  "u", "m1", "bq", "t2", "tp", "tpa", "tpb", "sw", "swb", "e1", "j4", "q0", "q2", "q3", "oa", "ob", "ba", "bb"])}
+TU = {n: i for i, n in enumerate(["tab%d" % k for k in range(9)] + ["m", "root", "root1", "l", "tp", "tpa", "tpb", "T", "sig", "b", "last", "pl", "d", "k2"])}
+TI = {"k": 0, "d": 1, "n": 2}
+CYC = 0.83e-3 * 1.25
+BIG = float(2 ** 90)
+STEP1 = 2.0 ** -10
 
 
 def rank_program(g, core, T, topo):
@@ -69,27 +64,29 @@ def rank_program(g, core, T, topo):
     AF = ActivationFunctionType
     Q = {"v": g.vector, "s": g.scalar, "t": g.tensor, "g": g, "y": g.sync}
     CS = {"v": "cv", "s": "cs_", "t": "ct", "g": "cg"}
+    WAKE = OPT["WAKE"]
     prog = []
+    TINY, R2, R4 = 64 * CYC, C // 2 * CYC, C * CYC
+    gat = lambda n=C: 0.055 + 0.0013 * n
+    GAT = gat()
 
     def op(eng, fn, reads, writes, cost=TINY, sem=None, inc=1, lat=0.0, remote=None):
         prog.append({"eng": eng, "fn": fn, "r": reads, "w": writes, "c": cost, "sem": sem, "inc": inc, "lat": lat, "remote": remote})
 
-    tf = lambda n: T.tf[:, TW * TF[n]:TW * TF[n] + TW]
+    tf = lambda n, k=1: T.tf[:, TW * TF[n]:TW * (TF[n] + k)]
     tu = lambda n, a=0, b=TW: T.tu[:, TW * TU[n] + a:TW * TU[n] + b]
     ti = lambda n: T.ti[:, TW * TI[n]:TW * TI[n] + TW]
     cl = lambda i: T.col[:, i:i + 1]
-    SLOT = {"%s%d" % (n, k): (m, C * k) for n, m, z in (("ro", "ro", 9), ("c", "cc", 6)) for k in range(z)}
+    SLOT = {"%s%d" % (n, k): (m, C * k) for n, m, z in (("ro", "ro", 9), ("c", "cc", 10), ("gr", "gr", 4), ("x", "c4s", 4), ("fh", "fh", 4), ("ft", "ft", 4), ("fs", "fs", 4),
+                                                       ("pp", "pp", 4), ("r2", "r2", 4)) for k in range(z)}
 
-    def row(n):
-        n, a = SLOT.get(n, (n, 0))
-        return T[n][:, a:a + C]
+    def row(n, a=0, b=C):
+        n, s = SLOT.get(n, (n, 0))
+        return T[n][:, s + a:s + b]
 
     def sampled(n):
         n, a = SLOT.get(n, (n, 0))
         return T[n][:, a + 15:a + C:16]
-
-    row1 = lambda n: T[n][:, 1:C + 1]
-    win1 = lambda n: T[n][:, 0:C + 1]
 
     def tt(out, wk, a, b, o, rk, c=TINY):
         op("v", lambda: g.vector.tensor_tensor(out, a, b, o), rk, wk, c)
@@ -106,290 +103,327 @@ def rank_program(g, core, T, topo):
     def act(out, wk, a, rk, c=GAT, func=None, **kw):
         op("s", lambda: g.scalar.activation(out, a, func or AF.Copy, **kw), rk, wk, c)
 
-    def scan(out, wk, d0, d1, init, o0, o1, rk, c=0.43):
+    def scan(out, wk, d0, d1, init, o0, o1, rk, c=R4):
         op("v", lambda: g.vector.tensor_tensor_scan(out, d0, d1, init, o0, o1), rk, wk, c)
 
-    def latch(ap, rk, cap, wk):
-        scan(cap, [wk], ap, row("lc"), -1024.0, A.max, A.add, (rk if isinstance(rk, list) else [rk]) + ["lc"], 0.26)
+    def pick(name, win, tab, rk, h, scale=1.0):
+        keys = []
+        if h:
+            act(row(name, 0, 16 * h), [name + "a"], win.indirect(tab(0, h)), rk, gat(16 * h), scale=scale)
+            keys.append(name + "a")
+        if h < TW:
+            ts(row(name, 16 * h, C), [name + "b"], win.indirect(tab(h, TW)), scale, None, A.mult, None, rk, gat(C - 16 * h))
+            keys.append(name + "b")
+        return keys
 
-    def tabs(cname, out, wk, col):
-        ts(out, wk, sampled(cname), cl(col), None, A.add, None, [cname, "col%d" % col])
+    def latch(src, rk, cname, fine=False, c=R2):
+        lc, low = ("lc9", -2.0) if fine else ("lc", -1024.0)
+        scan(row(cname), [cname], row(src), row(lc), low, A.max, A.add, rk + [lc], c)
 
-    def tabm(cname, out, wk, col):
-        ts(out, wk, sampled(cname), -1.0, cl(col), A.mult, A.add, [cname, "col%d" % col])
-
-    def load(eng, sem, out, src, key):
-        op(eng, lambda: Q[eng].dma_start(out, src), [], [key], 0.07, sem=sem, inc=16, lat=2.0)
-    load("y", "dfl", T.fl_s[:], T.fl[:], "fl_s")
-    load("s", "dx", T.xin[:], T.x[:], "xin")
-    load("y", "dml", T.ml_s[:], T.ml[:], "ml_s")
-    load("y", "du", T.uin[:], T.u[:], "uin")
-    load("y", "dwc", T.wq[:, 0:512].bitcast(dt.uint8), T.wc[:], "wq")
-    load("y", "dws", T.wqs[:, 0:512], T.ws[:], "wqs")
-    load("y", "dv", T.vin[:], T.v[:], "vin")
-
-    def iota(out, wk, pattern, base, cm, n, flag=True):
-        c = 0.15 + 0.00166 * n
-        if flag:
-            op("g", lambda: g.iota(out, pattern, base, cm, allow_small_or_imprecise_dtypes=True), [], wk, c)
+    def tabs(cname, out, wk, col, scale=None):
+        if scale:
+            ts(out, wk, sampled(cname), scale, cl(col), A.mult, A.add, [cname, "col%d" % col])
         else:
-            op("g", lambda: g.iota(out, pattern, base, cm), [], wk, c)
+            ts(out, wk, sampled(cname), cl(col), None, A.add, None, [cname, "col%d" % col])
+
+    def load(eng, sem, out, src, key, lat):
+        op(eng, lambda: Q[eng].dma_start(out, src), [], [key], 0.07, sem=sem, inc=16, lat=lat)
+    load("y", "dfl", T.fl_s[:], T.fl[:], "fl_s", 1.9)
+    load("s", "dx", T.xin[:], T.x[:], "xin", 4.2)
+    load("y", "dml", T.ml_s[:], T.ml[:], "ml_s", 2.0)
+    load("y", "du", T.uin[:], T.u[:], "uin", 2.6)
+    load("y", "dwc", T.wq[:, 0:512].bitcast(dt.uint8), T.wc[:], "wq", 3.2)
+    load("y", "dws", T.wqs[:, 0:512], T.ws[:], "wqs", 2.4)
+    load("y", "dv", T.vin[:], T.v[:], "vin", 2.6)
+
+    def iota(out, wk, pattern, base, cm, n, flag=True, rk=()):
+        c = 0.13 + 2 * CYC * n
+        if flag:
+            op("g", lambda: g.iota(out, pattern, base, cm, allow_small_or_imprecise_dtypes=True), list(rk), wk, c)
+        else:
+            op("g", lambda: g.iota(out, pattern, base, cm), list(rk), wk, c)
     iota(T.pq[:], ["pq"], [[0, TW]], 0, 1, TW, False)
     iota(T.t16[:], ["t16"], [[1, 16]], 0, 0, 16)
-    iota(T.ramp[:], ["ramp"], [[1, C + 16]], -224, 0, C + 16)
-    iota(row("k0"), ["k0"], [[1024, C]], 0, 0, C)
-    iota(row("k0m"), ["k0m"], [[1024, C]], -1, 0, C)
-    iota(tf("jt"), ["jt0"], [[16, TW]], 0, 0, TW)
-    iota(T.ofi[:], ["ofi"], [[16, 8]], 0, 0, 8, False)
-    iota(row("cpr"), ["cpr"], [[-1, C]], 449, 0, C)
-    iota(row("kd"), ["kd"], [[1024, C]], -1536, 0, C)
-    iota(row("kc"), ["kc"], [[1024, C]], -512, 0, C)
+    iota(T.ramp[:], ["ramp"], [[1, C + 16]], -224, 0, C + 16, rk=[">pq", ">t16"])
+    iota(tf("jt"), ["jt0"], [[16, TW]], 0, 0, TW, rk=[">ramp"])
+    iota(T.ofi[:], ["ofi"], [[16, 8]], 0, 0, 8, False, rk=[">ramp"])
+    iota(T.et[:], ["et"], [[0, 2048]], 0, 0, 2048, rk=[">jt0", ">ofi"])
+    act(row("k0m"), ["k0m"], row("ramp"), ["ramp"], R4, bias=-STEP1)
+    ts(row("code9"), ["code9"], row("ramp"), 2.0 ** -9, None, A.mult, None, ["ramp"], R2)
     ts(T.pqm[:], ["pqm"], T.pq[:], 15, None, A.bitwise_and, None, ["pq"])
     cp(cl(0), ["col0"], T.pqm[:, 0:1], ["pqm"])
     cp(T.ofq[:], ["ofq"], T.pqm[:], ["pqm"])
     ts(T.t16[:], ["t16"], T.t16[:], cl(0), None, A.subtract, None, ["t16", "col0"])
     ts(T.la16[:], ["la16"], T.t16[:], 0.0, -1024.0, A.is_lt, A.mult, ["t16"])
     ts(T.lb16[:], ["lb16"], T.t16[:], 0.0, 512.0, A.is_equal, A.mult, ["t16"])
+    ts(T.lc16[:], ["lc16"], T.t16[:], 15.0, -1024.0, A.is_equal, A.mult, ["t16"])
     tt(T.la16[:], ["la16"], T.la16[:], T.lb16[:], A.add, ["la16", "lb16"])
-    ts(T.lb16[:], ["lb16"], T.t16[:], 15.0, -1024.0, A.is_equal, A.mult, ["t16"])
-    tt(T.lc16[:], ["lc16"], T.la16[:], T.lb16[:], A.add, ["la16", "lb16"])
-    act(row("lc"), ["lc"], T.lc16[:].indirect(T.ofq[:]), ["lc16", "ofq"])
-    act(row("lck"), ["lck"], row("lc"), ["lc"], 0.43, scale=1024.0)
+    tt(T.lc16[:], ["lc16"], T.la16[:], T.lc16[:], A.add, ["la16", "lc16"])
+    cp(row("lc"), ["lc"], T.lc16[:].indirect(T.ofq[:]), ["lc16", "ofq"], GAT)
+    ts(row("lc9"), ["lc9"], row("lc"), 2.0 ** -9, None, A.mult, None, ["lc"], R2)
     ts(cl(1), ["col1"], cl(0), 0.0, 1024.0, A.is_equal, A.mult, ["col0"])
-    ts(cl(1), ["col1"], cl(1), -512.0, None, A.add, None, ["col1"])
-    ts(cl(2), ["col2"], cl(1), 224.0, None, A.add, None, ["col1"])
-    ts(cl(3), ["col3"], cl(1), 1024.0, 511.0, A.mult, A.add, ["col1"])
-    ts(cl(8), ["col8"], cl(1), 1024.0, 512.0, A.mult, A.add, ["col1"])
-    ts(cl(7), ["col7"], cl(1), -2.0, 1.0, A.mult, A.add, ["col1"])
-    ts(cl(6), ["col6"], cl(1), 511.0 / 1024 + 0.01, None, A.add, None, ["col1"])
-    ts(cl(4), ["col4"], cl(1), -1.0, 449.0, A.mult, A.add, ["col1"])
-    ts(cl(5), ["col5"], cl(1), -1.0, 224.0, A.mult, A.add, ["col1"])
-    for n in ["cp", "rst", "pm", "cm"]:
-        op("v", lambda n=n: g.vector.memset(T[n][:, 0:1], 0.0), [], [n + "0"])
-    op("v", lambda: g.vector.memset(T.ar[:, 0:1], 0.0), [], ["ar0"])
-    op("v", lambda: g.vector.memset(T.et[:], 0.5), [], ["et1"], 0.5)
-    op("g", lambda: g.affine_select(T.et[:], T.et[:], [[-1, 4], [1, 512]], A.is_equal, 0.0, 0, -4), ["et1"], ["et"], 3.6)
+    ts(cl(2), ["col2"], cl(1), 224.0 - 512.0, None, A.add, None, ["col1"])
+    ts(cl(3), ["col3"], cl(2), 1024.0, 511.0, A.mult, A.add, ["col2"])
+    ts(cl(4), ["col4"], cl(2), 511.0 / 1024 + 0.01, None, A.add, None, ["col2"])
+    ts(cl(5), ["col5"], cl(2), 511.0 / 1024 + 1.01, None, A.add, None, ["col2"])
+    ts(cl(6), ["col6"], cl(2), -1.0, 1.0, A.mult, A.add, ["col2"])
+    ts(cl(7), ["col7"], cl(2), -2.0, 449.0, A.mult, A.add, ["col2"])
+    ts(cl(8), ["col8"], cl(2), -1.0, None, A.add, None, ["col2"])
+    ts(cl(9), ["col9"], cl(2), -0.5, 0.5, A.mult, A.add, ["col2"])
+    ts(cl(10), ["col10"], cl(2), 4.0, 3.0, A.mult, A.add, ["col2"])
+    op("v", lambda: g.vector.memset(T.rst[:, 0:1], BIG), [], ["rst0"])
+    op("v", lambda: g.vector.memset(T.cum[:, 0:1], -224.0 * STEP1), [], ["cum0"])
+    op("v", lambda: g.vector.memset(T.half[:], 0.5), [], ["half"])
+    for b in range(4):
+        op("g", lambda b=b: g.affine_select(T.et[:, 512 * b + b:512 * b + 512:4], T.half[:], [[1, 128]], A.is_equal, 0.0, 0, -1), ["et", "half"], ["et%d" % b], 0.17 + 256 * CYC)
     cp(tu("tab0"), ["tu.tab0"], T.fl_s[:], ["fl_s"])
 
     KS, KM = ["ka", "kb"], ["kma", "kmb"]
 
-    def frow():
+    def levels(first):
         act(row("ro0"), ["ro0"], T.ramp[:].indirect(tu("tab0")), ["ramp", "tu.tab0"])
-
-    def levels():
         for k in range(9):
             if k < 8:
                 a, b = "ro%d" % k, "ro%d" % (k + 1)
                 act(row(b), [b], row(a).indirect(tu("tab%d" % k)), [a, "tu.tab%d" % k])
-            src = "k0" if k == 0 else KS[k % 2]
+            src = "ramp" if k == 0 else KS[k % 2]
             sm = "k0m" if k == 0 else KM[k % 2]
             dst, dm = KS[(k + 1) % 2], KM[(k + 1) % 2]
-            tt(row(dst), [dst], row(src).indirect(tu("tab%d" % k)), row(sm), A.min, [src, sm, "tu.tab%d" % k], GAT)
+            if first or k > 1:
+                tt(row(dst), [dst], row(src).indirect(tu("tab%d" % k)), row(sm), A.min, [src, sm, "tu.tab%d" % k], GAT)
             if k < 8:
                 c = "c%d" % (k % 2)
-                latch(row(b), b, row(c), c)
+                latch(b, [b], c)
                 tabs(c, tu("tab%d" % (k + 1)), ["tu.tab%d" % (k + 1)], 2)
-                act(row(dm), [dm], row(dst), [dst], 0.43, bias=-float(2 ** (k + 1)))
+                if k == 0 and not first:
+                    ts(tf("q0"), ["tf.q0"], tf("b"), 4.0, None, A.mult, None, ["tf.b"])
+                    ts(tf("q2"), ["tf.q2"], tf("f"), 4.0, 2.0, A.mult, A.add, ["tf.f"])
+                    tt(tf("q2"), ["tf.q2"], tf("q2"), tf("j4"), A.min, ["tf.q2", "tf.j4"])
+                    tabs(c, tf("q3"), ["tf.q3"], 10, 4.0)
+                    tt(tf("q0"), ["tf.q0"], tf("q0"), tf("q2"), A.min, ["tf.q0", "tf.q2"])
+                    tt(tf("q0"), ["tf.q0"], tf("q0"), tf("q3"), A.min, ["tf.q0", "tf.q3"])
+                    cp(tu("k2"), ["tu.k2"], tf("q0"), ["tf.q0"])
+                    act(row(KS[0]), [KS[0]], T.kw[:].indirect(tu("k2")), ["kw", "tu.k2"], scale=STEP1)
+                if first or k > 0:
+                    act(row(dm), [dm], row(dst), [dst], R4, bias=-STEP1 * 2 ** (k + 1))
 
     KF = KS[1]
 
-    def send(r, dst_name, src_name, rk, sem, code=False, w=C):
+    def send(r, o, i, rk, wk, sem, lat):
         dst = T.cores[rank ^ STEP[r]]
         rid, pid = topo.addr(dst)[0:2]
         m = topo.mask(core, dst)
         n = len(topo.engines(core, dst))
-        if code:
-            o, i = T[dst_name][:, 0:w].bitcast(dt.uint8), T[src_name][:, 0:w].bitcast(dt.uint8)
-        else:
-            o, i = T[dst_name][:, 0:w], T[src_name][:, 0:w]
         op("g", lambda: g.remote_dma(out_ap=o, in_ap=i, remote_sem=T.sem[sem], local_sem=T.sem.snt, pid=pid, routing_id=rid, dma_engine_mask=m),
-           rk, [dst_name], 0.5, lat=4.0 + (6.0 if code else 0.0), remote=(sem, n))
+           rk, [wk], 0.5, lat=OPT["REM"] + lat + OPT["RW"], remote=(sem, n))
+
+    sp = lambda r: T.sp[:, 3 * TW * r:3 * TW * (r + 1)]
+    sl = lambda r, a=0, b=TW: T.sl[:, TW * r + a:TW * r + b]
 
     def finish(r):
-        sp, sl = "sp%d" % r, "sl%d" % r
-        tt(row("yk"), ["yk"], row(KF).indirect(tu("tab0")), row("kc"), A.max, [KF, "tu.tab0", "kc"], GAT)
-        scan(row("ck"), ["ck"], row(KF), row("lck"), -1048576.0, A.max, A.add, [KF, "lck"])
-        ts(tu("root"), ["tu.root"], T.ck[:, 15:C:16], 2.0 ** -10, cl(6), A.mult, A.add, ["ck", "col6"])
-        ts(ti("k"), ["ti.k"], T.ck[:, 15:C:16], cl(3), None, A.add, None, ["ck", "col3"])
+        nxt = "tab1" if r and OPT["K2"] else "tab0"
+        tt(row("yk"), ["yk"], row(KF).indirect(tu(nxt)), row("kc"), A.max, [KF, "tu." + nxt, "kc"], GAT)
+        latch(KF, [KF], "ck", c=R4)
+        tabs("ck", tu("root1"), ["tu.root1"], 5)
+        tabs("ck", tu("root"), ["tu.root"], 4)
+        tabs("ck", ti("k"), ["ti.k"], 3, 1024.0)
         ts(ti("d"), ["ti.d"], ti("k"), 511, None, A.bitwise_and, None, ["ti.k"])
-        cp(T[sp][:, 2 * TW:3 * TW], [sp + "d"], ti("d"), ["ti.d"])
-        tt(tf("kmd"), ["tf.kmd"], ti("k"), ti("d"), A.subtract, ["ti.k", "ti.d"])
-        act(row("yr"), ["yr"], row("yk").indirect(tu("root")), ["yk", "tu.root"])
-        act(row("drow"), ["drow"], T.ramp[:].indirect(T[sp][:, 2 * TW:3 * TW]), ["ramp", sp + "d"])
-        scan(row("cs"), ["cs"], row("yk"), row("kd"), -1024.0 - 224.0 - 511.0, A.add, A.subtract, ["yk", "kd"])
-        tt(row("plg"), ["plg"], row("cs").indirect(tu("root")), row(KF), A.subtract, ["cs", "tu.root", KF], GAT)
-        latch(row("plg"), "plg", row("c2"), "c2")
-        tabs("c2", T[sp][:, 0:TW], [sp + "a"], 2)
-        op("v", lambda: g.vector.tensor_copy(win1("cp").indirect(T[sp][:, 0:TW]), row("cpr")), ["cpr", sp + "a", "cp0"], ["cp"], 1.4)
-        scan(row("cl"), ["cl"], row("yr"), row("lck"), -1048576.0, A.max, A.add, ["yr", "lck"])
-        ts(tf("lx"), ["tf.lx"], T["cl"][:, 15:C:16], cl(8), None, A.add, None, ["cl", "col8"])
-        tt(tf("ln"), ["tf.ln"], tf("lx"), tf("kmd"), A.subtract, ["tf.lx", "tf.kmd"])
-        cp(T[sp][:, TW:2 * TW], [sp + "b"], tf("ln"), ["tf.ln"])
-        tabs("c2", tf("pl"), ["tf.pl"], 2)
+        ts(tf("dq"), ["tf.dq"], ti("d"), cl(6), None, A.add, None, ["ti.d", "col6"])
+        cp(tu("d"), ["tu.d"], ti("d"), ["ti.d"])
+        act(row("drow"), ["drow"], T.ramp[:].indirect(tu("d")), ["ramp", "tu.d"])
+        scan(T.cum[:, 1:C + 1], ["cum"], row("yk"), row("kc"), -224.0 * STEP1, A.add, A.subtract, ["yk", "kc"])
+        ke = pick("erow", T.cum[:, 0:C + 1], lambda a, b: tu("root1", a, b), ["cum", "cum0", "tu.root1"], OPT["HE"], 1024.0)
+        act(row("srow"), ["srow"], T.cum[:, 0:C + 1].indirect(tu("root")), ["cum", "cum0", "tu.root"], scale=1024.0)
+        latch("erow", ke, "c2")
+        tt(tf("pl"), ["tf.pl"], sampled("c2"), tf("dq"), A.subtract, ["c2", "tf.dq"])
+        cp(tu("pl"), ["tu.pl"], tf("pl"), ["tf.pl"])
+        latch("srow", ["srow"], "c3")
+        tabs("c3", tf("st"), ["tf.st"], 2)
+        tt(tf("ln"), ["tf.ln"], sampled("c2"), sampled("c3"), A.subtract, ["c2", "c3"])
+        tt(tf("o"), ["tf.o"], tf("pl"), tf("st"), A.subtract, ["tf.pl", "tf.st"])
+        cp(sp(r), ["sp%d" % r], tf("o", 3), ["tf.o", "tf.ln", "tf.st"], 84 * CYC)
+        send(r, T["lp%d" % r][:], sp(r), ["sp%d" % r], "lp%d" % r, "al%d" % r, 0.35)
+        op("v", lambda: g.vector.tensor_copy(row("cp").indirect(tu("pl")), row("code9")), ["code9", "tu.pl", ">sp%d" % r], ["cp"], 1.45)
+        latch("cp", ["cp"], "c4", True)
+        tabs("c4", sl(r), ["sl%d" % r], 2, 512.0)
+        send(r, T["la%d" % r][:], sl(r), ["sl%d" % r], "la%d" % r, "aa%d" % r, 0.1)
+        tabs("c2", tu("last"), ["tu.last"], 8)
         ts(tf("ple"), ["tf.ple"], tf("pl"), cl(2), None, A.subtract, None, ["tf.pl", "col2"])
-        ts(tf("ple2"), ["tf.ple2"], tf("ple"), cl(2), None, A.subtract, None, ["tf.ple", "col2"])
-        tt(tf("cs"), ["tf.cs"], tf("pl"), ti("d"), A.add, ["tf.pl", "ti.d"])
-        cp(tu("end"), ["tu.end"], tf("cs"), ["tf.cs"])
-        ts(tf("c2"), ["tf.c2"], tf("cf"), -2.0, None, A.mult, None, ["tf.cf"])
-        ts(tf("pre0"), ["tf.pre0"], tf("cf"), cl(7), None, A.mult, None, ["tf.cf", "col7"])
-        tt(tf("pre"), ["tf.pre"], tf("pre0"), tf("hf"), A.add, ["tf.pre0", "tf.hf"])
-        send(r, "lp%d" % r, sp, [sp + "a", sp + "b", sp + "d"], "al%d" % r, w=3 * TW)
-        latch(row1("cp"), "cp", row("c4"), "c4")
-        tabm("c4", T[sl][:], [sl], 4)
-        send(r, "la%d" % r, sl, [sl], "aa%d" % r, w=TW)
+        act(row("plr"), ["plr"], T.ramp[:].indirect(tu("pl")), ["ramp", "tu.pl"])
 
-    def mm(dst, b, st, so, mv):
-        op("t", lambda: g.tensor.matmul_mx(T[dst][:, 512 * b:512 * b + C], T[st][:, so:so + 128], T[st + "s"][:, so:so + 128], T[mv][:, 0:C], T[mv + "s"][:, 0:C], True, True),
-           [st, st + "s", mv, mv + "s"], [dst + str(b)], 0.4)
+    def mm(dst, b, st, so, mv, a=0, z=C, rk=None):
+        op("t", lambda: g.tensor.matmul_mx(T[dst][:, 512 * b:512 * b + z - a], T[st][:, so:so + 128], T[st + "s"][:, so:so + 128], T[mv][:, a:z], T[mv + "s"][:, a:z], True, True),
+           [st, st + "s"] + (rk or [mv, mv + "s"]), [dst + str(b)], 0.5 * (z - a + 16) / (C + 16))
 
-    def quant(tile, keys, w, q):
-        op("v", lambda: g.vector.quantize_mx(T[q][:, 0:w], T[q + "s"][:, 0:w], T[tile][:, 0:4 * w]), keys, [q, q + "s"], 0.08 + 0.00088 * w)
+    def quant(tile, keys, w, q, a=0, wk=None):
+        op("v", lambda: g.vector.quantize_mx(T[q][:, a:a + w], T[q + "s"][:, a:a + w], T[tile][:, 4 * a:4 * (a + w)]), keys, wk or [q, q + "s"], 0.015 + 0.0011 * w)
 
     def state_made(r):
-        send(r, "lq%d" % r, "qx%d" % r, ["qx%d" % r], "aq%d" % r, code=True)
-        send(r, "lq%ds" % r, "qx%ds" % r, ["qx%ds" % r], "aq%d" % r)
-        mm("pb", 0, "qur", 0, "qx%d" % r)
-        act(row("sr"), ["sr"], T.pb[:, 0:C], ["pb0", "ro8"], 0.43)
+        q, l = "qx%d" % r, "lq%d" % r
+        send(r, T[l][:].bitcast(dt.uint8), T[q][:].bitcast(dt.uint8), [q], l, "aq%d" % r, 3.8)
+        send(r, T[l + "s"][:], T[q + "s"][:], [q + "s"], l + "s", "aq%d" % r, 1.0)
+        mm("pb", 0, "qur", 0, q)
+        act(row("sr"), ["sr"], T.pb[:, 0:C], ["pb0"], R4, scale=-1.0)
         for b in range(4):
-            mm("pa", b, "qe", 128 * b, "qx%d" % r)
+            mm("pa", b, "qe", 128 * b, q)
         for b in range(4):
-            mm("pb", b, "qe", 128 * b, "lq%d" % r)
+            mm("pb", b, "qe", 128 * b, l)
 
-    frow()
-    levels()
+    def halves(x, y, h, c):
+        tt(tf(h), ["tf." + h], tf(x), tf(y), A.add, ["tf." + x, "tf." + y])
+        ts(tf(h), ["tf." + h], tf(h), 0.5, None, A.mult, None, ["tf." + h])
+        tt(tf(c), ["tf." + c], tf(x), tf(h), A.subtract, ["tf." + x, "tf." + h])
+
+    def exchange(cname, s, h, c, x, tab):
+        tabs(cname, tf(s), ["tf." + s], 7, -2.0)
+        tt(tf(c), ["tf." + c], tf(s), tf(c), A.mult, ["tf." + s, "tf." + c])
+        tt(tf(x), ["tf." + x], tf(h), tf(c), A.add, ["tf." + h, "tf." + c])
+        cp(tu(tab), ["tu." + tab], tf(x), ["tf." + x])
+
+    levels(True)
     cp(tu("m"), ["tu.m"], T.ml_s[:], ["ml_s"])
     cp(tf("f"), ["tf.f"], T.fl_s[:], ["fl_s"])
     cp(tf("m"), ["tf.m"], T.ml_s[:], ["ml_s"])
-    act(row("fmr"), ["fmr"], row("ro0").indirect(tu("m")), ["ro0", "tu.m", "ro8"])
-    latch(row("fmr"), "fmr", row("c2"), "c2")
-    tabs("c2", tf("fm"), ["tf.fm"], 2)
-    tt(tf("hf"), ["tf.hf"], tf("fm"), tf("f"), A.add, ["tf.fm", "tf.f"])
-    ts(tf("hf"), ["tf.hf"], tf("hf"), 0.5, None, A.mult, None, ["tf.hf"])
-    tt(tf("cf"), ["tf.cf"], tf("f"), tf("hf"), A.subtract, ["tf.f", "tf.hf"])
+    act(row("fmr"), ["fmr"], row("ro0").indirect(tu("m")), ["ro0", "tu.m", ">ro8"])
+    latch("fmr", ["fmr"], "c8")
+    tabs("c8", tf("fm"), ["tf.fm"], 2)
+    halves("f", "fm", "hf", "cf")
     ts(tf("jt"), ["tf.jt"], tf("jt"), cl(0), None, A.add, None, ["jt0", "col0"])
-    tt(tf("hm"), ["tf.hm"], tf("m"), tf("jt"), A.add, ["tf.m", "tf.jt"])
-    ts(tf("hm"), ["tf.hm"], tf("hm"), 0.5, None, A.mult, None, ["tf.hm"])
-    tt(tf("cm"), ["tf.cm"], tf("jt"), tf("hm"), A.subtract, ["tf.jt", "tf.hm"])
-    ts(tf("sn"), ["tf.sn"], tf("cm"), 0.0, 2.0, A.is_lt, A.mult, ["tf.cm"])
-    ts(tu("sig"), ["tu.sig"], tf("sn"), 223.0, None, A.add, None, ["tf.sn"])
-    act(row("sgn"), ["sgn"], T.ramp[:].indirect(tu("sig")), ["ramp", "tu.sig", "ro8"])
-    quant("xin", ["xin", "tu.tab2"], C, "qx0")
+    ts(tf("j4"), ["tf.j4"], tf("jt"), 4.0, 1.0, A.mult, A.add, ["tf.jt"])
+    tt(tf("sn"), ["tf.sn"], tf("jt"), tf("m"), A.is_lt, ["tf.jt", "tf.m"])
+    ts(tf("oa"), ["tf.oa"], tf("sn"), -float(C), float(C), A.mult, A.add, ["tf.sn"])
+    ts(tf("ob"), ["tf.ob"], tf("sn"), float(C), None, A.mult, None, ["tf.sn"])
+    quant("xin", ["xin"], C, "qx0")
     quant("uin", ["uin"], 128, "qu")
     cp(T.ofu[:], ["ofu"], T.ofi[:], ["ofi"])
-    op("v", lambda: g.vector.tensor_copy(T.qur[:, 0:128].bitcast(dt.uint32), T.qu[:, 0:128].bitcast(dt.uint32).indirect(T.ofu[:, 0:8])), ["qu", "ofu"], ["qur"], 0.27)
-    op("s", lambda: g.scalar.activation(T.qurs[:, 0:128], T.qus[:, 0:128].indirect(T.ofu[:, 0:8]), AF.Copy), ["qus", "ofu"], ["qurs"], 0.27)
-    quant("et", ["et"], 512, "qe")
+    op("v", lambda: g.vector.tensor_copy(T.qur[:, 0:128].bitcast(dt.uint32), T.qu[:, 0:128].bitcast(dt.uint32).indirect(T.ofu[:, 0:8])), ["qu", "ofu"], ["qur"], gat(128))
+    op("s", lambda: g.scalar.activation(T.qurs[:, 0:128], T.qus[:, 0:128].indirect(T.ofu[:, 0:8]), AF.Copy), ["qus", "ofu"], ["qurs"], gat(128))
+    quant("et", ["et0", "et1", "et2", "et3"], 512, "qe")
     state_made(0)
+    iota(T.kw[:], ["kw"], [[1024, C], [1, 4]], -3 - 224 * 1024, 0, 4 * C, rk=[">et0", ">et1", ">et2", ">et3", ">qx0"])
+    act(row("kc"), ["kc"], row("ramp"), ["ramp", ">ro2"], R4, bias=-0.5)
     finish(0)
-    act(row("nsgn"), ["nsgn"], row("sgn"), ["sgn", "yr"], 0.43, scale=-1.0)
-    ts(tf("e1"), ["tf.e1"], ti("d"), 1.0, None, A.add, None, ["ti.d"])
-    tt(tf("wr"), ["tf.wr"], tf("e1"), tf("ln"), A.is_equal, ["tf.e1", "tf.ln"])
-    tt(tf("wl"), ["tf.wl"], tf("wr"), tf("ln"), A.mult, ["tf.wr", "tf.ln"])
-    tt(tf("pb"), ["tf.pb"], tf("pl"), tf("wl"), A.add, ["tf.pl", "tf.wl"])
-    ts(tu("b"), ["tu.b"], tf("pb"), -1.0, None, A.add, None, ["tf.pb"])
-    act(row("brow"), ["brow"], win1("cp").indirect(tu("b")), ["cp", "tu.b"], scale=-1.0, bias=225.0)
-    latch(row("brow"), "brow", row("c3"), "c3")
-    tabs("c3", tu("b"), ["tu.b"], 2)
+    ts(tf("e1"), ["tf.e1"], tf("o"), 0.0, None, A.is_equal, None, ["tf.o"])
+    tt(tf("e1"), ["tf.e1"], tf("e1"), tf("ln"), A.mult, ["tf.e1", "tf.ln"])
+    tt(tf("e1"), ["tf.e1"], tf("e1"), tf("pl"), A.add, ["tf.e1", "tf.pl"])
+    ts(tu("b"), ["tu.b"], tf("e1"), -1.0, None, A.add, None, ["tf.e1"])
+    act(row("brow"), ["brow"], row("cp").indirect(tu("b")), ["cp", "tu.b"], scale=512.0)
+    latch("brow", ["brow"], "c7")
+    tabs("c7", tu("b"), ["tu.b"], 2)
+    tabs("c7", tf("b"), ["tf.b"], 2)
+    act(row("mrow"), ["mrow"], T.ramp[:].indirect(tu("m")), ["ramp", "tu.m", ">ro8"])
+    act(row("mbr"), ["mbr"], row("mrow").indirect(tu("b")), ["mrow", "tu.b"])
+    latch("mbr", ["mbr"], "c8")
+    tabs("c8", tf("mb"), ["tf.mb"], 2)
+    halves("b", "mb", "hb", "cb")
 
-    grs = lambda i: T.gr[:, C * i:C * i + C]
+    def store(eng, out, src, keys, lat=2.0):
+        op(eng, lambda: Q[eng].dma_start(out, src), keys, [], 0.07, sem="outs", inc=16, lat=lat)
+
     for r in range(3):
-        sl, lp, la, sp = "sl%d" % r, "lp%d" % r, "la%d" % r, "sp%d" % r
+        lp, la, ks = "lp%d" % r, "la%d" % r, "sl%d" % r
         last = r == 2
-        act(row1("rst"), ["rst"], row("drow").indirect(T[sl][:]), ["drow", sl, "rst0"], scale=float(2 ** 90), bias=223.5 * float(2 ** 90))
-        cp(row("sa"), ["sa"], row("sr").indirect(T[sl][:]), ["sr", sl], GAT)
-        scan(row1("pm"), ["pm"], row("rst"), row("sa"), -float(2 ** 90), A.min, A.max, ["rst", "rst0", "sa", "pm0"])
-        tt(row("eq"), ["eq"], win1("pm").indirect(tu("end")), row("sr"), A.is_equal, ["pm", "tu.end", "sr"], GAT)
-        tt(row("cand"), ["cand"], row("eq").indirect(T[sl][:]), row1("cp"), A.mult, ["eq", sl, "cp"], GAT)
-        scan(row1("cm"), ["cm"], row("rst"), row("cand"), 0.0, A.min, A.max, ["rst", "cand", "cm0"])
-        act(T.lrow[:, 0:H], ["lrowa"], win1("cm").indirect(tu("end", 0, HW)), ["cm", "tu.end"], HALF, bias=-225.0)
-        ts(T.lrow[:, H:C], ["lrowb"], win1("cm").indirect(tu("end", HW)), -225.0, None, A.add, None, ["cm", "tu.end"], HALF)
-        latch(row("lrow"), ["lrowa", "lrowb"], row("c5"), "c5")
-        tabm("c5", tu("l"), ["tu.l"], 5)
-        act(row("plr"), ["plr"], T.ramp[:].indirect(T[sp][:, 0:TW]), ["ramp", sp + "a"])
+        act(T.rst[:, 1:C + 1], ["rst"], row("drow").indirect(sl(r)), ["drow", ks], scale=-BIG, bias=-223.5 * BIG)
+        ka = pick("sa", row("sr"), lambda a, b: sl(r, a, b), ["sr", ks], OPT["HA"])
+        scan(row("pm"), ["pm"], row("rst"), row("sa"), BIG, A.max, A.min, ["rst", "rst0"] + ka)
+        tt(row("neq"), ["neq"], row("pm").indirect(tu("last")), row("sr"), A.not_equal, ["pm", "tu.last", "sr"], GAT)
+        tt(row("cand"), ["cand"], row("neq").indirect(sl(r)), row("cp"), A.add, ["neq", ks, "cp"], GAT)
+        scan(row("cm"), ["cm"], row("rst"), row("cand"), BIG, A.max, A.min, ["rst", "rst0", "cand"], R2)
+        kl = pick("lrow", row("cm"), lambda a, b: tu("last", a, b), ["cm", "tu.last"], OPT["HL"], 512.0)
+        latch("lrow", kl, "c5")
+        tabs("c5", tu("l"), ["tu.l"], 2)
         for b in range(4):
-            act(row("fh%d" % b), ["fh%d" % b], T.pa[:, 512 * b:512 * b + C], ["pa%d" % b, "yr"], 0.43)
-        act(row("tcsr"), ["tcsr"], T.ramp[:].indirect(T[lp][:, 2 * TW:3 * TW]), ["ramp", lp])
-        act(row("tlenr"), ["tlenr"], T.ramp[:].indirect(T[lp][:, TW:2 * TW]), ["ramp", lp])
-        act(row("tplr"), ["tplr"], T.ramp[:].indirect(T[lp][:, 0:TW]), ["ramp", lp])
-        cp(grs(3), ["gr3"], row("tlenr").indirect(tu("l")), ["tlenr", "tu.l"], GAT)
-        act(grs(1), ["gr1"], row("plr").indirect(tu("l")), ["plr", "tu.l"])
-        cp(grs(2), ["gr2"], row("tcsr").indirect(tu("l")), ["tcsr", "tu.l"], GAT)
-        act(grs(0), ["gr0"], row("tplr").indirect(tu("l")), ["tplr", "tu.l"])
-        act(row1("ar"), ["ar"], T.ramp[:].indirect(T[la][:]), ["ramp", la, "ar0"])
-        for i in (3, 1, 2, 0):
-            latch(grs(i), "gr%d" % i, T.c4s[:, C * i:C * i + C], "c4s%d" % i)
-        x = lambda i: T.c4s[:, C * i + 15:C * i + C:16]
+            act(row("fh%d" % b), ["fh%d" % b], T.pa[:, 512 * b:512 * b + C], ["pa%d" % b], R4)
+        act(row("lenrow"), ["lenrow"], T.ramp[:].indirect(T[lp][:, TW:2 * TW]), ["ramp", lp])
+        act(row("orow"), ["orow"], T.ramp[:].indirect(T[lp][:, 0:TW]), ["ramp", lp])
+        act(row("strow"), ["strow"], T.ramp[:].indirect(T[lp][:, 2 * TW:3 * TW]), ["ramp", lp])
+        for i, n in enumerate(["lenrow", "plr", "orow", "strow"]):
+            kg = pick("gr%d" % i, row(n), lambda a, b: tu("l", a, b), [n, "tu.l"], {"v": 0, "s": TW, "h": 14}[OPT["BYL"][i]])
+            latch("gr%d" % i, kg, "x%d" % i)
+        act(row("ar"), ["ar"], T.ramp[:].indirect(T[la][:]), ["ramp", la])
+        xl, xp, xo, xs = [sampled("x%d" % i) for i in range(4)]
         for b in range(4):
-            act(row("ft%d" % b), ["ft%d" % b], T.pb[:, 512 * b:512 * b + C], ["pb%d" % b, "gr0"], 0.43)
-        ts(tf("l3"), ["tf.l3"], x(3), cl(2), None, A.add, None, ["c4s3", "col2"])
-        tt(tf("ng"), ["tf.ng"], tf("ple"), x(1), A.is_lt, ["c4s1", "tf.ple"])
-        tt(tf("vv"), ["tf.vv"], tf("ple2"), x(1), A.subtract, ["c4s1", "tf.ple2"])
-        tt(tf("vp"), ["tf.vp"], tf("pl"), x(1), A.subtract, ["c4s1", "tf.pl"])
-        op("v", lambda: g.vector.reciprocal(tf("inv"), tf("l3")), ["tf.l3"], ["tf.inv"], 0.33)
+            act(row("ft%d" % b), ["ft%d" % b], T.pb[:, 512 * b:512 * b + C], ["pb%d" % b], R4)
+        tabs("x0", tf("l3"), ["tf.l3"], 2)
+        op("v", lambda: g.vector.reciprocal(tf("inv"), tf("l3")), ["tf.l3"], ["tf.inv"], 0.19 + 6 * TW * CYC)
+        tabs("x0", tf("hl"), ["tf.hl"], 9, -0.5)
+        tt(tf("ng"), ["tf.ng"], tf("ple"), xp, A.is_lt, ["x1", "tf.ple"])
         tt(tf("t1"), ["tf.t1"], tf("ng"), tf("ln"), A.mult, ["tf.ng", "tf.ln"])
-        tt(tf("w"), ["tf.w"], x(2), tf("vv"), A.subtract, ["c4s2", "tf.vv"])
-        tt(tf("u"), ["tf.u"], tf("w"), tf("t1"), A.subtract, ["tf.w", "tf.t1"])
-        tt(tf("p0"), ["tf.p0"], x(0), tf("vp"), A.add, ["c4s0", "tf.vp"])
-        tt(tf("pi"), ["tf.pi"], tf("p0"), tf("t1"), A.add, ["tf.p0", "tf.t1"])
-        tt(tf("bq"), ["tf.bq"], tf("u"), tf("inv"), A.mult, ["tf.u", "tf.inv"])
-        ts(ti("n"), ["ti.n"], tf("bq"), -0.4989, None, A.add, None, ["tf.bq"])
+        tt(tf("w"), ["tf.w"], tf("pl"), xp, A.subtract, ["x1", "tf.pl"])
+        tt(tf("a1"), ["tf.a1"], tf("w"), tf("t1"), A.add, ["tf.w", "tf.t1"])
+        tt(tf("a2"), ["tf.a2"], xo, tf("hl"), A.add, ["x2", "tf.hl"])
+        tt(tf("u"), ["tf.u"], tf("a1"), tf("a2"), A.add, ["tf.a1", "tf.a2"])
+        tt(ti("n"), ["ti.n"], tf("u"), tf("inv"), A.mult, ["tf.u", "tf.inv"])
+        tt(tf("m1"), ["tf.m1"], xs, tf("hl"), A.subtract, ["x3", "tf.hl"])
         tt(tf("t2"), ["tf.t2"], ti("n"), tf("l3"), A.mult, ["ti.n", "tf.l3"])
-        tt(tf("tp"), ["tf.tp"], tf("pi"), tf("t2"), A.add, ["tf.pi", "tf.t2"])
-        cp(tu("tp"), ["tu.tp"], tf("tp"), ["tf.tp"])
-        act(T.trow[:, 0:H], ["trowa"], win1("ar").indirect(tu("tp", 0, HW)), ["ar", "tu.tp"], HALF)
-        cp(T.trow[:, H:C], ["trowb"], win1("ar").indirect(tu("tp", HW)), ["ar", "tu.tp"], HALF)
-        latch(row("trow"), ["trowa", "trowb"], row("c5"), "c5")
-        tabs("c5", tu("T"), ["tu.T"], 2)
-        tt(row("mu"), ["mu"], row("sr").indirect(tu("T")), row("sgn"), A.mult, ["sr", "tu.T", "sgn"], GAT)
+        tt(tf("bq"), ["tf.bq"], tf("m1"), tf("u"), A.add, ["tf.m1", "tf.u"])
+        tt(tf("tp"), ["tf.tp"], tf("bq"), tf("t2"), A.subtract, ["tf.bq", "tf.t2"])
+        for x in "ab":
+            tt(tf("b" + x), ["tf.b" + x], tf("bq"), tf("o" + x), A.add, ["tf.bq", "tf.o" + x])
+            tt(tf("tp" + x), ["tf.tp" + x], tf("b" + x), tf("t2"), A.subtract, ["tf.b" + x, "tf.t2"])
+        ts(tu("tp", 0, 3 * TW), ["tu.tp"], tf("tp", 3), cl(2), None, A.add, None, ["tf.tp", "tf.tpa", "tf.tpb", "col2"], 84 * CYC)
+        kt = pick("trow", row("ar"), lambda a, b: tu("tp", a, b), ["ar", "tu.tp"], OPT["HT"] if last else TW)
+        latch("trow", kt, "c6")
+        tabs("c6", tu("T"), ["tu.T"], 2)
+        zd = 0 if last else OPT["ZD"]
+        act(row("sfa"), ["sfa"], row("sr").indirect(T[la][:]), ["sr", la])
+        act(row("sfa", C, 2 * C), ["sfb"], row("sfa"), ["sfa"], R4, scale=-1.0)
+        cp(row("mu"), ["mu"], T.sfa[:].indirect(tu("tpa")), ["sfa", "sfb", "tu.tp"], GAT)
+        act(row("nu"), ["nu"], T.sfa[:].indirect(tu("tpb")), ["sfa", "sfb", "tu.tp"])
+        tt(row("sw"), ["sw"], row("mu").indirect(tu("m")), row("nu"), A.is_gt, ["mu", "nu", "tu.m"], GAT)
+        latch("sw", ["sw"], "c5")
+        exchange("c5", "sw", "hf", "cf", "f", "tab0")
+        act(row("swb"), ["swb"], row("sw").indirect(tu("b")), ["sw", "tu.b"])
+        latch("swb", ["swb"], "c7")
+        exchange("c7", "swb", "hb", "cb", "b", "b")
+        z = 16 * zd
         for b in range(4):
-            act(row("fs%d" % b), ["fs%d" % b], row("ft%d" % b).indirect(tu("T")), ["ft%d" % b, "tu.T"])
-        tt(row("nu"), ["nu"], row("sr").indirect(tu("T")), row("nsgn"), A.mult, ["sr", "tu.T", "nsgn"], GAT)
-        tt(row("sw"), ["sw"], row("mu").indirect(tu("m")), row("nu"), A.is_lt, ["mu", "nu", "tu.m"], GAT)
-        latch(row("sw"), "sw", row("c5"), "c5")
-        ts(tf("sw"), ["tf.sw"], sampled("c5"), -2.0, cl(7), A.mult, A.add, ["c5", "col7"])
-        tt(tf("si"), ["tf.si"], sampled("c5"), tf("c2"), A.mult, ["c5", "tf.c2"])
-        tt(tf("f"), ["tf.f"], tf("si"), tf("pre"), A.add, ["tf.si", "tf.pre"])
-        tt(tf("cf"), ["tf.cf"], tf("sw"), tf("cf"), A.mult, ["tf.sw", "tf.cf"])
-        cp(tu("tab0"), ["tu.tab0"], tf("f"), ["tf.f"])
-        for b in range(4):
-            tt(T.zt[:, b:4 * C:4], ["zt%d" % b], row("fh%d" % b).indirect(tu("tab0")), row("fs%d" % b), A.add, ["fh%d" % b, "fs%d" % b, "tu.tab0"], GAT)
-        quant("zt", ["zt0", "zt1", "zt2", "zt3"], C, "qz")
+            fh, ft, fs = "fh%d" % b, "ft%d" % b, "fs%d" % b
+            if zd:
+                act(T.zt[:, b:4 * z:4], ["zu%d" % b], row(ft).indirect(tu("T", 0, zd)), [ft, "tu.T"], gat(z))
+                act(T.za[:, b:4 * z:4], ["za%d" % b], row(fh).indirect(tu("tab0", 0, zd)), [fh, "tu.tab0"], gat(z))
+            if zd < TW:
+                act(row(fs, z, C), [fs], row(ft).indirect(tu("T", zd)), [ft, "tu.T"], gat(C - z))
+                tt(T.zt[:, 4 * z + b:4 * C:4], ["zt%d" % b], row(fh).indirect(tu("tab0", zd)), row(fs, z, C), A.add, [fh, fs, "tu.tab0"], gat(C - z))
+        if zd:
+            zk = ["zu%d" % b for b in range(4)]
+            op("g", lambda z=z: g.dma_start(T.zt[:, 0:4 * z], T.za[:, 0:4 * z], accum_op=A.add), zk + ["za%d" % b for b in range(4)], zk, 1.0, sem="zadd", inc=16, lat=OPT["DADD"] - 1.0)
+        quant("zt", ["zt0", "zt1", "zt2", "zt3", "zu0", "zu1", "zu2", "zu3"], C, "qz")
         for b in range(4):
             mm("pb", b, "wq", 128 * b, "qz")
-        tt(tf("sg"), ["tf.sg"], tf("sw"), tf("cm"), A.mult, ["tf.sw", "tf.cm"])
-        tt(tf("si"), ["tf.si"], tf("sg"), tf("hm"), A.add, ["tf.sg", "tf.hm"])
-        cp(tu("sig"), ["tu.sig"], tf("si"), ["tf.si"])
-        act(row("srow"), ["srow"], T.ramp[:].indirect(tu("sig")), ["ramp", "tu.sig"])
-        act(row("brow"), ["brow"], row("srow").indirect(tu("b")), ["srow", "tu.b"])
-        latch(row("brow"), "brow", row("c3"), "c3")
-        tabs("c3", tu("b"), ["tu.b"], 2)
         for b in range(4):
-            act(row("r2%d" % b), ["r2%d" % b], T.pb[:, 512 * b:512 * b + C], ["pb%d" % b], 0.43, scale=0.015625)
-        for b in range(4):
-            if b >= 4 - NP and not last:
-                act(row("pp%d" % b), ["pp%d" % b], row("r2%d" % b).indirect(tu("b")), ["r2%d" % b, "tu.b"])
-                tt(T.xt[:, b:4 * C:4], ["xt%d" % b], row("pp%d" % b), T.pa[:, 512 * b:512 * b + C], A.add, ["pp%d" % b, "pa%d" % b], 0.43)
+            act(row("r2%d" % b), ["r2%d" % b], T.pb[:, 512 * b:512 * b + C], ["pb%d" % b], R4, scale=0.015625)
+        for h, (a, z) in enumerate([(0, TW // 2), (TW // 2, TW)] if last and OPT["TAIL"] else [(0, TW)]):
+            n = 16 * (z - a)
+            for b in range(4):
+                out, key = T.xt[:, 64 * a + b:64 * z:4], "xt%d%d" % (h, b)
+                src = row("r2%d" % b).indirect(tu("b", a, z))
+                if b >= 4 - OPT["NP"][r]:
+                    act(row("pp%d" % b, 16 * a, 16 * z), ["pp%d%d" % (h, b)], src, ["r2%d" % b, "tu.b"], gat(n))
+                    tt(out, [key], row("pp%d" % b, 16 * a, 16 * z), T.pa[:, 512 * b + 16 * a:512 * b + 16 * z], A.add, ["pp%d%d" % (h, b), "pa%d" % b], n * CYC)
+                else:
+                    tt(out, [key], src, row("fh%d" % b, 16 * a, 16 * z), A.add, ["r2%d" % b, "fh%d" % b, "tu.b"], gat(n))
+            keys = ["xt%d%d" % (h, b) for b in range(4)]
+            if not last:
+                quant("xt", keys, C, "qx%d" % (r + 1))
                 continue
-            tt(T.xt[:, b:4 * C:4], ["xt%d" % b], row("r2%d" % b).indirect(tu("b")), row("fh%d" % b), A.add, ["r2%d" % b, "fh%d" % b, "tu.b"], GAT)
-        quant("xt", ["xt0", "xt1", "xt2", "xt3"], C, "qx%d" % (r + 1))
+            q = "qx3%d" % h
+            quant("xt", keys, n, "qx3", 16 * a, [q])
+            mm("pb", h, "qv", 0, "qx3", 16 * a, 16 * z, [q])
+            store("y", T.oc[:, 64 * a:64 * z], T.qx3[:, 16 * a:16 * z].bitcast(dt.uint8), [q], 1.8 + n / 400)
+            act(row("sa", 16 * a, 16 * z), ["y%d" % h, "saa", "sab"], T.pb[:, 512 * h:512 * h + n], ["pb%d" % h], n * CYC)
+            store("s", T.y[:, 16 * a:16 * z], row("sa", 16 * a, 16 * z), ["y%d" % h], 1.8 + n / 400)
         if last:
             break
-        frow()
-        levels()
+        levels(not OPT["K2"])
         state_made(r + 1)
         if r == 0:
             quant("vin", ["vin"], 128, "qv")
         finish(r + 1)
-    def store(eng, out, src, keys):
-        op(eng, lambda: Q[eng].dma_start(out, src), keys, [], 0.07, sem="outs", inc=16, lat=2.0)
     act(row("nlr"), ["nlr"], T.ramp[:].indirect(tu("tab0")), ["ramp", "tu.tab0"], bias=224.0)
     store("y", T.nl[:], T.nlr[0:128:16, :], ["nlr"])
-    mm("pb", 0, "qv", 0, "qx3")
-    store("y", T.oc[:], T.qx3[:, 0:C].bitcast(dt.uint8), ["qx3"])
-    act(row("ysb"), ["ysb"], T.pb[:, 0:C], ["pb0"], 0.43)
     for k in range(4):
-        store("y", T.osc[4 * k:4 * k + 4, :], T.qx3s[32 * k:32 * k + 4, 0:C], ["qx3s"])
-    store("s", T.y[:], row("ysb"), ["ysb"])
+        store("y", T.osc[4 * k:4 * k + 4, :], T.qx3s[32 * k:32 * k + 4, 0:C], ["qx30", "qx31"])
 
     n = len(prog)
     deps, kids = [set() for _ in range(n)], [[] for _ in range(n)]
@@ -403,55 +437,66 @@ def rank_program(g, core, T, topo):
                 deps[i].add(lw[k])
             deps[i].update(rd.get(k, []))
         for k in p["r"]:
+            if k[0] == ">":
+                deps[i].add(lw[k[1:]])
             rd.setdefault(k, []).append(i)
         for k in p["w"]:
             lw[k], rd[k] = i, []
         deps[i].discard(i)
         for d in deps[i]:
             kids[d].append(i)
+
+    def lay(rank_):
+        at, done, left, tq, link = [0.0] * n, [0.0] * n, [len(x) for x in deps], {e: 0.0 for e in Q}, 0.0
+        ready = {e: [] for e in Q}
+        for i in range(n):
+            if not left[i]:
+                ready[prog[i]["eng"]].append((0.0, i))
+        for _ in range(n):
+            t0, e = min((max(tq[e], min(ready[e])[0]), e) for e in Q if ready[e])
+            a, i = min((x for x in ready[e] if x[0] <= t0 + OPT["LOOK"]), key=lambda x: (rank_[x[1]], x[1]))
+            soon = [x for x in ready[e] if rank_[x[1]] < rank_[i] and x[0] - t0 + prog[x[1]]["c"] < OPT["KAP"] * prog[i]["c"]]
+            if soon:
+                a, i = min(soon)
+            ready[e].remove((a, i))
+            at[i] = max(t0, a)
+            tq[e] = at[i] + prog[i]["c"]
+            done[i] = tq[e] + prog[i]["lat"] + WAKE
+            if prog[i]["remote"]:
+                link = max(link, tq[e] + OPT["REM"]) + prog[i]["lat"] - OPT["REM"] - OPT["RW"]
+                done[i] = link + OPT["RW"] + WAKE
+            for k in kids[i]:
+                left[k] -= 1
+                if not left[k]:
+                    ready[prog[k]["eng"]].append((max(done[d] for d in deps[k]), k))
+        return at, done
+
     prio = [0.0] * n
     for i in range(n - 1, -1, -1):
-        prio[i] = prog[i]["c"] + prog[i]["lat"] + max([prio[k] + WAKE for k in kids[i]] + [0.0])
+        prio[i] = prog[i]["c"] + prog[i]["lat"] + WAKE + max([prio[k] for k in kids[i]] + [0.0])
     for i in range(n):
-        prio[i] += BIAS.get(prog[i]["w"][0].rstrip("0123456789") if prog[i]["w"] else "", 0.0)
-    done, left, tq, order = {}, [len(d) for d in deps], {e: 0.0 for e in Q}, []
-    ready = {e: [] for e in Q}
-    for i in range(n):
-        if not left[i]:
-            ready[prog[i]["eng"]].append((0.0, i))
-    while len(order) < n:
-        pick = None
-        for e in Q:
-            if not ready[e]:
-                continue
-            t0 = max(tq[e], min(a for a, i in ready[e]))
-            a, i = max((x for x in ready[e] if x[0] <= t0 + 1e-9), key=lambda x: (prio[x[1]], -x[1]))
-            if pick is None or t0 < pick[0]:
-                pick = (t0, e, a, i)
-        t0, e, a, i = pick
-        ready[e].remove((a, i))
-        order.append(i)
-        tq[e] = t0 + prog[i]["c"]
-        done[i] = tq[e] + prog[i]["lat"] + WAKE
-        for k in kids[i]:
-            left[k] -= 1
-            if not left[k]:
-                ready[prog[k]["eng"]].append((max(done[d] for d in deps[k]), k))
+        key = prog[i]["w"][0] if prog[i]["w"] else ""
+        prio[i] += OPT["BIAS"].get(key, OPT["BIAS"].get(key.rstrip("0123456789") + "*", 0.0))
+    at, done = lay([-x for x in prio])
+    order = sorted(range(n), key=lambda i: (at[i], i))
+    OPT["EST"] = max(done)
+    OPT["DBG"] = (prog, prio, kids, at)
+    OPT["LAY"] = (lay, deps)
 
     cnt = {s: 0 for s in SEMAPHORES}
     known = {e: {} for e in Q}
     clock, lastw, readers = {}, {}, {}
 
     def need(eng, ds):
-        best = {}
+        most = {}
         for s, v in ds:
-            best[s] = max(best.get(s, 0), v)
+            most[s] = max(most.get(s, 0), v)
         own = CS.get(eng)
-        for s in sorted(best, key=lambda x: (x == own, x)):
-            if known[eng].get(s, 0) >= best[s]:
+        for s in sorted(most, key=lambda x: (x == own, x)):
+            if known[eng].get(s, 0) >= most[s]:
                 continue
-            Q[eng].wait_ge(T.sem[s], best[s])
-            for x, y in clock[(s, best[s])].items():
+            Q[eng].wait_ge(T.sem[s], most[s])
+            for x, y in clock[(s, most[s])].items():
                 known[eng][x] = max(known[eng].get(x, 0), y)
 
     landed = {"aq%d" % i: 2 for i in range(3)}

@@ -1,10 +1,12 @@
+import math
+import numpy as np
 from concourse.mybir import dt, AluOpType, ActivationFunctionType
 
 C = 448
 TW = 28
 STEP = [1, 2, 3]
-OPT = {"NP": [1, 1, 0], "SA": True, "K2": True, "NU": False, "ZD": 0, "TAIL": True, "HE": 12, "HA": 0, "HL": 12, "HT": 12, "BYL": "vsss",
-       "WAKE": 0.15, "REM": 2.5, "RW": 0.9, "LOOK": 0.08, "KAP": 0.6, "BIAS": {"tf.swb": 5.0}, "DADD": 4.0}
+OPT = {"SR": [1, 0], "SK": [1, 1], "HE": 12, "HA": 0, "HL": 12, "HT": 12, "BYL": "vvss", "XCUT": [0, 20, 28], "SENDS": 2, "X3": True,
+       "RW": 0.9, "LOOK": 0.02, "KAP": 0.6, "PASS": 30, "ALPHA": 0.3, "TRIES": 40000, "HEAT": 0.2, "SEED": 1}
 SCRATCH = {}
 
 
@@ -15,15 +17,15 @@ def _decl():
     SCRATCH["sfa"] = ("sbuf", [128, 2 * C], f32)
     for n in ["cum", "rst", "ramp"]:
         SCRATCH[n] = ("sbuf", [128, C + 16], bf)
-    for n in ["neq", "cand", "cm", "cp", "code9", "lrow", "plr", "orow", "strow", "lenrow", "trow", "dif", "sw", "swb", "brow", "mrow", "mbr", "lc", "lc9", "fmr",
-              "erow", "srow", "drow", "ar", "sgn"]:
+    for n in ["neq", "cand", "cm", "cp", "code9", "lrow", "plr", "tprow", "tdrow", "lenrow", "trow", "sw", "swb", "brow", "mrow", "mbr", "lc", "lc9", "fmr",
+              "erow", "srow", "drow", "ar"]:
         SCRATCH[n] = ("sbuf", [128, C], bf)
     SCRATCH["ro"] = ("sbuf", [128, 9 * C], bf)
     SCRATCH["cc"] = ("sbuf", [128, 10 * C], f16)
     SCRATCH["c4s"] = ("sbuf", [128, 4 * C], f16)
-    for n in ["gr", "fh", "ft", "fs", "xin", "xt", "zt", "za"]:
+    for n in ["gr", "fh", "ft", "fs", "xin", "xt", "zt"]:
         SCRATCH[n] = ("sbuf", [128, 4 * C], bf)
-    for n in ["pp", "r2", "kw"]:
+    for n in ["r2", "kw"]:
         SCRATCH[n] = ("sbuf", [128, 4 * C], f32)
     for n in ["uin", "vin"]:
         SCRATCH[n] = ("sbuf", [128, 512], bf)
@@ -35,25 +37,29 @@ def _decl():
     for n, w, t in [("fl_s", TW, "int32"), ("ml_s", TW, "int32"), ("pq", TW, "int32"), ("pqm", TW, "int32"), ("ofq", TW, "uint16"), ("ofi", 8, "int32"), ("ofu", 8, "uint16"),
                     ("col", 12, f32), ("tf", TW * 50, f32), ("ti", TW * 4, "int32"), ("tu", TW * 24, "uint16"), ("t16", 16, bf), ("la16", 16, bf), ("lb16", 16, bf), ("lc16", 16, bf)]:
         SCRATCH[n] = ("sbuf", [128, w], t)
-    SCRATCH["sp"] = ("sbuf", [128, 3 * 3 * TW], "uint16")
-    SCRATCH["sl"] = ("sbuf", [128, 3 * TW], "uint16")
+    SCRATCH["sp"] = ("sbuf", [128, 3 * 4 * TW], "uint16")
     for i in range(3):
-        SCRATCH["lp%d" % i] = ("sbuf", [128, 3 * TW], "uint16")
-        SCRATCH["la%d" % i] = ("sbuf", [128, TW], "uint16")
+        for x in "dpla":
+            SCRATCH["l%s%d" % (x, i)] = ("sbuf", [128, 3 * TW], "uint16")
     SCRATCH["pa"] = ("psum", [128, 2048], f32)
     SCRATCH["pb"] = ("psum", [128, 2048], f32)
 
 
 _decl()
 LOADS = ["dfl", "dml", "dx", "du", "dv", "dwc", "dws"]
-SEMAPHORES = ["cv", "cs_", "ct", "cg", "snt", "outs", "zadd"] + LOADS + ["%s%d" % (n, i) for n in ("aq", "al", "aa") for i in range(3)]
-TF = {n: i for i, n in enumerate(["jt", "f", "m", "hf", "fm", "cf", "hb", "cb", "b", "mb", "sn", "dq", "pl", "ple", "o", "ln", "st", "l3", "inv", "ng", "t1", "w", "a1", "hl", "a2",
-                                  "u", "m1", "bq", "t2", "tp", "tpa", "tpb", "sw", "swb", "e1", "j4", "q0", "q2", "q3", "oa", "ob", "ba", "bb"])}
-TU = {n: i for i, n in enumerate(["tab%d" % k for k in range(9)] + ["m", "root", "root1", "l", "tp", "tpa", "tpb", "T", "sig", "b", "last", "pl", "d", "k2"])}
+SEMAPHORES = ["cv", "cs_", "ct", "cg", "snt", "outs"] + LOADS + ["a%s%d" % (n, i) for n in "qdpla" for i in range(3)]
+TF = {n: i for i, n in enumerate(["jt", "f", "m", "hf", "fm", "cf", "fp", "fq", "fr", "hb", "cb", "b", "mb", "sn", "dq", "pl", "ple", "ln", "l3", "inv", "ng", "t1", "w", "a1", "hl", "a2",
+                                  "u", "bq", "t2", "tp", "tpa", "tpb", "sw", "swb", "e1", "j4", "q0", "q2", "oa", "ob", "ba", "bb"])}
+TU = {n: i for i, n in enumerate(["tab%d" % k for k in range(9)] + ["m", "root", "root1", "l", "tp", "tpa", "tpb", "T", "b", "last", "k2"])}
 TI = {"k": 0, "d": 1, "n": 2}
-CYC = 0.83e-3 * 1.25
 BIG = float(2 ** 90)
 STEP1 = 2.0 ** -10
+CYC = 0.83e-3 * np.array([1.25, 1.05, 1.45])
+GEL = 0.83e-3 * np.array([1.56, 1.95, 1.15])
+SCA = 0.05 + 0.83e-3 * C * np.array([3.8, 5.5, 2.0])
+MMS = np.array([0.5, 0.62, 0.38])
+WAKES, STARTS, RATES = [0.15, 0.2, 0.09], [2.5, 4.0, 1.8], [1.0, 1.3, 0.5]
+ORDER = {}
 
 
 def rank_program(g, core, T, topo):
@@ -64,29 +70,29 @@ def rank_program(g, core, T, topo):
     AF = ActivationFunctionType
     Q = {"v": g.vector, "s": g.scalar, "t": g.tensor, "g": g, "y": g.sync}
     CS = {"v": "cv", "s": "cs_", "t": "ct", "g": "cg"}
-    WAKE = OPT["WAKE"]
     prog = []
     TINY, R2, R4 = 64 * CYC, C // 2 * CYC, C * CYC
-    gat = lambda n=C: 0.055 + 0.0013 * n
+    gat = lambda n=C: 0.055 + GEL * n
     GAT = gat()
 
     def op(eng, fn, reads, writes, cost=TINY, sem=None, inc=1, lat=0.0, remote=None):
-        prog.append({"eng": eng, "fn": fn, "r": reads, "w": writes, "c": cost, "sem": sem, "inc": inc, "lat": lat, "remote": remote})
+        cost = [float(x) for x in cost + 0 * CYC]
+        prog.append({"eng": eng, "fn": fn, "r": reads, "w": writes, "c": cost[0], "cs": cost, "sem": sem, "inc": inc, "lat": lat, "remote": remote})
 
     tf = lambda n, k=1: T.tf[:, TW * TF[n]:TW * (TF[n] + k)]
     tu = lambda n, a=0, b=TW: T.tu[:, TW * TU[n] + a:TW * TU[n] + b]
     ti = lambda n: T.ti[:, TW * TI[n]:TW * TI[n] + TW]
     cl = lambda i: T.col[:, i:i + 1]
     SLOT = {"%s%d" % (n, k): (m, C * k) for n, m, z in (("ro", "ro", 9), ("c", "cc", 10), ("gr", "gr", 4), ("x", "c4s", 4), ("fh", "fh", 4), ("ft", "ft", 4), ("fs", "fs", 4),
-                                                       ("pp", "pp", 4), ("r2", "r2", 4)) for k in range(z)}
+                                                       ("r2", "r2", 4)) for k in range(z)}
 
     def row(n, a=0, b=C):
         n, s = SLOT.get(n, (n, 0))
         return T[n][:, s + a:s + b]
 
-    def sampled(n):
-        n, a = SLOT.get(n, (n, 0))
-        return T[n][:, a + 15:a + C:16]
+    def sampled(n, a=0, b=TW):
+        n, s = SLOT.get(n, (n, 0))
+        return T[n][:, s + 16 * a + 15:s + 16 * b:16]
 
     def tt(out, wk, a, b, o, rk, c=TINY):
         op("v", lambda: g.vector.tensor_tensor(out, a, b, o), rk, wk, c)
@@ -100,8 +106,11 @@ def rank_program(g, core, T, topo):
     def cp(out, wk, a, rk, c=TINY):
         op("v", lambda: g.vector.tensor_copy(out, a), rk, wk, c)
 
-    def act(out, wk, a, rk, c=GAT, func=None, **kw):
-        op("s", lambda: g.scalar.activation(out, a, func or AF.Copy, **kw), rk, wk, c)
+    def t2(out, a, b, o):
+        tt(tf(out), ["tf." + out], tf(a), tf(b), o, ["tf." + a, "tf." + b])
+
+    def act(out, wk, a, rk, c=GAT, **kw):
+        op("s", lambda: g.scalar.activation(out, a, AF.Copy, **kw), rk, wk, c)
 
     def scan(out, wk, d0, d1, init, o0, o1, rk, c=R4):
         op("v", lambda: g.vector.tensor_tensor_scan(out, d0, d1, init, o0, o1), rk, wk, c)
@@ -144,11 +153,11 @@ def rank_program(g, core, T, topo):
             op("g", lambda: g.iota(out, pattern, base, cm), list(rk), wk, c)
     iota(T.pq[:], ["pq"], [[0, TW]], 0, 1, TW, False)
     iota(T.t16[:], ["t16"], [[1, 16]], 0, 0, 16)
-    iota(T.ramp[:], ["ramp"], [[1, C + 16]], -224, 0, C + 16, rk=[">pq", ">t16"])
+    iota(T.ramp[:], ["ramp", "rampa", "rampb"], [[1, C + 16]], -224, 0, C + 16, rk=[">pq", ">t16"])
     iota(tf("jt"), ["jt0"], [[16, TW]], 0, 0, TW, rk=[">ramp"])
     iota(T.ofi[:], ["ofi"], [[16, 8]], 0, 0, 8, False, rk=[">ramp"])
     iota(T.et[:], ["et"], [[0, 2048]], 0, 0, 2048, rk=[">jt0", ">ofi"])
-    act(row("k0m"), ["k0m"], row("ramp"), ["ramp"], R4, bias=-STEP1)
+    act(row("k0m"), ["k0ma", "k0mb"], row("ramp"), ["ramp"], R4, bias=-STEP1)
     ts(row("code9"), ["code9"], row("ramp"), 2.0 ** -9, None, A.mult, None, ["ramp"], R2)
     ts(T.pqm[:], ["pqm"], T.pq[:], 15, None, A.bitwise_and, None, ["pq"])
     cp(cl(0), ["col0"], T.pqm[:, 0:1], ["pqm"])
@@ -163,49 +172,50 @@ def rank_program(g, core, T, topo):
     ts(row("lc9"), ["lc9"], row("lc"), 2.0 ** -9, None, A.mult, None, ["lc"], R2)
     ts(cl(1), ["col1"], cl(0), 0.0, 1024.0, A.is_equal, A.mult, ["col0"])
     ts(cl(2), ["col2"], cl(1), 224.0 - 512.0, None, A.add, None, ["col1"])
-    ts(cl(3), ["col3"], cl(2), 1024.0, 511.0, A.mult, A.add, ["col2"])
-    ts(cl(4), ["col4"], cl(2), 511.0 / 1024 + 0.01, None, A.add, None, ["col2"])
-    ts(cl(5), ["col5"], cl(2), 511.0 / 1024 + 1.01, None, A.add, None, ["col2"])
-    ts(cl(6), ["col6"], cl(2), -1.0, 1.0, A.mult, A.add, ["col2"])
-    ts(cl(7), ["col7"], cl(2), -2.0, 449.0, A.mult, A.add, ["col2"])
-    ts(cl(8), ["col8"], cl(2), -1.0, None, A.add, None, ["col2"])
-    ts(cl(9), ["col9"], cl(2), -0.5, 0.5, A.mult, A.add, ["col2"])
-    ts(cl(10), ["col10"], cl(2), 4.0, 3.0, A.mult, A.add, ["col2"])
+    for k, (a, b) in enumerate([(1024.0, 511.0), (1.0, 511.0 / 1024 + 0.01), (1.0, 511.0 / 1024 + 1.01), (-1.0, 1.0), (-2.0, 449.0), (1.0, -1.0), (-1.5, -0.5), (4.0, 3.0), (-1.0, -0.75)], 3):
+        ts(cl(k), ["col%d" % k], cl(2), a, b, A.mult, A.add, ["col2"])
     op("v", lambda: g.vector.memset(T.rst[:, 0:1], BIG), [], ["rst0"])
     op("v", lambda: g.vector.memset(T.cum[:, 0:1], -224.0 * STEP1), [], ["cum0"])
     op("v", lambda: g.vector.memset(T.half[:], 0.5), [], ["half"])
     for b in range(4):
         op("g", lambda b=b: g.affine_select(T.et[:, 512 * b + b:512 * b + 512:4], T.half[:], [[1, 128]], A.is_equal, 0.0, 0, -1), ["et", "half"], ["et%d" % b], 0.17 + 256 * CYC)
-    cp(tu("tab0"), ["tu.tab0"], T.fl_s[:], ["fl_s"])
+    both = lambda n: [n + "a", n + "b"]
+    cp(tu("tab0"), ["tu.tab0"] + both("tu.tab0"), T.fl_s[:], ["fl_s"])
 
     KS, KM = ["ka", "kb"], ["kma", "kmb"]
 
     def levels(first):
-        act(row("ro0"), ["ro0"], T.ramp[:].indirect(tu("tab0")), ["ramp", "tu.tab0"])
+        SR, SK = OPT["SR"][0 if first else 1], OPT["SK"][0 if first else 1]
+        parts = lambda two: [("a", 0, TW // 2), ("b", TW // 2, TW)] if two else [("ab", 0, TW)]
+        some = lambda n, h: [n + x for x in h]
+        act(row("ro0"), both("ro0"), T.ramp[:].indirect(tu("tab0")), ["ramp"] + both("tu.tab0"))
         for k in range(9):
-            if k < 8:
-                a, b = "ro%d" % k, "ro%d" % (k + 1)
-                act(row(b), [b], row(a).indirect(tu("tab%d" % k)), [a, "tu.tab%d" % k])
+            tab, nxt = "tab%d" % k, "tab%d" % (k + 1)
+            a, b = "ro%d" % k, "ro%d" % (k + 1)
             src = "ramp" if k == 0 else KS[k % 2]
             sm = "k0m" if k == 0 else KM[k % 2]
             dst, dm = KS[(k + 1) % 2], KM[(k + 1) % 2]
-            if first or k > 1:
-                tt(row(dst), [dst], row(src).indirect(tu("tab%d" % k)), row(sm), A.min, [src, sm, "tu.tab%d" % k], GAT)
-            if k < 8:
-                c = "c%d" % (k % 2)
-                latch(b, [b], c)
-                tabs(c, tu("tab%d" % (k + 1)), ["tu.tab%d" % (k + 1)], 2)
-                if k == 0 and not first:
-                    ts(tf("q0"), ["tf.q0"], tf("b"), 4.0, None, A.mult, None, ["tf.b"])
-                    ts(tf("q2"), ["tf.q2"], tf("f"), 4.0, 2.0, A.mult, A.add, ["tf.f"])
-                    tt(tf("q2"), ["tf.q2"], tf("q2"), tf("j4"), A.min, ["tf.q2", "tf.j4"])
-                    tabs(c, tf("q3"), ["tf.q3"], 10, 4.0)
-                    tt(tf("q0"), ["tf.q0"], tf("q0"), tf("q2"), A.min, ["tf.q0", "tf.q2"])
-                    tt(tf("q0"), ["tf.q0"], tf("q0"), tf("q3"), A.min, ["tf.q0", "tf.q3"])
-                    cp(tu("k2"), ["tu.k2"], tf("q0"), ["tf.q0"])
-                    act(row(KS[0]), [KS[0]], T.kw[:].indirect(tu("k2")), ["kw", "tu.k2"], scale=STEP1)
-                if first or k > 0:
-                    act(row(dm), [dm], row(dst), [dst], R4, bias=-STEP1 * 2 ** (k + 1))
+            c = "c%d" % (k % 2)
+            for h, x, y in parts(SR) if k < 8 else []:
+                act(row(b, 16 * x, 16 * y), some(b, h), row(a).indirect(tu(tab, x, y)), both(a) + some("tu." + tab, h), gat(16 * (y - x)))
+            for h, x, y in parts(SK) if first or k > 1 else []:
+                tt(row(dst, 16 * x, 16 * y), some(dst, h), row(src).indirect(tu(tab, x, y)), row(sm, 16 * x, 16 * y), A.min,
+                   both(src) + some(sm, h) + some("tu." + tab, h), gat(16 * (y - x)))
+            if k == 8:
+                break
+            for h, x, y in parts(SR):
+                scan(row(c, 16 * x, 16 * y), some(c, h), row(b, 16 * x, 16 * y), row("lc", 16 * x, 16 * y), -1024.0, A.max, A.add, some(b, h) + ["lc"], 8 * (y - x) * CYC)
+                ts(tu(nxt, x, y), some("tu." + nxt, h), sampled(c, x, y), cl(2), None, A.add, None, some(c, h) + ["col2"])
+            if k == 0 and not first:
+                ts(tf("q0"), ["tf.q0"], tf("b"), cl(11), None, A.add, None, ["tf.b", "col11"])
+                ts(tf("q2"), ["tf.q2"], tf("f"), cl(11), 0.5, A.add, A.add, ["tf.f", "col11"])
+                t2("q2", "q2", "j4", A.min)
+                t2("q0", "q0", "q2", A.min)
+                tt(tf("q0"), ["tf.q0"], tf("q0"), sampled(c), A.min, ["tf.q0"] + both(c))
+                ts(tu("k2"), ["tu.k2"], tf("q0"), 4.0, cl(10), A.mult, A.add, ["tf.q0", "col10"])
+                act(row(KS[0]), both(KS[0]), T.kw[:].indirect(tu("k2")), ["kw", "tu.k2"], scale=STEP1)
+            for h, x, y in parts(SK) if first or k > 0 else []:
+                act(row(dm, 16 * x, 16 * y), some(dm, h), row(dst, 16 * x, 16 * y), some(dst, h), 16 * (y - x) * CYC, bias=-STEP1 * 2 ** (k + 1))
 
     KF = KS[1]
 
@@ -215,53 +225,57 @@ def rank_program(g, core, T, topo):
         m = topo.mask(core, dst)
         n = len(topo.engines(core, dst))
         op("g", lambda: g.remote_dma(out_ap=o, in_ap=i, remote_sem=T.sem[sem], local_sem=T.sem.snt, pid=pid, routing_id=rid, dma_engine_mask=m),
-           rk, [wk], 0.5, lat=OPT["REM"] + lat + OPT["RW"], remote=(sem, n))
+           rk, wk, 0.5, lat=lat, remote=(sem, n))
 
-    sp = lambda r: T.sp[:, 3 * TW * r:3 * TW * (r + 1)]
-    sl = lambda r, a=0, b=TW: T.sl[:, TW * r + a:TW * r + b]
+    sp = lambda r, x, a=0, b=TW: T.sp[:, TW * (4 * r + "dpla".index(x)) + a:TW * (4 * r + "dpla".index(x)) + b]
+    PARCELS = {1: ["dpl", "a"], 2: ["d", "pl", "a"], 3: ["d", "p", "l", "a"], 4: ["dp", "l", "a"]}[OPT["SENDS"]]
+
+    def landed(r, x):
+        p = [y for y in PARCELS if x in y][0]
+        return T["l%s%d" % (p[0], r)][:, TW * p.index(x):TW * p.index(x) + TW]
 
     def finish(r):
-        nxt = "tab1" if r and OPT["K2"] else "tab0"
-        tt(row("yk"), ["yk"], row(KF).indirect(tu(nxt)), row("kc"), A.max, [KF, "tu." + nxt, "kc"], GAT)
-        latch(KF, [KF], "ck", c=R4)
+        nxt = "tu.tab1" if r else "tu.tab0"
+        kd, kp, kl, ka = ["sp%d%s" % (r, x) for x in "dpla"]
+        tt(row("yk"), ["yk"], row(KF).indirect(tu(nxt[3:])), row("kc"), A.max, both(KF) + both(nxt) + ["kc"], GAT)
+        latch(KF, both(KF), "ck", c=R4)
         tabs("ck", tu("root1"), ["tu.root1"], 5)
         tabs("ck", tu("root"), ["tu.root"], 4)
         tabs("ck", ti("k"), ["ti.k"], 3, 1024.0)
         ts(ti("d"), ["ti.d"], ti("k"), 511, None, A.bitwise_and, None, ["ti.k"])
         ts(tf("dq"), ["tf.dq"], ti("d"), cl(6), None, A.add, None, ["ti.d", "col6"])
-        cp(tu("d"), ["tu.d"], ti("d"), ["ti.d"])
-        act(row("drow"), ["drow"], T.ramp[:].indirect(tu("d")), ["ramp", "tu.d"])
+        cp(sp(r, "d"), [kd], ti("d"), ["ti.d"])
+        act(row("drow"), ["drow"], T.ramp[:].indirect(sp(r, "d")), ["ramp", kd])
         scan(T.cum[:, 1:C + 1], ["cum"], row("yk"), row("kc"), -224.0 * STEP1, A.add, A.subtract, ["yk", "kc"])
         ke = pick("erow", T.cum[:, 0:C + 1], lambda a, b: tu("root1", a, b), ["cum", "cum0", "tu.root1"], OPT["HE"], 1024.0)
         act(row("srow"), ["srow"], T.cum[:, 0:C + 1].indirect(tu("root")), ["cum", "cum0", "tu.root"], scale=1024.0)
         latch("erow", ke, "c2")
         tt(tf("pl"), ["tf.pl"], sampled("c2"), tf("dq"), A.subtract, ["c2", "tf.dq"])
-        cp(tu("pl"), ["tu.pl"], tf("pl"), ["tf.pl"])
+        cp(sp(r, "p"), [kp], tf("pl"), ["tf.pl"])
         latch("srow", ["srow"], "c3")
-        tabs("c3", tf("st"), ["tf.st"], 2)
         tt(tf("ln"), ["tf.ln"], sampled("c2"), sampled("c3"), A.subtract, ["c2", "c3"])
-        tt(tf("o"), ["tf.o"], tf("pl"), tf("st"), A.subtract, ["tf.pl", "tf.st"])
-        cp(sp(r), ["sp%d" % r], tf("o", 3), ["tf.o", "tf.ln", "tf.st"], 84 * CYC)
-        send(r, T["lp%d" % r][:], sp(r), ["sp%d" % r], "lp%d" % r, "al%d" % r, 0.35)
-        op("v", lambda: g.vector.tensor_copy(row("cp").indirect(tu("pl")), row("code9")), ["code9", "tu.pl", ">sp%d" % r], ["cp"], 1.45)
+        cp(sp(r, "l"), [kl], tf("ln"), ["tf.ln"])
+        op("v", lambda: g.vector.tensor_copy(row("cp").indirect(sp(r, "p")), row("code9")), ["code9", kp] + OPT.get("PRE", 1) * [">" + kl], ["cp"], SCA)
         latch("cp", ["cp"], "c4", True)
-        tabs("c4", sl(r), ["sl%d" % r], 2, 512.0)
-        send(r, T["la%d" % r][:], sl(r), ["sl%d" % r], "la%d" % r, "aa%d" % r, 0.1)
+        tabs("c4", sp(r, "a"), [ka], 2, 512.0)
+        for p in PARCELS:
+            w = TW * len(p)
+            send(r, T["l%s%d" % (p[0], r)][:, 0:w], sp(r, p[0], 0, w), ["sp%d%s" % (r, x) for x in p], ["l%d%s" % (r, x) for x in p], "a%s%d" % (p[0], r), 0.12 * len(p))
         tabs("c2", tu("last"), ["tu.last"], 8)
         ts(tf("ple"), ["tf.ple"], tf("pl"), cl(2), None, A.subtract, None, ["tf.pl", "col2"])
-        act(row("plr"), ["plr"], T.ramp[:].indirect(tu("pl")), ["ramp", "tu.pl"])
+        act(row("plr"), ["plr"], T.ramp[:].indirect(sp(r, "p")), ["ramp", kp])
 
     def mm(dst, b, st, so, mv, a=0, z=C, rk=None):
         op("t", lambda: g.tensor.matmul_mx(T[dst][:, 512 * b:512 * b + z - a], T[st][:, so:so + 128], T[st + "s"][:, so:so + 128], T[mv][:, a:z], T[mv + "s"][:, a:z], True, True),
-           [st, st + "s"] + (rk or [mv, mv + "s"]), [dst + str(b)], 0.5 * (z - a + 16) / (C + 16))
+           [st, st + "s"] + (rk or [mv, mv + "s"]), [dst + str(b)], MMS * (z - a + 16) / (C + 16))
 
     def quant(tile, keys, w, q, a=0, wk=None):
-        op("v", lambda: g.vector.quantize_mx(T[q][:, a:a + w], T[q + "s"][:, a:a + w], T[tile][:, 4 * a:4 * (a + w)]), keys, wk or [q, q + "s"], 0.015 + 0.0011 * w)
+        op("v", lambda: g.vector.quantize_mx(T[q][:, a:a + w], T[q + "s"][:, a:a + w], T[tile][:, 4 * a:4 * (a + w)]), keys, wk or [q, q + "s"], (14.5 + 1.06 * w) * CYC)
 
     def state_made(r):
         q, l = "qx%d" % r, "lq%d" % r
-        send(r, T[l][:].bitcast(dt.uint8), T[q][:].bitcast(dt.uint8), [q], l, "aq%d" % r, 3.8)
-        send(r, T[l + "s"][:], T[q + "s"][:], [q + "s"], l + "s", "aq%d" % r, 1.0)
+        send(r, T[l][:].bitcast(dt.uint8), T[q][:].bitcast(dt.uint8), [q], [l], "aq%d" % r, 3.8)
+        send(r, T[l + "s"][:], T[q + "s"][:], [q + "s"], [l + "s"], "aq%d" % r, 1.0)
         mm("pb", 0, "qur", 0, q)
         act(row("sr"), ["sr"], T.pb[:, 0:C], ["pb0"], R4, scale=-1.0)
         for b in range(4):
@@ -270,27 +284,26 @@ def rank_program(g, core, T, topo):
             mm("pb", b, "qe", 128 * b, l)
 
     def halves(x, y, h, c):
-        tt(tf(h), ["tf." + h], tf(x), tf(y), A.add, ["tf." + x, "tf." + y])
+        t2(h, x, y, A.add)
         ts(tf(h), ["tf." + h], tf(h), 0.5, None, A.mult, None, ["tf." + h])
-        tt(tf(c), ["tf." + c], tf(x), tf(h), A.subtract, ["tf." + x, "tf." + h])
+        t2(c, x, h, A.subtract)
 
-    def exchange(cname, s, h, c, x, tab):
-        tabs(cname, tf(s), ["tf." + s], 7, -2.0)
-        tt(tf(c), ["tf." + c], tf(s), tf(c), A.mult, ["tf." + s, "tf." + c])
-        tt(tf(x), ["tf." + x], tf(h), tf(c), A.add, ["tf." + h, "tf." + c])
-        cp(tu(tab), ["tu." + tab], tf(x), ["tf." + x])
+    def ahead():
+        ts(tf("fp"), ["tf.fp"], tf("cf"), -2.0, None, A.mult, None, ["tf.cf"])
+        ts(tf("fr"), ["tf.fr"], tf("cf"), cl(7), None, A.mult, None, ["tf.cf", "col7"])
+        t2("fq", "fr", "hf", A.add)
 
     levels(True)
     cp(tu("m"), ["tu.m"], T.ml_s[:], ["ml_s"])
     cp(tf("f"), ["tf.f"], T.fl_s[:], ["fl_s"])
     cp(tf("m"), ["tf.m"], T.ml_s[:], ["ml_s"])
-    act(row("fmr"), ["fmr"], row("ro0").indirect(tu("m")), ["ro0", "tu.m", ">ro8"])
+    act(row("fmr"), ["fmr"], row("ro0").indirect(tu("m")), both("ro0") + ["tu.m", ">ro8b"])
     latch("fmr", ["fmr"], "c8")
     tabs("c8", tf("fm"), ["tf.fm"], 2)
     halves("f", "fm", "hf", "cf")
     ts(tf("jt"), ["tf.jt"], tf("jt"), cl(0), None, A.add, None, ["jt0", "col0"])
-    ts(tf("j4"), ["tf.j4"], tf("jt"), 4.0, 1.0, A.mult, A.add, ["tf.jt"])
-    tt(tf("sn"), ["tf.sn"], tf("jt"), tf("m"), A.is_lt, ["tf.jt", "tf.m"])
+    ts(tf("j4"), ["tf.j4"], tf("jt"), cl(11), 0.25, A.add, A.add, ["tf.jt", "col11"])
+    t2("sn", "jt", "m", A.is_lt)
     ts(tf("oa"), ["tf.oa"], tf("sn"), -float(C), float(C), A.mult, A.add, ["tf.sn"])
     ts(tf("ob"), ["tf.ob"], tf("sn"), float(C), None, A.mult, None, ["tf.sn"])
     quant("xin", ["xin"], C, "qx0")
@@ -300,18 +313,18 @@ def rank_program(g, core, T, topo):
     op("s", lambda: g.scalar.activation(T.qurs[:, 0:128], T.qus[:, 0:128].indirect(T.ofu[:, 0:8]), AF.Copy), ["qus", "ofu"], ["qurs"], gat(128))
     quant("et", ["et0", "et1", "et2", "et3"], 512, "qe")
     state_made(0)
-    iota(T.kw[:], ["kw"], [[1024, C], [1, 4]], -3 - 224 * 1024, 0, 4 * C, rk=[">et0", ">et1", ">et2", ">et3", ">qx0"])
-    act(row("kc"), ["kc"], row("ramp"), ["ramp", ">ro2"], R4, bias=-0.5)
+    act(row("kc"), ["kc"], row("ramp"), ["ramp", ">ro2b"], R4, bias=-0.5)
     finish(0)
-    ts(tf("e1"), ["tf.e1"], tf("o"), 0.0, None, A.is_equal, None, ["tf.o"])
-    tt(tf("e1"), ["tf.e1"], tf("e1"), tf("ln"), A.mult, ["tf.e1", "tf.ln"])
-    tt(tf("e1"), ["tf.e1"], tf("e1"), tf("pl"), A.add, ["tf.e1", "tf.pl"])
+    iota(T.kw[:], ["kw"], [[1024, C], [1, 4]], -3 - 224 * 1024, 0, 4 * C, rk=[">l0a"])
+    tt(tf("e1"), ["tf.e1"], tf("ple"), sampled("c3"), A.is_equal, ["tf.ple", "c3"])
+    t2("e1", "e1", "ln", A.mult)
+    t2("e1", "e1", "pl", A.add)
     ts(tu("b"), ["tu.b"], tf("e1"), -1.0, None, A.add, None, ["tf.e1"])
     act(row("brow"), ["brow"], row("cp").indirect(tu("b")), ["cp", "tu.b"], scale=512.0)
     latch("brow", ["brow"], "c7")
     tabs("c7", tu("b"), ["tu.b"], 2)
     tabs("c7", tf("b"), ["tf.b"], 2)
-    act(row("mrow"), ["mrow"], T.ramp[:].indirect(tu("m")), ["ramp", "tu.m", ">ro8"])
+    act(row("mrow"), ["mrow"], T.ramp[:].indirect(tu("m")), ["ramp", "tu.m", ">ro8b"])
     act(row("mbr"), ["mbr"], row("mrow").indirect(tu("b")), ["mrow", "tu.b"])
     latch("mbr", ["mbr"], "c8")
     tabs("c8", tf("mb"), ["tf.mb"], 2)
@@ -321,88 +334,83 @@ def rank_program(g, core, T, topo):
         op(eng, lambda: Q[eng].dma_start(out, src), keys, [], 0.07, sem="outs", inc=16, lat=lat)
 
     for r in range(3):
-        lp, la, ks = "lp%d" % r, "la%d" % r, "sl%d" % r
+        ks = "sp%da" % r
         last = r == 2
-        act(T.rst[:, 1:C + 1], ["rst"], row("drow").indirect(sl(r)), ["drow", ks], scale=-BIG, bias=-223.5 * BIG)
-        ka = pick("sa", row("sr"), lambda a, b: sl(r, a, b), ["sr", ks], OPT["HA"])
+        act(T.rst[:, 1:C + 1], ["rst"], row("drow").indirect(sp(r, "a")), ["drow", ks], scale=-BIG, bias=-223.5 * BIG)
+        ka = pick("sa", row("sr"), lambda a, b: sp(r, "a", a, b), ["sr", ks], OPT["HA"])
         scan(row("pm"), ["pm"], row("rst"), row("sa"), BIG, A.max, A.min, ["rst", "rst0"] + ka)
         tt(row("neq"), ["neq"], row("pm").indirect(tu("last")), row("sr"), A.not_equal, ["pm", "tu.last", "sr"], GAT)
-        tt(row("cand"), ["cand"], row("neq").indirect(sl(r)), row("cp"), A.add, ["neq", ks, "cp"], GAT)
+        tt(row("cand"), ["cand"], row("neq").indirect(sp(r, "a")), row("cp"), A.add, ["neq", ks, "cp"], GAT)
         scan(row("cm"), ["cm"], row("rst"), row("cand"), BIG, A.max, A.min, ["rst", "rst0", "cand"], R2)
         kl = pick("lrow", row("cm"), lambda a, b: tu("last", a, b), ["cm", "tu.last"], OPT["HL"], 512.0)
         latch("lrow", kl, "c5")
         tabs("c5", tu("l"), ["tu.l"], 2)
         for b in range(4):
             act(row("fh%d" % b), ["fh%d" % b], T.pa[:, 512 * b:512 * b + C], ["pa%d" % b], R4)
-        act(row("lenrow"), ["lenrow"], T.ramp[:].indirect(T[lp][:, TW:2 * TW]), ["ramp", lp])
-        act(row("orow"), ["orow"], T.ramp[:].indirect(T[lp][:, 0:TW]), ["ramp", lp])
-        act(row("strow"), ["strow"], T.ramp[:].indirect(T[lp][:, 2 * TW:3 * TW]), ["ramp", lp])
-        for i, n in enumerate(["lenrow", "plr", "orow", "strow"]):
+        for x, n in zip("dlpa", ["tdrow", "lenrow", "tprow", "ar"]):
+            act(row(n), [n], T.ramp[:].indirect(landed(r, x)), ["ramp", "l%d%s" % (r, x)])
+        for i, n in enumerate(["lenrow", "plr", "tdrow", "tprow"]):
             kg = pick("gr%d" % i, row(n), lambda a, b: tu("l", a, b), [n, "tu.l"], {"v": 0, "s": TW, "h": 14}[OPT["BYL"][i]])
             latch("gr%d" % i, kg, "x%d" % i)
-        act(row("ar"), ["ar"], T.ramp[:].indirect(T[la][:]), ["ramp", la])
-        xl, xp, xo, xs = [sampled("x%d" % i) for i in range(4)]
+        xl, xp, xd, xt = [sampled("x%d" % i) for i in range(4)]
         for b in range(4):
             act(row("ft%d" % b), ["ft%d" % b], T.pb[:, 512 * b:512 * b + C], ["pb%d" % b], R4)
         tabs("x0", tf("l3"), ["tf.l3"], 2)
         op("v", lambda: g.vector.reciprocal(tf("inv"), tf("l3")), ["tf.l3"], ["tf.inv"], 0.19 + 6 * TW * CYC)
-        tabs("x0", tf("hl"), ["tf.hl"], 9, -0.5)
+        tabs("x0", tf("hl"), ["tf.hl"], 9, 0.5)
         tt(tf("ng"), ["tf.ng"], tf("ple"), xp, A.is_lt, ["x1", "tf.ple"])
-        tt(tf("t1"), ["tf.t1"], tf("ng"), tf("ln"), A.mult, ["tf.ng", "tf.ln"])
+        t2("t1", "ng", "ln", A.mult)
         tt(tf("w"), ["tf.w"], tf("pl"), xp, A.subtract, ["x1", "tf.pl"])
-        tt(tf("a1"), ["tf.a1"], tf("w"), tf("t1"), A.add, ["tf.w", "tf.t1"])
-        tt(tf("a2"), ["tf.a2"], xo, tf("hl"), A.add, ["x2", "tf.hl"])
-        tt(tf("u"), ["tf.u"], tf("a1"), tf("a2"), A.add, ["tf.a1", "tf.a2"])
+        t2("a1", "w", "t1", A.add)
+        tt(tf("a2"), ["tf.a2"], tf("hl"), xd, A.subtract, ["x2", "tf.hl"])
+        t2("u", "a1", "a2", A.add)
         tt(ti("n"), ["ti.n"], tf("u"), tf("inv"), A.mult, ["tf.u", "tf.inv"])
-        tt(tf("m1"), ["tf.m1"], xs, tf("hl"), A.subtract, ["x3", "tf.hl"])
         tt(tf("t2"), ["tf.t2"], ti("n"), tf("l3"), A.mult, ["ti.n", "tf.l3"])
-        tt(tf("bq"), ["tf.bq"], tf("m1"), tf("u"), A.add, ["tf.m1", "tf.u"])
-        tt(tf("tp"), ["tf.tp"], tf("bq"), tf("t2"), A.subtract, ["tf.bq", "tf.t2"])
+        tt(tf("bq"), ["tf.bq"], tf("a1"), xt, A.add, ["x3", "tf.a1"])
+        t2("tp", "bq", "t2", A.subtract)
         for x in "ab":
-            tt(tf("b" + x), ["tf.b" + x], tf("bq"), tf("o" + x), A.add, ["tf.bq", "tf.o" + x])
-            tt(tf("tp" + x), ["tf.tp" + x], tf("b" + x), tf("t2"), A.subtract, ["tf.b" + x, "tf.t2"])
-        ts(tu("tp", 0, 3 * TW), ["tu.tp"], tf("tp", 3), cl(2), None, A.add, None, ["tf.tp", "tf.tpa", "tf.tpb", "col2"], 84 * CYC)
+            t2("b" + x, "bq", "o" + x, A.add)
+            t2("tp" + x, "b" + x, "t2", A.subtract)
+        cp(tu("tp", 0, 3 * TW), ["tu.tp"], tf("tp", 3), ["tf.tp", "tf.tpa", "tf.tpb"], 84 * CYC)
         kt = pick("trow", row("ar"), lambda a, b: tu("tp", a, b), ["ar", "tu.tp"], OPT["HT"] if last else TW)
         latch("trow", kt, "c6")
         tabs("c6", tu("T"), ["tu.T"], 2)
-        zd = 0 if last else OPT["ZD"]
-        act(row("sfa"), ["sfa"], row("sr").indirect(T[la][:]), ["sr", la])
+        act(row("sfa"), ["sfa"], row("sr").indirect(landed(r, "a")), ["sr", "l%da" % r])
         act(row("sfa", C, 2 * C), ["sfb"], row("sfa"), ["sfa"], R4, scale=-1.0)
         cp(row("mu"), ["mu"], T.sfa[:].indirect(tu("tpa")), ["sfa", "sfb", "tu.tp"], GAT)
         act(row("nu"), ["nu"], T.sfa[:].indirect(tu("tpb")), ["sfa", "sfb", "tu.tp"])
         tt(row("sw"), ["sw"], row("mu").indirect(tu("m")), row("nu"), A.is_gt, ["mu", "nu", "tu.m"], GAT)
-        latch("sw", ["sw"], "c5")
-        exchange("c5", "sw", "hf", "cf", "f", "tab0")
+        latch("sw", ["sw"], "c9")
+        if OPT["X3"]:
+            ahead()
+            tt(tf("sw"), ["tf.sw"], sampled("c9"), tf("fp"), A.mult, ["c9", "tf.fp"])
+            t2("f", "sw", "fq", A.add)
+            if not last:
+                t2("cf", "f", "hf", A.subtract)
+        else:
+            tabs("c9", tf("sw"), ["tf.sw"], 7, -2.0)
+            t2("cf", "sw", "cf", A.mult)
+            t2("f", "hf", "cf", A.add)
+        cp(tu("tab0"), ["tu.tab0"] + both("tu.tab0"), tf("f"), ["tf.f"])
         act(row("swb"), ["swb"], row("sw").indirect(tu("b")), ["sw", "tu.b"])
         latch("swb", ["swb"], "c7")
-        exchange("c7", "swb", "hb", "cb", "b", "b")
-        z = 16 * zd
+        tabs("c7", tf("swb"), ["tf.swb"], 7, -2.0)
+        t2("cb", "swb", "cb", A.mult)
+        t2("b", "hb", "cb", A.add)
+        cp(tu("b"), ["tu.b"], tf("b"), ["tf.b"])
         for b in range(4):
-            fh, ft, fs = "fh%d" % b, "ft%d" % b, "fs%d" % b
-            if zd:
-                act(T.zt[:, b:4 * z:4], ["zu%d" % b], row(ft).indirect(tu("T", 0, zd)), [ft, "tu.T"], gat(z))
-                act(T.za[:, b:4 * z:4], ["za%d" % b], row(fh).indirect(tu("tab0", 0, zd)), [fh, "tu.tab0"], gat(z))
-            if zd < TW:
-                act(row(fs, z, C), [fs], row(ft).indirect(tu("T", zd)), [ft, "tu.T"], gat(C - z))
-                tt(T.zt[:, 4 * z + b:4 * C:4], ["zt%d" % b], row(fh).indirect(tu("tab0", zd)), row(fs, z, C), A.add, [fh, fs, "tu.tab0"], gat(C - z))
-        if zd:
-            zk = ["zu%d" % b for b in range(4)]
-            op("g", lambda z=z: g.dma_start(T.zt[:, 0:4 * z], T.za[:, 0:4 * z], accum_op=A.add), zk + ["za%d" % b for b in range(4)], zk, 1.0, sem="zadd", inc=16, lat=OPT["DADD"] - 1.0)
-        quant("zt", ["zt0", "zt1", "zt2", "zt3", "zu0", "zu1", "zu2", "zu3"], C, "qz")
+            act(row("fs%d" % b), ["fs%d" % b], row("ft%d" % b).indirect(tu("T")), ["ft%d" % b, "tu.T"])
+            tt(T.zt[:, b:4 * C:4], ["zt%d" % b], row("fh%d" % b).indirect(tu("tab0")), row("fs%d" % b), A.add, ["fh%d" % b, "fs%d" % b, "tu.tab0"], GAT)
+        quant("zt", ["zt0", "zt1", "zt2", "zt3"], C, "qz")
+        if last:
+            quant("vin", ["vin", ">qz"], 128, "qv")
         for b in range(4):
             mm("pb", b, "wq", 128 * b, "qz")
-        for b in range(4):
             act(row("r2%d" % b), ["r2%d" % b], T.pb[:, 512 * b:512 * b + C], ["pb%d" % b], R4, scale=0.015625)
-        for h, (a, z) in enumerate([(0, TW // 2), (TW // 2, TW)] if last and OPT["TAIL"] else [(0, TW)]):
+        for h, (a, z) in enumerate(zip(OPT["XCUT"], OPT["XCUT"][1:]) if last else [(0, TW)]):
             n = 16 * (z - a)
             for b in range(4):
-                out, key = T.xt[:, 64 * a + b:64 * z:4], "xt%d%d" % (h, b)
-                src = row("r2%d" % b).indirect(tu("b", a, z))
-                if b >= 4 - OPT["NP"][r]:
-                    act(row("pp%d" % b, 16 * a, 16 * z), ["pp%d%d" % (h, b)], src, ["r2%d" % b, "tu.b"], gat(n))
-                    tt(out, [key], row("pp%d" % b, 16 * a, 16 * z), T.pa[:, 512 * b + 16 * a:512 * b + 16 * z], A.add, ["pp%d%d" % (h, b), "pa%d" % b], n * CYC)
-                else:
-                    tt(out, [key], src, row("fh%d" % b, 16 * a, 16 * z), A.add, ["r2%d" % b, "fh%d" % b, "tu.b"], gat(n))
+                tt(T.xt[:, 64 * a + b:64 * z:4], ["xt%d%d" % (h, b)], row("r2%d" % b).indirect(tu("b", a, z)), row("fh%d" % b, 16 * a, 16 * z), A.add, ["r2%d" % b, "fh%d" % b, "tu.b"], gat(n))
             keys = ["xt%d%d" % (h, b) for b in range(4)]
             if not last:
                 quant("xt", keys, C, "qx%d" % (r + 1))
@@ -415,36 +423,36 @@ def rank_program(g, core, T, topo):
             store("s", T.y[:, 16 * a:16 * z], row("sa", 16 * a, 16 * z), ["y%d" % h], 1.8 + n / 400)
         if last:
             break
-        levels(not OPT["K2"])
+        levels(False)
         state_made(r + 1)
-        if r == 0:
-            quant("vin", ["vin"], 128, "qv")
         finish(r + 1)
     act(row("nlr"), ["nlr"], T.ramp[:].indirect(tu("tab0")), ["ramp", "tu.tab0"], bias=224.0)
     store("y", T.nl[:], T.nlr[0:128:16, :], ["nlr"])
     for k in range(4):
-        store("y", T.osc[4 * k:4 * k + 4, :], T.qx3s[32 * k:32 * k + 4, 0:C], ["qx30", "qx31"])
+        store("y", T.osc[4 * k:4 * k + 4, :], T.qx3s[32 * k:32 * k + 4, 0:C], ["qx30", "qx31", "qx32"])
 
     n = len(prog)
     deps, kids = [set() for _ in range(n)], [[] for _ in range(n)]
     lw, rd = {}, {}
     for i, p in enumerate(prog):
         for k in p["r"]:
-            if k in lw:
+            if k[0] == ">":
+                deps[i].add(lw[k[1:]])
+            elif k in lw:
                 deps[i].add(lw[k])
         for k in p["w"]:
             if k in lw:
                 deps[i].add(lw[k])
             deps[i].update(rd.get(k, []))
         for k in p["r"]:
-            if k[0] == ">":
-                deps[i].add(lw[k[1:]])
             rd.setdefault(k, []).append(i)
         for k in p["w"]:
             lw[k], rd[k] = i, []
         deps[i].discard(i)
         for d in deps[i]:
             kids[d].append(i)
+    dl, far = [list(d) for d in deps], [bool(p["remote"]) for p in prog]
+    lat, cost = [p["lat"] for p in prog], [[p["cs"][m] for p in prog] for m in range(3)]
 
     def lay(rank_):
         at, done, left, tq, link = [0.0] * n, [0.0] * n, [len(x) for x in deps], {e: 0.0 for e in Q}, 0.0
@@ -455,33 +463,116 @@ def rank_program(g, core, T, topo):
         for _ in range(n):
             t0, e = min((max(tq[e], min(ready[e])[0]), e) for e in Q if ready[e])
             a, i = min((x for x in ready[e] if x[0] <= t0 + OPT["LOOK"]), key=lambda x: (rank_[x[1]], x[1]))
-            soon = [x for x in ready[e] if rank_[x[1]] < rank_[i] and x[0] - t0 + prog[x[1]]["c"] < OPT["KAP"] * prog[i]["c"]]
+            soon = [x for x in ready[e] if rank_[x[1]] < rank_[i] and x[0] - t0 + cost[0][x[1]] < OPT["KAP"] * cost[0][i]]
             if soon:
                 a, i = min(soon)
             ready[e].remove((a, i))
             at[i] = max(t0, a)
-            tq[e] = at[i] + prog[i]["c"]
-            done[i] = tq[e] + prog[i]["lat"] + WAKE
-            if prog[i]["remote"]:
-                link = max(link, tq[e] + OPT["REM"]) + prog[i]["lat"] - OPT["REM"] - OPT["RW"]
-                done[i] = link + OPT["RW"] + WAKE
+            tq[e] = at[i] + cost[0][i]
+            done[i] = tq[e] + lat[i] + WAKES[0]
+            if far[i]:
+                link = max(link, tq[e] + STARTS[0]) + lat[i]
+                done[i] = link + OPT["RW"] + WAKES[0]
             for k in kids[i]:
                 left[k] -= 1
                 if not left[k]:
                     ready[prog[k]["eng"]].append((max(done[d] for d in deps[k]), k))
         return at, done
 
-    prio = [0.0] * n
-    for i in range(n - 1, -1, -1):
-        prio[i] = prog[i]["c"] + prog[i]["lat"] + WAKE + max([prio[k] for k in kids[i]] + [0.0])
-    for i in range(n):
-        key = prog[i]["w"][0] if prog[i]["w"] else ""
-        prio[i] += OPT["BIAS"].get(key, OPT["BIAS"].get(key.rstrip("0123456789") + "*", 0.0))
-    at, done = lay([-x for x in prio])
-    order = sorted(range(n), key=lambda i: (at[i], i))
-    OPT["EST"] = max(done)
-    OPT["DBG"] = (prog, prio, kids, at)
-    OPT["LAY"] = (lay, deps)
+    def clock_of(seq, m):
+        c, wake, start, rate = cost[m], WAKES[m], STARTS[m], RATES[m]
+        at, done, by, link, left = [0.0] * n, [-1.0] * n, [-1] * n, 0.0, n
+        state = [[q, 0, 0.0] for q in seq.values()]
+        while left:
+            before = left
+            for st in state:
+                q, pos, t = st
+                while pos < len(q):
+                    i = q[pos]
+                    t1, who = t, q[pos - 1] if pos else -1
+                    for d in dl[i]:
+                        x = done[d]
+                        if x > t1:
+                            t1, who = x, d
+                        elif x < 0:
+                            break
+                    else:
+                        at[i], by[i] = t1, who
+                        t = t1 + c[i]
+                        if far[i]:
+                            link = max(link, t + start) + lat[i] * rate
+                            done[i] = link + OPT["RW"] + wake
+                        else:
+                            done[i] = t + lat[i] + wake
+                        pos += 1
+                        left -= 1
+                        continue
+                    break
+                st[1], st[2] = pos, t
+            if left == before:
+                return None
+        return at, done, by
+
+    if "seq" not in ORDER:
+        span = [cost[0][i] + lat[i] + WAKES[0] + far[i] * (STARTS[0] + OPT["RW"]) for i in range(n)]
+        prio = [0.0] * n
+        for i in range(n - 1, -1, -1):
+            prio[i] = span[i] + max([prio[k] for k in kids[i]] + [0.0])
+        total = lambda runs: sum(max(x[1]) for x in runs)
+        kept = None
+        for _ in range(OPT["PASS"] + 1):
+            at, done = lay([-x for x in prio])
+            order = sorted(range(n), key=lambda i: (at[i], i))
+            seq = {e: [i for i in order if prog[i]["eng"] == e] for e in Q}
+            runs = [clock_of(seq, m) for m in range(3)]
+            if kept is None or total(runs) < kept[0]:
+                kept = (total(runs), seq, runs[0][0])
+            tail, behind = [0.0] * n, {}
+            for i in reversed(order):
+                own = span[i] + max([tail[k] for k in kids[i]] + [0.0])
+                tail[i] = max(own, cost[0][i] + behind.get(prog[i]["eng"], 0.0))
+                behind[prog[i]["eng"]] = tail[i]
+                prio[i] += OPT["ALPHA"] * (own - prio[i])
+        seed = [OPT["SEED"]]
+
+        def draw(k):
+            seed[0] = (seed[0] * 1103515245 + 12345) % 2 ** 31
+            return (seed[0] >> 8) % k
+
+        seq = {e: list(q) for e, q in kept[1].items()}
+        runs = [clock_of(seq, m) for m in range(3)]
+        for it in range(OPT["TRIES"]):
+            at, done, by = runs[draw(3)]
+            if draw(10) < 8:
+                i, pairs = done.index(max(done)), []
+                while by[i] >= 0:
+                    if by[i] not in deps[i]:
+                        pairs.append(i)
+                    i = by[i]
+                i = pairs[draw(len(pairs))]
+                q = seq[prog[i]["eng"]]
+                a, hop = q.index(i), [1, 1, 2, 3, 5, 9][draw(6)]
+                a, b = (a, max(0, a - hop)) if draw(2) else (a - 1, min(len(q) - 1, a - 1 + hop))
+            else:
+                q = seq["vs"[draw(2)]]
+                a = draw(len(q))
+                b = min(len(q) - 1, max(0, a + draw(7) - 3))
+            q.insert(b, q.pop(a))
+            allow = -(OPT["HEAT"] * (1.0 - it / OPT["TRIES"]) + 0.01) * math.log((draw(9999) + 1) / 10000)
+            first = clock_of(seq, 0)
+            new = first and max(first[1]) - max(runs[0][1]) < allow / 2 + 0.1 and [first, clock_of(seq, 1), clock_of(seq, 2)]
+            if new and total(new) - total(runs) < allow:
+                runs = new
+                if total(runs) < kept[0]:
+                    kept = (total(runs), {e: list(z) for e, z in seq.items()}, runs[0][0])
+            else:
+                q.insert(a, q.pop(b))
+        ORDER["seq"] = kept
+    at = ORDER["seq"][2]
+    place = {i: k for q in ORDER["seq"][1].values() for k, i in enumerate(q)}
+    order = sorted(range(n), key=lambda i: (at[i], place[i]))
+    OPT["EST"] = ORDER["seq"][0] / 3
+    OPT["DBG"] = (prog, None, kids, at)
 
     cnt = {s: 0 for s in SEMAPHORES}
     known = {e: {} for e in Q}
@@ -499,7 +590,7 @@ def rank_program(g, core, T, topo):
             for x, y in clock[(s, most[s])].items():
                 known[eng][x] = max(known[eng].get(x, 0), y)
 
-    landed = {"aq%d" % i: 2 for i in range(3)}
+    whole = {"aq%d" % i: 2 for i in range(3)}
     for i in order:
         p = prog[i]
         ds = []
@@ -512,9 +603,10 @@ def rank_program(g, core, T, topo):
             sem, m = p["remote"]
             cnt["snt"] += m
             cnt[sem] += m
-            me = (sem, m * landed.get(sem, 1))
+            me = (sem, m * whole.get(sem, 1))
             clock[me] = {sem: me[1]}
-            lastw[p["w"][0]] = me
+            for k in p["w"]:
+                lastw[k] = me
             continue
         for k in p["w"]:
             if k in lastw:

@@ -5,8 +5,9 @@ from concourse.mybir import dt, AluOpType, ActivationFunctionType
 C = 448
 TW = 28
 STEP = [1, 2, 3]
-OPT = {"SR": [1, 0], "SK": [1, 1], "HE": 12, "HA": 0, "HL": 12, "HT": 12, "BYL": "vvss", "XCUT": [0, 20, 28], "SENDS": 2, "X3": True,
-       "RW": 0.9, "LOOK": 0.02, "KAP": 0.6, "PASS": 30, "ALPHA": 0.3, "TRIES": 40000, "HEAT": 0.2, "SEED": 1}
+OPT = {"HE": 12, "HL": 12, "HT": 12, "HB": 14, "ZCUT": [0, 16, 28], "XCUT": [0, 20, 28], "NL": 3, "FTV": 2,
+       "LOOK": 0.02, "KAP": 0.6, "PASS": 30, "ALPHA": 0.3, "KINDS": 350, "TRIES": 75000, "HEAT": 0.3, "SEED": 6}
+PARCELS = ["dp", "la"]
 SCRATCH = {}
 
 
@@ -15,17 +16,20 @@ def _decl():
     for n in ["k0m", "kc", "ka", "kb", "kma", "kmb", "yk", "sr", "sa", "pm", "mu", "nu", "ck", "nlr"]:
         SCRATCH[n] = ("sbuf", [128, C], f32)
     SCRATCH["sfa"] = ("sbuf", [128, 2 * C], f32)
-    for n in ["cum", "rst", "ramp"]:
+    SCRATCH["lcp"] = ("sbuf", [128, C], f16)
+    for n, k in [("z", 7), ("y", 4), ("v", 3)]:
+        for i in range(3):
+            SCRATCH["%s%d" % (n, i)] = ("sbuf", [128, k * TW], f32)
+    for n in ["cum", "rst", "rs2", "ramp"]:
         SCRATCH[n] = ("sbuf", [128, C + 16], bf)
-    for n in ["neq", "cand", "cm", "cp", "code9", "lrow", "plr", "tprow", "tdrow", "lenrow", "trow", "sw", "swb", "brow", "mrow", "mbr", "lc", "lc9", "fmr",
-              "erow", "srow", "drow", "ar"]:
+    for n in ["neq", "cand", "cp", "code9", "tprow", "tdrow", "lenrow", "trow", "sw", "swb", "brow", "mrow", "mbr", "lc", "lc9", "fmr", "erow", "srow", "drow", "ar", "ends"]:
         SCRATCH[n] = ("sbuf", [128, C], bf)
     SCRATCH["ro"] = ("sbuf", [128, 9 * C], bf)
     SCRATCH["cc"] = ("sbuf", [128, 10 * C], f16)
-    SCRATCH["c4s"] = ("sbuf", [128, 4 * C], f16)
+    SCRATCH["c4s"] = ("sbuf", [128, 3 * C], f16)
     for n in ["gr", "fh", "ft", "fs", "xin", "xt", "zt"]:
         SCRATCH[n] = ("sbuf", [128, 4 * C], bf)
-    for n in ["r2", "kw"]:
+    for n in ["r2", "kw", "pp"]:
         SCRATCH[n] = ("sbuf", [128, 4 * C], f32)
     for n in ["uin", "vin"]:
         SCRATCH[n] = ("sbuf", [128, 512], bf)
@@ -35,30 +39,32 @@ def _decl():
         SCRATCH[n] = ("sbuf", [128, w], "float8_e4m3fn_x4")
         SCRATCH[n + "s"] = ("sbuf", [128, w], "uint8")
     for n, w, t in [("fl_s", TW, "int32"), ("ml_s", TW, "int32"), ("pq", TW, "int32"), ("pqm", TW, "int32"), ("ofq", TW, "uint16"), ("ofi", 8, "int32"), ("ofu", 8, "uint16"),
-                    ("col", 12, f32), ("tf", TW * 50, f32), ("ti", TW * 4, "int32"), ("tu", TW * 24, "uint16"), ("t16", 16, bf), ("la16", 16, bf), ("lb16", 16, bf), ("lc16", 16, bf)]:
+                    ("col", 16, f32), ("tf", TW * 24, f32), ("ti", TW * 4, "int32"), ("tu", TW * 24, "uint16"), ("t16", 16, bf), ("la16", 16, bf), ("lb16", 16, bf), ("lc16", 16, bf)]:
         SCRATCH[n] = ("sbuf", [128, w], t)
     SCRATCH["sp"] = ("sbuf", [128, 3 * 4 * TW], "uint16")
     for i in range(3):
-        for x in "dpla":
-            SCRATCH["l%s%d" % (x, i)] = ("sbuf", [128, 3 * TW], "uint16")
+        for x in PARCELS:
+            SCRATCH["l%s%d" % (x[0], i)] = ("sbuf", [128, len(x) * TW], "uint16")
     SCRATCH["pa"] = ("psum", [128, 2048], f32)
     SCRATCH["pb"] = ("psum", [128, 2048], f32)
 
 
 _decl()
 LOADS = ["dfl", "dml", "dx", "du", "dv", "dwc", "dws"]
-SEMAPHORES = ["cv", "cs_", "ct", "cg", "snt", "outs"] + LOADS + ["a%s%d" % (n, i) for n in "qdpla" for i in range(3)]
-TF = {n: i for i, n in enumerate(["jt", "f", "m", "hf", "fm", "cf", "fp", "fq", "fr", "hb", "cb", "b", "mb", "sn", "dq", "pl", "ple", "ln", "l3", "inv", "ng", "t1", "w", "a1", "hl", "a2",
-                                  "u", "bq", "t2", "tp", "tpa", "tpb", "sw", "swb", "e1", "j4", "q0", "q2", "oa", "ob", "ba", "bb"])}
+SEMAPHORES = ["cv", "cs_", "ct", "cg", "snt", "outs"] + LOADS + ["a%s%d" % (n, i) for n in "qdl" for i in range(3)]
+TF = {n: i for i, n in enumerate(["j16", "m", "fm", "hb", "cb", "mb", "sn", "en", "ple", "ln", "ng", "t1", "w", "hl", "swb", "e1", "q0"])}
+STEPS = {"b": ("y1", 0, 4), "f": ("y1", 1, 4), "jt": ("y1", 2, 4), "sw": ("v1", 0, 3), "cf": ("v0", 1, 3), "hf": ("v1", 2, 3)}
 TU = {n: i for i, n in enumerate(["tab%d" % k for k in range(9)] + ["m", "root", "root1", "l", "tp", "tpa", "tpb", "T", "b", "last", "k2"])}
-TI = {"k": 0, "d": 1, "n": 2}
+TI = {"k": 0, "d": 1, "e": 2}
 BIG = float(2 ** 90)
 STEP1 = 2.0 ** -10
-CYC = 0.83e-3 * np.array([1.25, 1.05, 1.45])
-GEL = 0.83e-3 * np.array([1.56, 1.95, 1.15])
-SCA = 0.05 + 0.83e-3 * C * np.array([3.8, 5.5, 2.0])
-MMS = np.array([0.5, 0.62, 0.38])
-WAKES, STARTS, RATES = [0.15, 0.2, 0.09], [2.5, 4.0, 1.8], [1.0, 1.3, 0.5]
+WHOLE = 3 * 2 ** 22
+CYC = 0.83e-3 * np.array([1.25, 1.05, 1.45, 1.4, 1.1])
+GEL = 0.83e-3 * np.array([1.56, 1.95, 1.15, 1.9, 1.25])
+SCA = 0.05 + 0.83e-3 * C * np.array([3.8, 5.5, 2.0, 2.2, 5.2])
+MMS, ISSUE = np.array([0.5, 0.62, 0.38, 0.4, 0.62]), np.array([0.5, 0.95, 0.3, 0.4, 0.9])
+WAKES, STARTS, RATES, FARWAKE = [0.15, 0.2, 0.09, 0.2, 0.1], [1.8, 2.8, 1.2, 1.4, 2.6], [0.9, 1.3, 0.6, 0.6, 1.2], 0.6
+GUESSES = range(len(WAKES))
 ORDER = {}
 
 
@@ -79,12 +85,15 @@ def rank_program(g, core, T, topo):
         cost = [float(x) for x in cost + 0 * CYC]
         prog.append({"eng": eng, "fn": fn, "r": reads, "w": writes, "c": cost[0], "cs": cost, "sem": sem, "inc": inc, "lat": lat, "remote": remote})
 
-    tf = lambda n, k=1: T.tf[:, TW * TF[n]:TW * (TF[n] + k)]
+    step = lambda n, k, of: T[n][:, k:of * TW:of]
+    tf = lambda n: step(*STEPS[n]) if n in STEPS else T.tf[:, TW * TF[n]:TW * TF[n] + TW]
     tu = lambda n, a=0, b=TW: T.tu[:, TW * TU[n] + a:TW * TU[n] + b]
     ti = lambda n: T.ti[:, TW * TI[n]:TW * TI[n] + TW]
     cl = lambda i: T.col[:, i:i + 1]
-    SLOT = {"%s%d" % (n, k): (m, C * k) for n, m, z in (("ro", "ro", 9), ("c", "cc", 10), ("gr", "gr", 4), ("x", "c4s", 4), ("fh", "fh", 4), ("ft", "ft", 4), ("fs", "fs", 4),
-                                                       ("r2", "r2", 4)) for k in range(z)}
+    z0, z1, z2 = [(lambda k, n=n: step(n, k, 7)) for n in ("z0", "z1", "z2")]
+    both = lambda n: [n + "a", n + "b"]
+    SLOT = {"%s%d" % (n, k): (m, C * k) for n, m, z in (("ro", "ro", 9), ("c", "cc", 10), ("gr", "gr", 3), ("x", "c4s", 3), ("fh", "fh", 4), ("ft", "ft", 4), ("fs", "fs", 4),
+                                                       ("r2", "r2", 4), ("pp", "pp", 4)) for k in range(z)}
 
     def row(n, a=0, b=C):
         n, s = SLOT.get(n, (n, 0))
@@ -106,6 +115,9 @@ def rank_program(g, core, T, topo):
     def cp(out, wk, a, rk, c=TINY):
         op("v", lambda: g.vector.tensor_copy(out, a), rk, wk, c)
 
+    def fill(out, x, wk, c=TINY):
+        op("v", lambda: g.vector.memset(out, x), [], wk, c)
+
     def t2(out, a, b, o):
         tt(tf(out), ["tf." + out], tf(a), tf(b), o, ["tf." + a, "tf." + b])
 
@@ -125,15 +137,14 @@ def rank_program(g, core, T, topo):
             keys.append(name + "b")
         return keys
 
-    def latch(src, rk, cname, fine=False, c=R2):
-        lc, low = ("lc9", -2.0) if fine else ("lc", -1024.0)
-        scan(row(cname), [cname], row(src), row(lc), low, A.max, A.add, rk + [lc], c)
+    def latch(src, rk, cname, lc="lc", low=-1024.0, c=R2):
+        scan(row(cname), both(cname), row(src), row(lc), low, A.max, A.add, rk + [lc], c)
 
     def tabs(cname, out, wk, col, scale=None):
         if scale:
-            ts(out, wk, sampled(cname), scale, cl(col), A.mult, A.add, [cname, "col%d" % col])
+            ts(out, wk, sampled(cname), scale, cl(col), A.mult, A.add, both(cname) + ["col%d" % col])
         else:
-            ts(out, wk, sampled(cname), cl(col), None, A.add, None, [cname, "col%d" % col])
+            ts(out, wk, sampled(cname), cl(col), None, A.add, None, both(cname) + ["col%d" % col])
 
     def load(eng, sem, out, src, key, lat):
         op(eng, lambda: Q[eng].dma_start(out, src), [], [key], 0.07, sem=sem, inc=16, lat=lat)
@@ -153,13 +164,19 @@ def rank_program(g, core, T, topo):
             op("g", lambda: g.iota(out, pattern, base, cm), list(rk), wk, c)
     iota(T.pq[:], ["pq"], [[0, TW]], 0, 1, TW, False)
     iota(T.t16[:], ["t16"], [[1, 16]], 0, 0, 16)
-    iota(T.ramp[:], ["ramp", "rampa", "rampb"], [[1, C + 16]], -224, 0, C + 16, rk=[">pq", ">t16"])
-    iota(tf("jt"), ["jt0"], [[16, TW]], 0, 0, TW, rk=[">ramp"])
+    iota(T.ramp[:], ["ramp"] + both("ramp"), [[1, C + 16]], -224, 0, C + 16, rk=[">pq", ">t16"])
+    iota(tf("j16"), ["tf.j16"], [[16, TW]], 0, 0, TW, rk=[">ramp"])
     iota(T.ofi[:], ["ofi"], [[16, 8]], 0, 0, 8, False, rk=[">ramp"])
-    iota(T.et[:], ["et"], [[0, 2048]], 0, 0, 2048, rk=[">jt0", ">ofi"])
-    act(row("k0m"), ["k0ma", "k0mb"], row("ramp"), ["ramp"], R4, bias=-STEP1)
-    ts(row("code9"), ["code9"], row("ramp"), 2.0 ** -9, None, A.mult, None, ["ramp"], R2)
-    ts(T.pqm[:], ["pqm"], T.pq[:], 15, None, A.bitwise_and, None, ["pq"])
+    for out, x, wk, n in [(T.y1[:], 2 ** 20, ["y1", "tf.f", "tf.b", "tf.jt"], 4 * TW), (step("y0", 0, 4), 2 ** 20, ["y00"], TW),
+                          (T.v0[:], 1, ["v0", "tf.cf"], 3 * TW), (step("v0", 0, 3), 0, ["v0"], TW), (T.v1[:], 0, ["v1", "tf.hf", "tf.sw"], 3 * TW),
+                          (T.z0[:], 1, ["z0"], 7 * TW), (z0(0), 0, ["z0"], TW), (z0(3), -1, ["z0"], TW), (T.z1[:], WHOLE, ["z1%d" % k for k in range(7)], 7 * TW),
+                          (T.rst[:, 0:1], 0, ["rst0"], 1), (T.rs2[:, 0:1], 4, ["rs20"], 1)]:
+        iota(out, wk, [[0, n]], x, 0, n, rk=[">tf.j16", ">ofi"])
+    iota(T.et[:], ["et"], [[0, 2048]], 0, 0, 2048, rk=[">y1", ">y00", ">v0", ">v1", ">z0", ">z10", ">rst0", ">rs20"])
+    act(row("k0m"), both("k0m"), row("ramp"), ["ramp"], R4, bias=-STEP1)
+    fill(T.ends[:, 0:1], BIG, ["ends0"])
+    fill(T.cum[:, 0:1], -224.0 * STEP1, ["cum0"])
+    ts(T.pqm[:], ["pqm"], T.pq[:], 15, None, A.bitwise_and, None, ["pq", ">ends0", ">cum0"])
     cp(cl(0), ["col0"], T.pqm[:, 0:1], ["pqm"])
     cp(T.ofq[:], ["ofq"], T.pqm[:], ["pqm"])
     ts(T.t16[:], ["t16"], T.t16[:], cl(0), None, A.subtract, None, ["t16", "col0"])
@@ -169,52 +186,52 @@ def rank_program(g, core, T, topo):
     tt(T.la16[:], ["la16"], T.la16[:], T.lb16[:], A.add, ["la16", "lb16"])
     tt(T.lc16[:], ["lc16"], T.la16[:], T.lc16[:], A.add, ["la16", "lc16"])
     cp(row("lc"), ["lc"], T.lc16[:].indirect(T.ofq[:]), ["lc16", "ofq"], GAT)
-    ts(row("lc9"), ["lc9"], row("lc"), 2.0 ** -9, None, A.mult, None, ["lc"], R2)
     ts(cl(1), ["col1"], cl(0), 0.0, 1024.0, A.is_equal, A.mult, ["col0"])
     ts(cl(2), ["col2"], cl(1), 224.0 - 512.0, None, A.add, None, ["col1"])
-    for k, (a, b) in enumerate([(1024.0, 511.0), (1.0, 511.0 / 1024 + 0.01), (1.0, 511.0 / 1024 + 1.01), (-1.0, 1.0), (-2.0, 449.0), (1.0, -1.0), (-1.5, -0.5), (4.0, 3.0), (-1.0, -0.75)], 3):
+    for k, (a, b) in enumerate([(1024.0, 511.0), (1.0, 511.0 / 1024 + 0.01), (1.0, 511.0 / 1024 + 1.01), (1.0, 0.01), (-2.0, 449.0), (1.0, -1.0), (-0.5, -0.5), (4.0, 3.0), (-1.0, -0.5)], 3):
         ts(cl(k), ["col%d" % k], cl(2), a, b, A.mult, A.add, ["col2"])
-    op("v", lambda: g.vector.memset(T.rst[:, 0:1], BIG), [], ["rst0"])
-    op("v", lambda: g.vector.memset(T.cum[:, 0:1], -224.0 * STEP1), [], ["cum0"])
-    op("v", lambda: g.vector.memset(T.half[:], 0.5), [], ["half"])
+    fill(T.ends[:, 1:C], 2.0 ** -19, ["ends"], R2)
+    fill(T.half[:], 0.5, ["half"])
+    fill(step("y0", 1, 4), -0.5, ["y01"])
+    fill(step("y0", 2, 4), 0.25, ["y02"])
     for b in range(4):
         op("g", lambda b=b: g.affine_select(T.et[:, 512 * b + b:512 * b + 512:4], T.half[:], [[1, 128]], A.is_equal, 0.0, 0, -1), ["et", "half"], ["et%d" % b], 0.17 + 256 * CYC)
-    both = lambda n: [n + "a", n + "b"]
-    cp(tu("tab0"), ["tu.tab0"] + both("tu.tab0"), T.fl_s[:], ["fl_s"])
+    op("g", lambda: g.affine_select(row("lcp"), row("lc"), [[0, C]], A.is_equal, 0.0, 0, 0), ["lc", ">et3"], ["lcp"], 0.17 + 2 * C * CYC)
+    cp(tu("tab0"), ["tu.tab0"] + both("tu.tab0"), T.fl_s[:], ["fl_s", ">ends", ">half", ">y01", ">y02"] + [">col%d" % k for k in range(3, 12)])
 
     KS, KM = ["ka", "kb"], ["kma", "kmb"]
+    parts = lambda two: [("a", 0, TW // 2), ("b", TW // 2, TW)] if two else [("ab", 0, TW)]
+    some = lambda n, h: [n + x for x in h]
 
     def levels(first):
-        SR, SK = OPT["SR"][0 if first else 1], OPT["SK"][0 if first else 1]
-        parts = lambda two: [("a", 0, TW // 2), ("b", TW // 2, TW)] if two else [("ab", 0, TW)]
-        some = lambda n, h: [n + x for x in h]
+        rows = 7 if first else 8
         act(row("ro0"), both("ro0"), T.ramp[:].indirect(tu("tab0")), ["ramp"] + both("tu.tab0"))
         for k in range(9):
-            tab, nxt = "tab%d" % k, "tab%d" % (k + 1)
+            tab, nxt = "tab%d" % min(k, rows), "tab%d" % (k + 1)
             a, b = "ro%d" % k, "ro%d" % (k + 1)
             src = "ramp" if k == 0 else KS[k % 2]
             sm = "k0m" if k == 0 else KM[k % 2]
             dst, dm = KS[(k + 1) % 2], KM[(k + 1) % 2]
             c = "c%d" % (k % 2)
-            for h, x, y in parts(SR) if k < 8 else []:
+            if k > rows:
+                act(row("yk"), ["yk"], row(src).indirect(tu(tab)), both(src) + both("tu." + tab))
+                src = "yk"
+            for h, x, y in parts(first) if k < rows else []:
                 act(row(b, 16 * x, 16 * y), some(b, h), row(a).indirect(tu(tab, x, y)), both(a) + some("tu." + tab, h), gat(16 * (y - x)))
-            for h, x, y in parts(SK) if first or k > 1 else []:
+            for h, x, y in parts(True) if first or k > 1 else []:
                 tt(row(dst, 16 * x, 16 * y), some(dst, h), row(src).indirect(tu(tab, x, y)), row(sm, 16 * x, 16 * y), A.min,
-                   both(src) + some(sm, h) + some("tu." + tab, h), gat(16 * (y - x)))
+                   [src] + both(src) + some(sm, h) + some("tu." + tab, h), gat(16 * (y - x)))
             if k == 8:
                 break
-            for h, x, y in parts(SR):
+            for h, x, y in parts(first) if k < rows else []:
                 scan(row(c, 16 * x, 16 * y), some(c, h), row(b, 16 * x, 16 * y), row("lc", 16 * x, 16 * y), -1024.0, A.max, A.add, some(b, h) + ["lc"], 8 * (y - x) * CYC)
                 ts(tu(nxt, x, y), some("tu." + nxt, h), sampled(c, x, y), cl(2), None, A.add, None, some(c, h) + ["col2"])
             if k == 0 and not first:
-                ts(tf("q0"), ["tf.q0"], tf("b"), cl(11), None, A.add, None, ["tf.b", "col11"])
-                ts(tf("q2"), ["tf.q2"], tf("f"), cl(11), 0.5, A.add, A.add, ["tf.f", "col11"])
-                t2("q2", "q2", "j4", A.min)
-                t2("q0", "q0", "q2", A.min)
-                tt(tf("q0"), ["tf.q0"], tf("q0"), sampled(c), A.min, ["tf.q0"] + both(c))
+                scan(T.y2[:], ["y2"], T.y0[:], T.y1[:], 0.0, A.add, A.min, ["y00", "y01", "y02", "y03", "y1", "tf.b", "tf.f", "tf.jt"], 4 * TW * CYC)
+                tt(tf("q0"), ["tf.q0"], step("y2", 3, 4), sampled(c), A.min, ["y2"] + both(c))
                 ts(tu("k2"), ["tu.k2"], tf("q0"), 4.0, cl(10), A.mult, A.add, ["tf.q0", "col10"])
                 act(row(KS[0]), both(KS[0]), T.kw[:].indirect(tu("k2")), ["kw", "tu.k2"], scale=STEP1)
-            for h, x, y in parts(SK) if first or k > 0 else []:
+            for h, x, y in parts(True) if first or k > 0 else []:
                 act(row(dm, 16 * x, 16 * y), some(dm, h), row(dst, 16 * x, 16 * y), some(dst, h), 16 * (y - x) * CYC, bias=-STEP1 * 2 ** (k + 1))
 
     KF = KS[1]
@@ -225,45 +242,42 @@ def rank_program(g, core, T, topo):
         m = topo.mask(core, dst)
         n = len(topo.engines(core, dst))
         op("g", lambda: g.remote_dma(out_ap=o, in_ap=i, remote_sem=T.sem[sem], local_sem=T.sem.snt, pid=pid, routing_id=rid, dma_engine_mask=m),
-           rk, wk, 0.5, lat=lat, remote=(sem, n))
+           rk, wk, ISSUE, lat=lat, remote=(sem, n))
 
     sp = lambda r, x, a=0, b=TW: T.sp[:, TW * (4 * r + "dpla".index(x)) + a:TW * (4 * r + "dpla".index(x)) + b]
-    PARCELS = {1: ["dpl", "a"], 2: ["d", "pl", "a"], 3: ["d", "p", "l", "a"], 4: ["dp", "l", "a"]}[OPT["SENDS"]]
 
     def landed(r, x):
         p = [y for y in PARCELS if x in y][0]
         return T["l%s%d" % (p[0], r)][:, TW * p.index(x):TW * p.index(x) + TW]
 
     def finish(r):
-        nxt = "tu.tab1" if r else "tu.tab0"
+        nxt = "tab1" if r else "tab0"
         kd, kp, kl, ka = ["sp%d%s" % (r, x) for x in "dpla"]
-        tt(row("yk"), ["yk"], row(KF).indirect(tu(nxt[3:])), row("kc"), A.max, both(KF) + both(nxt) + ["kc"], GAT)
-        latch(KF, both(KF), "ck", c=R4)
+        tt(row("yk"), ["yk"], row(KF).indirect(tu(nxt)), row("kc"), A.max, both(KF) + both("tu." + nxt) + ["kc"], GAT)
+        for h, x, y in parts(True):
+            scan(row("ck", 16 * x, 16 * y), some("ck", h), row(KF, 16 * x, 16 * y), row("lc", 16 * x, 16 * y), -1024.0, A.max, A.add, some(KF, h) + ["lc"], 16 * (y - x) * CYC)
         tabs("ck", tu("root1"), ["tu.root1"], 5)
         tabs("ck", tu("root"), ["tu.root"], 4)
         tabs("ck", ti("k"), ["ti.k"], 3, 1024.0)
         ts(ti("d"), ["ti.d"], ti("k"), 511, None, A.bitwise_and, None, ["ti.k"])
-        ts(tf("dq"), ["tf.dq"], ti("d"), cl(6), None, A.add, None, ["ti.d", "col6"])
         cp(sp(r, "d"), [kd], ti("d"), ["ti.d"])
-        act(row("drow"), ["drow"], T.ramp[:].indirect(sp(r, "d")), ["ramp", kd])
+        act(row("drow"), ["drow"], row("ends").indirect(sp(r, "d")), ["ends", "ends0", kd])
         scan(T.cum[:, 1:C + 1], ["cum"], row("yk"), row("kc"), -224.0 * STEP1, A.add, A.subtract, ["yk", "kc"])
         ke = pick("erow", T.cum[:, 0:C + 1], lambda a, b: tu("root1", a, b), ["cum", "cum0", "tu.root1"], OPT["HE"], 1024.0)
         act(row("srow"), ["srow"], T.cum[:, 0:C + 1].indirect(tu("root")), ["cum", "cum0", "tu.root"], scale=1024.0)
-        latch("erow", ke, "c2")
-        tt(tf("pl"), ["tf.pl"], sampled("c2"), tf("dq"), A.subtract, ["c2", "tf.dq"])
-        cp(sp(r, "p"), [kp], tf("pl"), ["tf.pl"])
-        latch("srow", ["srow"], "c3")
-        tt(tf("ln"), ["tf.ln"], sampled("c2"), sampled("c3"), A.subtract, ["c2", "c3"])
+        tt(sampled("lcp"), ["lcp"], sampled("lc"), ti("d"), A.subtract, ["lc", "ti.d"])
+        latch("erow", ke, "c2", "lcp")
+        tabs("c2", sp(r, "p"), [kp], 8)
+        op("v", lambda: g.vector.tensor_copy(row("cp").indirect(sp(r, "p")), row("code9")), ["code9", kp], ["cp"], SCA)
+        tt(tf("en"), ["tf.en"], sampled("c2"), ti("d"), A.add, both("c2") + ["ti.d", ">cp"])
+        latch("srow", ["srow", ">cp"], "c3")
+        tt(tf("ln"), ["tf.ln"], tf("en"), sampled("c3"), A.subtract, both("c3") + ["tf.en"])
         cp(sp(r, "l"), [kl], tf("ln"), ["tf.ln"])
-        op("v", lambda: g.vector.tensor_copy(row("cp").indirect(sp(r, "p")), row("code9")), ["code9", kp] + OPT.get("PRE", 1) * [">" + kl], ["cp"], SCA)
-        latch("cp", ["cp"], "c4", True)
+        latch("cp", ["cp"], "c4", "lc9", -2.0)
         tabs("c4", sp(r, "a"), [ka], 2, 512.0)
         for p in PARCELS:
-            w = TW * len(p)
-            send(r, T["l%s%d" % (p[0], r)][:, 0:w], sp(r, p[0], 0, w), ["sp%d%s" % (r, x) for x in p], ["l%d%s" % (r, x) for x in p], "a%s%d" % (p[0], r), 0.12 * len(p))
-        tabs("c2", tu("last"), ["tu.last"], 8)
-        ts(tf("ple"), ["tf.ple"], tf("pl"), cl(2), None, A.subtract, None, ["tf.pl", "col2"])
-        act(row("plr"), ["plr"], T.ramp[:].indirect(sp(r, "p")), ["ramp", kp])
+            send(r, T["l%s%d" % (p[0], r)][:], sp(r, p[0], 0, TW * len(p)), ["sp%d%s" % (r, x) for x in p], ["l%d%s" % (r, x) for x in p], "a%s%d" % (p[0], r), 0.12 * len(p))
+        ts(tu("last"), ["tu.last"], tf("en"), cl(8), None, A.add, None, ["tf.en", "col8"])
 
     def mm(dst, b, st, so, mv, a=0, z=C, rk=None):
         op("t", lambda: g.tensor.matmul_mx(T[dst][:, 512 * b:512 * b + z - a], T[st][:, so:so + 128], T[st + "s"][:, so:so + 128], T[mv][:, a:z], T[mv + "s"][:, a:z], True, True),
@@ -288,24 +302,19 @@ def rank_program(g, core, T, topo):
         ts(tf(h), ["tf." + h], tf(h), 0.5, None, A.mult, None, ["tf." + h])
         t2(c, x, h, A.subtract)
 
-    def ahead():
-        ts(tf("fp"), ["tf.fp"], tf("cf"), -2.0, None, A.mult, None, ["tf.cf"])
-        ts(tf("fr"), ["tf.fr"], tf("cf"), cl(7), None, A.mult, None, ["tf.cf", "col7"])
-        t2("fq", "fr", "hf", A.add)
-
     levels(True)
     cp(tu("m"), ["tu.m"], T.ml_s[:], ["ml_s"])
     cp(tf("f"), ["tf.f"], T.fl_s[:], ["fl_s"])
     cp(tf("m"), ["tf.m"], T.ml_s[:], ["ml_s"])
-    act(row("fmr"), ["fmr"], row("ro0").indirect(tu("m")), both("ro0") + ["tu.m", ">ro8b"])
+    act(row("fmr"), ["fmr"], row("ro0").indirect(tu("m")), both("ro0") + ["tu.m", ">ro7b"])
     latch("fmr", ["fmr"], "c8")
     tabs("c8", tf("fm"), ["tf.fm"], 2)
     halves("f", "fm", "hf", "cf")
-    ts(tf("jt"), ["tf.jt"], tf("jt"), cl(0), None, A.add, None, ["jt0", "col0"])
-    ts(tf("j4"), ["tf.j4"], tf("jt"), cl(11), 0.25, A.add, A.add, ["tf.jt", "col11"])
+    ts(tf("jt"), ["tf.jt"], tf("j16"), cl(0), None, A.add, None, ["tf.j16", "col0"])
+    ts(step("y0", 3, 4), ["y03"], tf("j16"), 0.0, cl(11), A.mult, A.add, ["tf.j16", "col11"])
     t2("sn", "jt", "m", A.is_lt)
-    ts(tf("oa"), ["tf.oa"], tf("sn"), -float(C), float(C), A.mult, A.add, ["tf.sn"])
-    ts(tf("ob"), ["tf.ob"], tf("sn"), float(C), None, A.mult, None, ["tf.sn"])
+    ts(z1(5), ["z15"], tf("sn"), -float(C), float(C), A.mult, A.add, ["tf.sn"])
+    ts(z1(6), ["z16"], tf("sn"), 2.0 * C, -float(C), A.mult, A.add, ["tf.sn"])
     quant("xin", ["xin"], C, "qx0")
     quant("uin", ["uin"], 128, "qu")
     cp(T.ofu[:], ["ofu"], T.ofi[:], ["ofi"])
@@ -313,18 +322,21 @@ def rank_program(g, core, T, topo):
     op("s", lambda: g.scalar.activation(T.qurs[:, 0:128], T.qus[:, 0:128].indirect(T.ofu[:, 0:8]), AF.Copy), ["qus", "ofu"], ["qurs"], gat(128))
     quant("et", ["et0", "et1", "et2", "et3"], 512, "qe")
     state_made(0)
-    act(row("kc"), ["kc"], row("ramp"), ["ramp", ">ro2b"], R4, bias=-0.5)
+    act(row("kc"), ["kc"], row("ramp"), ["ramp", ">ro7b"], R4, bias=-0.5)
+    act(row("code9"), ["code9"], row("ramp"), ["ramp", ">kc"], R4, scale=2.0 ** -9)
+    act(row("lc9"), ["lc9"], row("lc"), ["lc", ">kc"], R4, scale=2.0 ** -9)
     finish(0)
     iota(T.kw[:], ["kw"], [[1024, C], [1, 4]], -3 - 224 * 1024, 0, 4 * C, rk=[">l0a"])
-    tt(tf("e1"), ["tf.e1"], tf("ple"), sampled("c3"), A.is_equal, ["tf.ple", "c3"])
+    ts(tf("ple"), ["tf.ple"], sampled("c2"), -1.0, None, A.add, None, both("c2"))
+    tt(tf("e1"), ["tf.e1"], tf("ple"), sampled("c3"), A.is_equal, ["tf.ple"] + both("c3"))
     t2("e1", "e1", "ln", A.mult)
-    t2("e1", "e1", "pl", A.add)
-    ts(tu("b"), ["tu.b"], tf("e1"), -1.0, None, A.add, None, ["tf.e1"])
+    t2("e1", "e1", "ple", A.add)
+    ts(tu("b"), ["tu.b"], tf("e1"), cl(8), None, A.add, None, ["tf.e1", "col8"])
     act(row("brow"), ["brow"], row("cp").indirect(tu("b")), ["cp", "tu.b"], scale=512.0)
     latch("brow", ["brow"], "c7")
     tabs("c7", tu("b"), ["tu.b"], 2)
     tabs("c7", tf("b"), ["tf.b"], 2)
-    act(row("mrow"), ["mrow"], T.ramp[:].indirect(tu("m")), ["ramp", "tu.m", ">ro8b"])
+    act(row("mrow"), ["mrow"], T.ramp[:].indirect(tu("m")), ["ramp", "tu.m", ">ro7b"])
     act(row("mbr"), ["mbr"], row("mrow").indirect(tu("b")), ["mrow", "tu.b"])
     latch("mbr", ["mbr"], "c8")
     tabs("c8", tf("mb"), ["tf.mb"], 2)
@@ -333,84 +345,91 @@ def rank_program(g, core, T, topo):
     def store(eng, out, src, keys, lat=2.0):
         op(eng, lambda: Q[eng].dma_start(out, src), keys, [], 0.07, sem="outs", inc=16, lat=lat)
 
+    marks = []
     for r in range(3):
         ks = "sp%da" % r
         last = r == 2
-        act(T.rst[:, 1:C + 1], ["rst"], row("drow").indirect(sp(r, "a")), ["drow", ks], scale=-BIG, bias=-223.5 * BIG)
-        ka = pick("sa", row("sr"), lambda a, b: sp(r, "a", a, b), ["sr", ks], OPT["HA"])
-        scan(row("pm"), ["pm"], row("rst"), row("sa"), BIG, A.max, A.min, ["rst", "rst0"] + ka)
+        marks.append(len(prog))
+        act(T.rst[:, 1:C + 1], ["rst"], row("drow").indirect(sp(r, "a")), ["drow", ks], bias=-BIG / 2)
+        act(T.rs2[:, 1:C + 1], ["rs2"], row("drow").indirect(sp(r, "a")), ["drow", ks])
+        cp(row("sa"), both("sa"), row("sr").indirect(sp(r, "a")), ["sr", ks], GAT)
+        scan(row("pm"), ["pm"], row("rst"), row("sa"), BIG, A.max, A.min, ["rst", "rst0"] + both("sa"))
         tt(row("neq"), ["neq"], row("pm").indirect(tu("last")), row("sr"), A.not_equal, ["pm", "tu.last", "sr"], GAT)
         tt(row("cand"), ["cand"], row("neq").indirect(sp(r, "a")), row("cp"), A.add, ["neq", ks, "cp"], GAT)
-        scan(row("cm"), ["cm"], row("rst"), row("cand"), BIG, A.max, A.min, ["rst", "rst0", "cand"], R2)
-        kl = pick("lrow", row("cm"), lambda a, b: tu("last", a, b), ["cm", "tu.last"], OPT["HL"], 512.0)
-        latch("lrow", kl, "c5")
-        tabs("c5", tu("l"), ["tu.l"], 2)
+        scan(row("pm"), ["pm"], row("rs2"), row("cand"), 0.0, A.add, A.min, ["rs2", "rs20", "cand"])
+        latch("sa", pick("sa", row("pm"), lambda a, b: tu("last", a, b), ["pm", "tu.last"], OPT["HL"], 512.0), "ck", c=R4)
+        tabs("ck", tu("l"), ["tu.l"], 6)
+        ts(ti("k"), ["ti.k"], sampled("ck"), cl(2), 1024.0, A.add, A.mult, both("ck") + ["col2"])
+        ts(ti("e"), ["ti.e"], ti("k"), 1023, None, A.bitwise_and, None, ["ti.k"])
         for b in range(4):
             act(row("fh%d" % b), ["fh%d" % b], T.pa[:, 512 * b:512 * b + C], ["pa%d" % b], R4)
         for x, n in zip("dlpa", ["tdrow", "lenrow", "tprow", "ar"]):
             act(row(n), [n], T.ramp[:].indirect(landed(r, x)), ["ramp", "l%d%s" % (r, x)])
-        for i, n in enumerate(["lenrow", "plr", "tdrow", "tprow"]):
-            kg = pick("gr%d" % i, row(n), lambda a, b: tu("l", a, b), [n, "tu.l"], {"v": 0, "s": TW, "h": 14}[OPT["BYL"][i]])
-            latch("gr%d" % i, kg, "x%d" % i)
-        xl, xp, xd, xt = [sampled("x%d" % i) for i in range(4)]
+        for i, (n, h) in enumerate([("lenrow", 0), ("tdrow", TW), ("tprow", TW)]):
+            latch("gr%d" % i, pick("gr%d" % i, row(n), lambda a, b: tu("l", a, b), [n, "tu.l"], h), "x%d" % i)
         for b in range(4):
-            act(row("ft%d" % b), ["ft%d" % b], T.pb[:, 512 * b:512 * b + C], ["pb%d" % b], R4)
-        tabs("x0", tf("l3"), ["tf.l3"], 2)
-        op("v", lambda: g.vector.reciprocal(tf("inv"), tf("l3")), ["tf.l3"], ["tf.inv"], 0.19 + 6 * TW * CYC)
+            if b >= OPT["FTV"]:
+                act(row("ft%d" % b), ["ft%d_0" % b], T.pb[:, 512 * b:512 * b + C], ["pb%d" % b], R4)
+                continue
+            for x in range(0, C, C // 4):
+                cp(row("ft%d" % b, x, x + C // 4), ["ft%d_%d" % (b, x)], T.pb[:, 512 * b + x:512 * b + x + C // 4], ["pb%d" % b], C // 4 * CYC)
+        ts(z0(4), ["z04"], sampled("x0"), cl(2), None, A.add, None, both("x0") + ["col2", "z0"])
+        op("v", lambda: g.vector.reciprocal(z0(2), z0(4)), ["z04", "z0"], ["z02"], 0.19 + 6 * TW * CYC)
         tabs("x0", tf("hl"), ["tf.hl"], 9, 0.5)
-        tt(tf("ng"), ["tf.ng"], tf("ple"), xp, A.is_lt, ["x1", "tf.ple"])
+        tt(tf("ng"), ["tf.ng"], ti("e"), ti("d"), A.is_lt, ["ti.e", "ti.d"])
+        tt(tf("w"), ["tf.w"], ti("e"), ti("d"), A.subtract, ["ti.e", "ti.d"])
         t2("t1", "ng", "ln", A.mult)
-        tt(tf("w"), ["tf.w"], tf("pl"), xp, A.subtract, ["x1", "tf.pl"])
-        t2("a1", "w", "t1", A.add)
-        tt(tf("a2"), ["tf.a2"], tf("hl"), xd, A.subtract, ["x2", "tf.hl"])
-        t2("u", "a1", "a2", A.add)
-        tt(ti("n"), ["ti.n"], tf("u"), tf("inv"), A.mult, ["tf.u", "tf.inv"])
-        tt(tf("t2"), ["tf.t2"], ti("n"), tf("l3"), A.mult, ["ti.n", "tf.l3"])
-        tt(tf("bq"), ["tf.bq"], tf("a1"), xt, A.add, ["x3", "tf.a1"])
-        t2("tp", "bq", "t2", A.subtract)
-        for x in "ab":
-            t2("b" + x, "bq", "o" + x, A.add)
-            t2("tp" + x, "b" + x, "t2", A.subtract)
-        cp(tu("tp", 0, 3 * TW), ["tu.tp"], tf("tp", 3), ["tf.tp", "tf.tpa", "tf.tpb"], 84 * CYC)
-        kt = pick("trow", row("ar"), lambda a, b: tu("tp", a, b), ["ar", "tu.tp"], OPT["HT"] if last else TW)
-        latch("trow", kt, "c6")
+        tt(z1(1), ["z11"], tf("w"), tf("t1"), A.add, ["tf.w", "tf.t1"])
+        tt(z1(0), ["z10"], tf("hl"), sampled("x1"), A.subtract, both("x1") + ["tf.hl"])
+        tt(z1(4), ["z14"], z1(1), sampled("x2"), A.add, both("x2") + ["z11"])
+        scan(T.z2[:], ["z2"], T.z0[:], T.z1[:], 0.0, A.mult, A.add, ["z0", "z02", "z04"] + ["z1%d" % k for k in range(7)], 7 * TW * CYC)
+        for k, x in ((5, "tpa"), (6, "tpb"), (4, "tp")):
+            ts(tu(x), ["tu." + x], z2(k), cl(2), None, A.add, None, ["z2", "col2"])
+        latch("trow", pick("trow", row("ar"), lambda a, b: tu("tp", a, b), ["ar", "tu.tp"], OPT["HT"] if last else TW), "c6")
         tabs("c6", tu("T"), ["tu.T"], 2)
         act(row("sfa"), ["sfa"], row("sr").indirect(landed(r, "a")), ["sr", "l%da" % r])
         act(row("sfa", C, 2 * C), ["sfb"], row("sfa"), ["sfa"], R4, scale=-1.0)
-        cp(row("mu"), ["mu"], T.sfa[:].indirect(tu("tpa")), ["sfa", "sfb", "tu.tp"], GAT)
-        act(row("nu"), ["nu"], T.sfa[:].indirect(tu("tpb")), ["sfa", "sfb", "tu.tp"])
+        cp(row("mu"), ["mu"], T.sfa[:].indirect(tu("tpa")), ["sfa", "sfb", "tu.tpa"], GAT)
+        act(row("nu"), ["nu"], T.sfa[:].indirect(tu("tpb")), ["sfa", "sfb", "tu.tpb"])
         tt(row("sw"), ["sw"], row("mu").indirect(tu("m")), row("nu"), A.is_gt, ["mu", "nu", "tu.m"], GAT)
         latch("sw", ["sw"], "c9")
-        if OPT["X3"]:
-            ahead()
-            tt(tf("sw"), ["tf.sw"], sampled("c9"), tf("fp"), A.mult, ["c9", "tf.fp"])
-            t2("f", "sw", "fq", A.add)
-            if not last:
-                t2("cf", "f", "hf", A.subtract)
-        else:
-            tabs("c9", tf("sw"), ["tf.sw"], 7, -2.0)
-            t2("cf", "sw", "cf", A.mult)
-            t2("f", "hf", "cf", A.add)
-        cp(tu("tab0"), ["tu.tab0"] + both("tu.tab0"), tf("f"), ["tf.f"])
-        act(row("swb"), ["swb"], row("sw").indirect(tu("b")), ["sw", "tu.b"])
-        latch("swb", ["swb"], "c7")
+        tabs("c9", tf("sw"), ["tf.sw"], 7, -2.0)
+        scan(T.v2[:], ["v2"], T.v0[:], T.v1[:], 0.0, A.mult, A.add, ["v0", "v1", "tf.cf", "tf.hf", "tf.sw"], 3 * TW * CYC)
+        if not last:
+            cp(tf("cf"), ["tf.cf"], step("v2", 1, 3), ["v2"])
+            cp(tf("f"), ["tf.f"], step("v2", 2, 3), ["v2"])
+        cp(tu("tab0"), ["tu.tab0"] + both("tu.tab0"), step("v2", 2, 3), ["v2"])
+        latch("swb", pick("swb", row("sw"), lambda a, b: tu("b", a, b), ["sw", "tu.b"], TW if last else OPT["HB"]) + [">tu.tab0"], "c7")
         tabs("c7", tf("swb"), ["tf.swb"], 7, -2.0)
         t2("cb", "swb", "cb", A.mult)
         t2("b", "hb", "cb", A.add)
         cp(tu("b"), ["tu.b"], tf("b"), ["tf.b"])
+        if not last:
+            levels(False)
         for b in range(4):
-            act(row("fs%d" % b), ["fs%d" % b], row("ft%d" % b).indirect(tu("T")), ["ft%d" % b, "tu.T"])
-            tt(T.zt[:, b:4 * C:4], ["zt%d" % b], row("fh%d" % b).indirect(tu("tab0")), row("fs%d" % b), A.add, ["fh%d" % b, "fs%d" % b, "tu.tab0"], GAT)
-        quant("zt", ["zt0", "zt1", "zt2", "zt3"], C, "qz")
+            act(row("fs%d" % b), ["fs%d" % b], row("ft%d" % b).indirect(tu("T")), ["ft%d_%d" % (b, x) for x in range(0, C, C // 4)] + ["tu.T"])
+        cuts = OPT["ZCUT"] if last else [0, TW]
+        for h, (a, z) in enumerate(zip(cuts, cuts[1:])):
+            n = 16 * (z - a)
+            for b in range(4):
+                tt(T.zt[:, 64 * a + b:64 * z:4], ["zt%d%d" % (h, b)], row("fh%d" % b).indirect(tu("tab0", a, z)), row("fs%d" % b, 16 * a, 16 * z), A.add,
+                   ["fh%d" % b, "fs%d" % b, "tu.tab0"], gat(n))
+            quant("zt", ["zt%d%d" % (h, b) for b in range(4)], n, "qz", 16 * a, ["qz%d" % h])
+            for b in range(4):
+                k = (b + 2 * h) % 4
+                mm("pb", k, "wq", 128 * b, "qz", 16 * a, 16 * z, ["qz%d" % h])
+                act(row("r2%d" % b, 16 * a, 16 * z), ["r2%d%d" % (h, b)], T.pb[:, 512 * k:512 * k + n], ["pb%d" % k], n * CYC, scale=0.015625)
         if last:
-            quant("vin", ["vin", ">qz"], 128, "qv")
-        for b in range(4):
-            mm("pb", b, "wq", 128 * b, "qz")
-            act(row("r2%d" % b), ["r2%d" % b], T.pb[:, 512 * b:512 * b + C], ["pb%d" % b], R4, scale=0.015625)
+            quant("vin", ["vin", ">qz0"], 128, "qv")
         for h, (a, z) in enumerate(zip(OPT["XCUT"], OPT["XCUT"][1:]) if last else [(0, TW)]):
             n = 16 * (z - a)
             for b in range(4):
-                tt(T.xt[:, 64 * a + b:64 * z:4], ["xt%d%d" % (h, b)], row("r2%d" % b).indirect(tu("b", a, z)), row("fh%d" % b, 16 * a, 16 * z), A.add, ["r2%d" % b, "fh%d" % b, "tu.b"], gat(n))
+                out, src, rk = T.xt[:, 64 * a + b:64 * z:4], row("r2%d" % b).indirect(tu("b", a, z)), ["r20%d" % b, "r21%d" % b, "tu.b"]
+                if h and b >= 4 - OPT["NL"]:
+                    act(row("pp%d" % b, 0, n), ["pp%d" % b], src, rk, gat(n))
+                    tt(out, ["xt%d%d" % (h, b)], row("pp%d" % b, 0, n), T.pa[:, 512 * b + 16 * a:512 * b + 16 * z], A.add, ["pp%d" % b, "pa%d" % b], n * CYC)
+                else:
+                    tt(out, ["xt%d%d" % (h, b)], src, row("fh%d" % b, 16 * a, 16 * z), A.add, rk + ["fh%d" % b], gat(n))
             keys = ["xt%d%d" % (h, b) for b in range(4)]
             if not last:
                 quant("xt", keys, C, "qx%d" % (r + 1))
@@ -419,17 +438,16 @@ def rank_program(g, core, T, topo):
             quant("xt", keys, n, "qx3", 16 * a, [q])
             mm("pb", h, "qv", 0, "qx3", 16 * a, 16 * z, [q])
             store("y", T.oc[:, 64 * a:64 * z], T.qx3[:, 16 * a:16 * z].bitcast(dt.uint8), [q], 1.8 + n / 400)
-            act(row("sa", 16 * a, 16 * z), ["y%d" % h, "saa", "sab"], T.pb[:, 512 * h:512 * h + n], ["pb%d" % h], n * CYC)
-            store("s", T.y[:, 16 * a:16 * z], row("sa", 16 * a, 16 * z), ["y%d" % h], 1.8 + n / 400)
+            act(row("sa", 16 * a, 16 * z), ["y%d_" % h] + both("sa"), T.pb[:, 512 * h:512 * h + n], ["pb%d" % h], n * CYC)
+            store("s", T.y[:, 16 * a:16 * z], row("sa", 16 * a, 16 * z), ["y%d_" % h], 1.8 + n / 400)
         if last:
             break
-        levels(False)
         state_made(r + 1)
         finish(r + 1)
     act(row("nlr"), ["nlr"], T.ramp[:].indirect(tu("tab0")), ["ramp", "tu.tab0"], bias=224.0)
     store("y", T.nl[:], T.nlr[0:128:16, :], ["nlr"])
     for k in range(4):
-        store("y", T.osc[4 * k:4 * k + 4, :], T.qx3s[32 * k:32 * k + 4, 0:C], ["qx30", "qx31", "qx32"])
+        store("y", T.osc[4 * k:4 * k + 4, :], T.qx3s[32 * k:32 * k + 4, 0:C], ["qx30", "qx31"])
 
     n = len(prog)
     deps, kids = [set() for _ in range(n)], [[] for _ in range(n)]
@@ -452,7 +470,7 @@ def rank_program(g, core, T, topo):
         for d in deps[i]:
             kids[d].append(i)
     dl, far = [list(d) for d in deps], [bool(p["remote"]) for p in prog]
-    lat, cost = [p["lat"] for p in prog], [[p["cs"][m] for p in prog] for m in range(3)]
+    lat, cost = [p["lat"] for p in prog], [[p["cs"][m] for p in prog] for m in GUESSES]
 
     def lay(rank_):
         at, done, left, tq, link = [0.0] * n, [0.0] * n, [len(x) for x in deps], {e: 0.0 for e in Q}, 0.0
@@ -472,17 +490,28 @@ def rank_program(g, core, T, topo):
             done[i] = tq[e] + lat[i] + WAKES[0]
             if far[i]:
                 link = max(link, tq[e] + STARTS[0]) + lat[i]
-                done[i] = link + OPT["RW"] + WAKES[0]
+                done[i] = link + FARWAKE + WAKES[0]
             for k in kids[i]:
                 left[k] -= 1
                 if not left[k]:
                     ready[prog[k]["eng"]].append((max(done[d] for d in deps[k]), k))
         return at, done
 
-    def clock_of(seq, m):
+    def clock_of(seq, m, old=None, since=0.0):
         c, wake, start, rate = cost[m], WAKES[m], STARTS[m], RATES[m]
         at, done, by, link, left = [0.0] * n, [-1.0] * n, [-1] * n, 0.0, n
         state = [[q, 0, 0.0] for q in seq.values()]
+        for st in state if old else []:
+            q, pos = st[0], 0
+            while pos < len(q) and old[0][q[pos]] < since:
+                i = q[pos]
+                at[i], done[i], by[i] = old[0][i], old[1][i], old[2][i]
+                if far[i]:
+                    link = done[i] - FARWAKE - wake
+                pos += 1
+            if pos:
+                st[1], st[2] = pos, at[q[pos - 1]] + c[q[pos - 1]]
+                left -= pos
         while left:
             before = left
             for st in state:
@@ -501,7 +530,7 @@ def rank_program(g, core, T, topo):
                         t = t1 + c[i]
                         if far[i]:
                             link = max(link, t + start) + lat[i] * rate
-                            done[i] = link + OPT["RW"] + wake
+                            done[i] = link + FARWAKE + wake
                         else:
                             done[i] = t + lat[i] + wake
                         pos += 1
@@ -514,59 +543,99 @@ def rank_program(g, core, T, topo):
         return at, done, by
 
     if "seq" not in ORDER:
-        span = [cost[0][i] + lat[i] + WAKES[0] + far[i] * (STARTS[0] + OPT["RW"]) for i in range(n)]
+        span = [cost[0][i] + lat[i] + WAKES[0] + far[i] * (STARTS[0] + FARWAKE) for i in range(n)]
         prio = [0.0] * n
         for i in range(n - 1, -1, -1):
             prio[i] = span[i] + max([prio[k] for k in kids[i]] + [0.0])
         total = lambda runs: sum(max(x[1]) for x in runs)
-        kept = None
-        for _ in range(OPT["PASS"] + 1):
-            at, done = lay([-x for x in prio])
-            order = sorted(range(n), key=lambda i: (at[i], i))
-            seq = {e: [i for i in order if prog[i]["eng"] == e] for e in Q}
-            runs = [clock_of(seq, m) for m in range(3)]
-            if kept is None or total(runs) < kept[0]:
-                kept = (total(runs), seq, runs[0][0])
-            tail, behind = [0.0] * n, {}
-            for i in reversed(order):
-                own = span[i] + max([tail[k] for k in kids[i]] + [0.0])
-                tail[i] = max(own, cost[0][i] + behind.get(prog[i]["eng"], 0.0))
-                behind[prog[i]["eng"]] = tail[i]
-                prio[i] += OPT["ALPHA"] * (own - prio[i])
         seed = [OPT["SEED"]]
 
         def draw(k):
             seed[0] = (seed[0] * 1103515245 + 12345) % 2 ** 31
             return (seed[0] >> 8) % k
 
+        def laid(pr):
+            at, done = lay([-x for x in pr])
+            order = sorted(range(n), key=lambda i: (at[i], i))
+            seq = {e: [i for i in order if prog[i]["eng"] == e] for e in Q}
+            return max(done) + sum(max(clock_of(seq, m)[1]) for m in GUESSES[1:]), seq, at, order
+
+        kept, pr = None, list(prio)
+        for _ in range(OPT["PASS"] + 1):
+            new = laid(pr)
+            if kept is None or new[0] < kept[0]:
+                kept, prio = new, list(pr)
+            tail, behind = [0.0] * n, {}
+            for i in reversed(new[3]):
+                own = span[i] + max([tail[k] for k in kids[i]] + [0.0])
+                tail[i] = max(own, cost[0][i] + behind.get(prog[i]["eng"], 0.0))
+                behind[prog[i]["eng"]] = tail[i]
+                pr[i] += OPT["ALPHA"] * (own - pr[i])
+        kinds = {}
+        for i, p in enumerate(prog):
+            kinds.setdefault(p["w"][0].rstrip("0123456789") if p["w"] else "", []).append(i)
+        kinds = list(kinds.values())
+        for _ in range(OPT["KINDS"]):
+            pr, more = list(prio), [-4.0, -2.0, -1.0, -0.4, 0.4, 1.0, 2.0, 4.0][draw(8)]
+            for i in kinds[draw(len(kinds))]:
+                pr[i] += more
+            new = laid(pr)
+            if new[0] <= kept[0]:
+                kept, prio = new, pr
+        OPT["MID"] = kept[0] / 3
         seq = {e: list(q) for e, q in kept[1].items()}
-        runs = [clock_of(seq, m) for m in range(3)]
+        runs = [clock_of(seq, m) for m in GUESSES]
+        twin = marks[1] - marks[0]
+
+        def chain_of(run):
+            i, chain = run[1].index(max(run[1])), []
+            while run[2][i] >= 0:
+                chain.append(i)
+                i = run[2][i]
+            return chain, [i for i in chain if run[2][i] not in deps[i]]
+
+        ends, chains = [max(x[1]) for x in runs], {}
         for it in range(OPT["TRIES"]):
-            at, done, by = runs[draw(3)]
-            if draw(10) < 8:
-                i, pairs = done.index(max(done)), []
-                while by[i] >= 0:
-                    if by[i] not in deps[i]:
-                        pairs.append(i)
-                    i = by[i]
+            m = draw(len(runs))
+            if m not in chains:
+                chains[m] = chain_of(runs[m])
+            at, (chain, pairs) = runs[m][0], chains[m]
+            if draw(10) < 6:
                 i = pairs[draw(len(pairs))]
                 q = seq[prog[i]["eng"]]
                 a, hop = q.index(i), [1, 1, 2, 3, 5, 9][draw(6)]
                 a, b = (a, max(0, a - hop)) if draw(2) else (a - 1, min(len(q) - 1, a - 1 + hop))
             else:
-                q = seq["vs"[draw(2)]]
-                a = draw(len(q))
+                t, q = at[chain[draw(len(chain))]], seq["vs"[draw(2)]]
+                a, b = 0, len(q)
+                while a < b:
+                    a, b = ((a + b) // 2 + 1, b) if at[q[(a + b) // 2]] < t else (a, (a + b) // 2)
+                a = min(len(q) - 1, max(0, a + draw(9) - 6))
                 b = min(len(q) - 1, max(0, a + draw(7) - 3))
+            i, j = q[a], q[b]
+            if a == b or any(x in deps[i] for x in q[b:a]) or any(i in deps[x] for x in q[a + 1:b + 1]):
+                continue
+            was = list(q)
             q.insert(b, q.pop(a))
+            for lo, hi, shift in ((marks[0], marks[1], twin), (marks[1], marks[2], -twin)) if draw(10) < 8 else ():
+                if lo <= i < hi and lo <= j < hi:
+                    q.remove(i + shift)
+                    q.insert(q.index(j + shift) + (b > a), i + shift)
             allow = -(OPT["HEAT"] * (1.0 - it / OPT["TRIES"]) + 0.01) * math.log((draw(9999) + 1) / 10000)
-            first = clock_of(seq, 0)
-            new = first and max(first[1]) - max(runs[0][1]) < allow / 2 + 0.1 and [first, clock_of(seq, 1), clock_of(seq, 2)]
-            if new and total(new) - total(runs) < allow:
-                runs = new
-                if total(runs) < kept[0]:
-                    kept = (total(runs), {e: list(z) for e, z in seq.items()}, runs[0][0])
+            k = next((x for x, y in zip(was, q) if x != y), q[-1])
+            new, more = [], 0.0
+            for m in GUESSES:
+                run = clock_of(seq, m, runs[m], runs[m][0][k])
+                more += max(run[1]) - ends[m] if run else 99.0
+                if more > allow * (m + 2) / (len(runs) + 1) + 0.1 * (len(runs) - 1 - m):
+                    break
+                new.append(run)
+            if len(new) == len(runs):
+                runs, ends, chains = new, [max(x[1]) for x in new], {}
+                if sum(ends) < kept[0]:
+                    kept = (sum(ends), {e: list(z) for e, z in seq.items()}, runs[0][0])
             else:
-                q.insert(a, q.pop(b))
+                q[:] = was
         ORDER["seq"] = kept
     at = ORDER["seq"][2]
     place = {i: k for q in ORDER["seq"][1].values() for k, i in enumerate(q)}

import math
import numpy as np
from concourse.mybir import dt, AluOpType, ActivationFunctionType

C = 448
TW = 28
STEP = [1, 2, 3]
OPT = {"HE": 12, "HL": 12, "HT": 12, "HB": 14, "ZCUT": [0, 16, 28], "XCUT": [0, 20, 28], "NL": 3, "FTV": 2,
       "LOOK": 0.02, "KAP": 0.6, "PASS": 30, "ALPHA": 0.3, "KINDS": 350, "TRIES": 75000, "HEAT": 0.3, "SEED": 6}
PARCELS = ["dp", "la"]
SCRATCH = {}


def _decl():
    f32, bf, f16 = "float32", "bfloat16", "float16"
    for n in ["k0m", "kc", "ka", "kb", "kma", "kmb", "yk", "sr", "sa", "pm", "mu", "nu", "ck", "nlr"]:
        SCRATCH[n] = ("sbuf", [128, C], f32)
    SCRATCH["sfa"] = ("sbuf", [128, 2 * C], f32)
    SCRATCH["lcp"] = ("sbuf", [128, C], f16)
    for n, k in [("z", 7), ("y", 4), ("v", 3)]:
        for i in range(3):
            SCRATCH["%s%d" % (n, i)] = ("sbuf", [128, k * TW], f32)
    for n in ["cum", "rst", "rs2", "ramp"]:
        SCRATCH[n] = ("sbuf", [128, C + 16], bf)
    for n in ["neq", "cand", "cp", "code9", "tprow", "tdrow", "lenrow", "trow", "sw", "swb", "brow", "mrow", "mbr", "lc", "lc9", "fmr", "erow", "srow", "drow", "ar", "ends"]:
        SCRATCH[n] = ("sbuf", [128, C], bf)
    SCRATCH["ro"] = ("sbuf", [128, 9 * C], bf)
    SCRATCH["cc"] = ("sbuf", [128, 10 * C], f16)
    SCRATCH["c4s"] = ("sbuf", [128, 3 * C], f16)
    for n in ["gr", "fh", "ft", "fs", "xin", "xt", "zt"]:
        SCRATCH[n] = ("sbuf", [128, 4 * C], bf)
    for n in ["r2", "kw", "pp"]:
        SCRATCH[n] = ("sbuf", [128, 4 * C], f32)
    for n in ["uin", "vin"]:
        SCRATCH[n] = ("sbuf", [128, 512], bf)
    SCRATCH["et"] = ("sbuf", [128, 2048], bf)
    SCRATCH["half"] = ("sbuf", [128, 128], bf)
    for n, w in [("wq", 512), ("qe", 512), ("qu", 128), ("qur", 128), ("qv", 128), ("qz", C)] + [("qx%d" % i, C) for i in range(4)] + [("lq%d" % i, C) for i in range(3)]:
        SCRATCH[n] = ("sbuf", [128, w], "float8_e4m3fn_x4")
        SCRATCH[n + "s"] = ("sbuf", [128, w], "uint8")
    for n, w, t in [("fl_s", TW, "int32"), ("ml_s", TW, "int32"), ("pq", TW, "int32"), ("pqm", TW, "int32"), ("ofq", TW, "uint16"), ("ofi", 8, "int32"), ("ofu", 8, "uint16"),
                    ("col", 16, f32), ("tf", TW * 24, f32), ("ti", TW * 4, "int32"), ("tu", TW * 24, "uint16"), ("t16", 16, bf), ("la16", 16, bf), ("lb16", 16, bf), ("lc16", 16, bf)]:
        SCRATCH[n] = ("sbuf", [128, w], t)
    SCRATCH["sp"] = ("sbuf", [128, 3 * 4 * TW], "uint16")
    for i in range(3):
        for x in PARCELS:
            SCRATCH["l%s%d" % (x[0], i)] = ("sbuf", [128, len(x) * TW], "uint16")
    SCRATCH["pa"] = ("psum", [128, 2048], f32)
    SCRATCH["pb"] = ("psum", [128, 2048], f32)


_decl()
LOADS = ["dfl", "dml", "dx", "du", "dv", "dwc", "dws"]
SEMAPHORES = ["cv", "cs_", "ct", "cg", "snt", "outs"] + LOADS + ["a%s%d" % (n, i) for n in "qdl" for i in range(3)]
TF = {n: i for i, n in enumerate(["j16", "m", "fm", "hb", "cb", "mb", "sn", "en", "ple", "ln", "ng", "t1", "w", "hl", "swb", "e1", "q0"])}
STEPS = {"b": ("y1", 0, 4), "f": ("y1", 1, 4), "jt": ("y1", 2, 4), "sw": ("v1", 0, 3), "cf": ("v0", 1, 3), "hf": ("v1", 2, 3)}
TU = {n: i for i, n in enumerate(["tab%d" % k for k in range(9)] + ["m", "root", "root1", "l", "tp", "tpa", "tpb", "T", "b", "last", "k2"])}
TI = {"k": 0, "d": 1, "e": 2}
BIG = float(2 ** 90)
STEP1 = 2.0 ** -10
WHOLE = 3 * 2 ** 22
CYC = 0.83e-3 * np.array([1.25, 1.05, 1.45, 1.4, 1.1])
GEL = 0.83e-3 * np.array([1.56, 1.95, 1.15, 1.9, 1.25])
SCA = 0.05 + 0.83e-3 * C * np.array([3.8, 5.5, 2.0, 2.2, 5.2])
MMS, ISSUE = np.array([0.5, 0.62, 0.38, 0.4, 0.62]), np.array([0.5, 0.95, 0.3, 0.4, 0.9])
WAKES, STARTS, RATES, FARWAKE = [0.15, 0.2, 0.09, 0.2, 0.1], [1.8, 2.8, 1.2, 1.4, 2.6], [0.9, 1.3, 0.6, 0.6, 1.2], 0.6
GUESSES = range(len(WAKES))
ORDER = {}


def rank_program(g, core, T, topo):
    rank = T.rank_of(core)
    if rank is None:
        return
    A = AluOpType
    AF = ActivationFunctionType
    Q = {"v": g.vector, "s": g.scalar, "t": g.tensor, "g": g, "y": g.sync}
    CS = {"v": "cv", "s": "cs_", "t": "ct", "g": "cg"}
    prog = []
    TINY, R2, R4 = 64 * CYC, C // 2 * CYC, C * CYC
    gat = lambda n=C: 0.055 + GEL * n
    GAT = gat()

    def op(eng, fn, reads, writes, cost=TINY, sem=None, inc=1, lat=0.0, remote=None):
        cost = [float(x) for x in cost + 0 * CYC]
        prog.append({"eng": eng, "fn": fn, "r": reads, "w": writes, "c": cost[0], "cs": cost, "sem": sem, "inc": inc, "lat": lat, "remote": remote})

    step = lambda n, k, of: T[n][:, k:of * TW:of]
    tf = lambda n: step(*STEPS[n]) if n in STEPS else T.tf[:, TW * TF[n]:TW * TF[n] + TW]
    tu = lambda n, a=0, b=TW: T.tu[:, TW * TU[n] + a:TW * TU[n] + b]
    ti = lambda n: T.ti[:, TW * TI[n]:TW * TI[n] + TW]
    cl = lambda i: T.col[:, i:i + 1]
    z0, z1, z2 = [(lambda k, n=n: step(n, k, 7)) for n in ("z0", "z1", "z2")]
    both = lambda n: [n + "a", n + "b"]
    SLOT = {"%s%d" % (n, k): (m, C * k) for n, m, z in (("ro", "ro", 9), ("c", "cc", 10), ("gr", "gr", 3), ("x", "c4s", 3), ("fh", "fh", 4), ("ft", "ft", 4), ("fs", "fs", 4),
                                                       ("r2", "r2", 4), ("pp", "pp", 4)) for k in range(z)}

    def row(n, a=0, b=C):
        n, s = SLOT.get(n, (n, 0))
        return T[n][:, s + a:s + b]

    def sampled(n, a=0, b=TW):
        n, s = SLOT.get(n, (n, 0))
        return T[n][:, s + 16 * a + 15:s + 16 * b:16]

    def tt(out, wk, a, b, o, rk, c=TINY):
        op("v", lambda: g.vector.tensor_tensor(out, a, b, o), rk, wk, c)

    def ts(out, wk, a, s1, s2, o0, o1, rk, c=TINY):
        if o1 is None:
            op("v", lambda: g.vector.tensor_scalar(out, a, s1, None, o0), rk, wk, c)
        else:
            op("v", lambda: g.vector.tensor_scalar(out, a, s1, s2, o0, o1), rk, wk, c)

    def cp(out, wk, a, rk, c=TINY):
        op("v", lambda: g.vector.tensor_copy(out, a), rk, wk, c)

    def fill(out, x, wk, c=TINY):
        op("v", lambda: g.vector.memset(out, x), [], wk, c)

    def t2(out, a, b, o):
        tt(tf(out), ["tf." + out], tf(a), tf(b), o, ["tf." + a, "tf." + b])

    def act(out, wk, a, rk, c=GAT, **kw):
        op("s", lambda: g.scalar.activation(out, a, AF.Copy, **kw), rk, wk, c)

    def scan(out, wk, d0, d1, init, o0, o1, rk, c=R4):
        op("v", lambda: g.vector.tensor_tensor_scan(out, d0, d1, init, o0, o1), rk, wk, c)

    def pick(name, win, tab, rk, h, scale=1.0):
        keys = []
        if h:
            act(row(name, 0, 16 * h), [name + "a"], win.indirect(tab(0, h)), rk, gat(16 * h), scale=scale)
            keys.append(name + "a")
        if h < TW:
            ts(row(name, 16 * h, C), [name + "b"], win.indirect(tab(h, TW)), scale, None, A.mult, None, rk, gat(C - 16 * h))
            keys.append(name + "b")
        return keys

    def latch(src, rk, cname, lc="lc", low=-1024.0, c=R2):
        scan(row(cname), both(cname), row(src), row(lc), low, A.max, A.add, rk + [lc], c)

    def tabs(cname, out, wk, col, scale=None):
        if scale:
            ts(out, wk, sampled(cname), scale, cl(col), A.mult, A.add, both(cname) + ["col%d" % col])
        else:
            ts(out, wk, sampled(cname), cl(col), None, A.add, None, both(cname) + ["col%d" % col])

    def load(eng, sem, out, src, key, lat):
        op(eng, lambda: Q[eng].dma_start(out, src), [], [key], 0.07, sem=sem, inc=16, lat=lat)
    load("y", "dfl", T.fl_s[:], T.fl[:], "fl_s", 1.9)
    load("s", "dx", T.xin[:], T.x[:], "xin", 4.2)
    load("y", "dml", T.ml_s[:], T.ml[:], "ml_s", 2.0)
    load("y", "du", T.uin[:], T.u[:], "uin", 2.6)
    load("y", "dwc", T.wq[:, 0:512].bitcast(dt.uint8), T.wc[:], "wq", 3.2)
    load("y", "dws", T.wqs[:, 0:512], T.ws[:], "wqs", 2.4)
    load("y", "dv", T.vin[:], T.v[:], "vin", 2.6)

    def iota(out, wk, pattern, base, cm, n, flag=True, rk=()):
        c = 0.13 + 2 * CYC * n
        if flag:
            op("g", lambda: g.iota(out, pattern, base, cm, allow_small_or_imprecise_dtypes=True), list(rk), wk, c)
        else:
            op("g", lambda: g.iota(out, pattern, base, cm), list(rk), wk, c)
    iota(T.pq[:], ["pq"], [[0, TW]], 0, 1, TW, False)
    iota(T.t16[:], ["t16"], [[1, 16]], 0, 0, 16)
    iota(T.ramp[:], ["ramp"] + both("ramp"), [[1, C + 16]], -224, 0, C + 16, rk=[">pq", ">t16"])
    iota(tf("j16"), ["tf.j16"], [[16, TW]], 0, 0, TW, rk=[">ramp"])
    iota(T.ofi[:], ["ofi"], [[16, 8]], 0, 0, 8, False, rk=[">ramp"])
    for out, x, wk, n in [(T.y1[:], 2 ** 20, ["y1", "tf.f", "tf.b", "tf.jt"], 4 * TW), (step("y0", 0, 4), 2 ** 20, ["y00"], TW),
                          (T.v0[:], 1, ["v0", "tf.cf"], 3 * TW), (step("v0", 0, 3), 0, ["v0"], TW), (T.v1[:], 0, ["v1", "tf.hf", "tf.sw"], 3 * TW),
                          (T.z0[:], 1, ["z0"], 7 * TW), (z0(0), 0, ["z0"], TW), (z0(3), -1, ["z0"], TW), (T.z1[:], WHOLE, ["z1%d" % k for k in range(7)], 7 * TW),
                          (T.rst[:, 0:1], 0, ["rst0"], 1), (T.rs2[:, 0:1], 4, ["rs20"], 1)]:
        iota(out, wk, [[0, n]], x, 0, n, rk=[">tf.j16", ">ofi"])
    iota(T.et[:], ["et"], [[0, 2048]], 0, 0, 2048, rk=[">y1", ">y00", ">v0", ">v1", ">z0", ">z10", ">rst0", ">rs20"])
    act(row("k0m"), both("k0m"), row("ramp"), ["ramp"], R4, bias=-STEP1)
    fill(T.ends[:, 0:1], BIG, ["ends0"])
    fill(T.cum[:, 0:1], -224.0 * STEP1, ["cum0"])
    ts(T.pqm[:], ["pqm"], T.pq[:], 15, None, A.bitwise_and, None, ["pq", ">ends0", ">cum0"])
    cp(cl(0), ["col0"], T.pqm[:, 0:1], ["pqm"])
    cp(T.ofq[:], ["ofq"], T.pqm[:], ["pqm"])
    ts(T.t16[:], ["t16"], T.t16[:], cl(0), None, A.subtract, None, ["t16", "col0"])
    ts(T.la16[:], ["la16"], T.t16[:], 0.0, -1024.0, A.is_lt, A.mult, ["t16"])
    ts(T.lb16[:], ["lb16"], T.t16[:], 0.0, 512.0, A.is_equal, A.mult, ["t16"])
    ts(T.lc16[:], ["lc16"], T.t16[:], 15.0, -1024.0, A.is_equal, A.mult, ["t16"])
    tt(T.la16[:], ["la16"], T.la16[:], T.lb16[:], A.add, ["la16", "lb16"])
    tt(T.lc16[:], ["lc16"], T.la16[:], T.lc16[:], A.add, ["la16", "lc16"])
    cp(row("lc"), ["lc"], T.lc16[:].indirect(T.ofq[:]), ["lc16", "ofq"], GAT)
    ts(cl(1), ["col1"], cl(0), 0.0, 1024.0, A.is_equal, A.mult, ["col0"])
    ts(cl(2), ["col2"], cl(1), 224.0 - 512.0, None, A.add, None, ["col1"])
    for k, (a, b) in enumerate([(1024.0, 511.0), (1.0, 511.0 / 1024 + 0.01), (1.0, 511.0 / 1024 + 1.01), (1.0, 0.01), (-2.0, 449.0), (1.0, -1.0), (-0.5, -0.5), (4.0, 3.0), (-1.0, -0.5)], 3):
        ts(cl(k), ["col%d" % k], cl(2), a, b, A.mult, A.add, ["col2"])
    fill(T.ends[:, 1:C], 2.0 ** -19, ["ends"], R2)
    fill(T.half[:], 0.5, ["half"])
    fill(step("y0", 1, 4), -0.5, ["y01"])
    fill(step("y0", 2, 4), 0.25, ["y02"])
    for b in range(4):
        op("g", lambda b=b: g.affine_select(T.et[:, 512 * b + b:512 * b + 512:4], T.half[:], [[1, 128]], A.is_equal, 0.0, 0, -1), ["et", "half"], ["et%d" % b], 0.17 + 256 * CYC)
    op("g", lambda: g.affine_select(row("lcp"), row("lc"), [[0, C]], A.is_equal, 0.0, 0, 0), ["lc", ">et3"], ["lcp"], 0.17 + 2 * C * CYC)
    cp(tu("tab0"), ["tu.tab0"] + both("tu.tab0"), T.fl_s[:], ["fl_s", ">ends", ">half", ">y01", ">y02"] + [">col%d" % k for k in range(3, 12)])

    KS, KM = ["ka", "kb"], ["kma", "kmb"]
    parts = lambda two: [("a", 0, TW // 2), ("b", TW // 2, TW)] if two else [("ab", 0, TW)]
    some = lambda n, h: [n + x for x in h]

    def levels(first):
        rows = 7 if first else 8
        act(row("ro0"), both("ro0"), T.ramp[:].indirect(tu("tab0")), ["ramp"] + both("tu.tab0"))
        for k in range(9):
            tab, nxt = "tab%d" % min(k, rows), "tab%d" % (k + 1)
            a, b = "ro%d" % k, "ro%d" % (k + 1)
            src = "ramp" if k == 0 else KS[k % 2]
            sm = "k0m" if k == 0 else KM[k % 2]
            dst, dm = KS[(k + 1) % 2], KM[(k + 1) % 2]
            c = "c%d" % (k % 2)
            if k > rows:
                act(row("yk"), ["yk"], row(src).indirect(tu(tab)), both(src) + both("tu." + tab))
                src = "yk"
            for h, x, y in parts(first) if k < rows else []:
                act(row(b, 16 * x, 16 * y), some(b, h), row(a).indirect(tu(tab, x, y)), both(a) + some("tu." + tab, h), gat(16 * (y - x)))
            for h, x, y in parts(True) if first or k > 1 else []:
                tt(row(dst, 16 * x, 16 * y), some(dst, h), row(src).indirect(tu(tab, x, y)), row(sm, 16 * x, 16 * y), A.min,
                   [src] + both(src) + some(sm, h) + some("tu." + tab, h), gat(16 * (y - x)))
            if k == 8:
                break
            for h, x, y in parts(first) if k < rows else []:
                scan(row(c, 16 * x, 16 * y), some(c, h), row(b, 16 * x, 16 * y), row("lc", 16 * x, 16 * y), -1024.0, A.max, A.add, some(b, h) + ["lc"], 8 * (y - x) * CYC)
                ts(tu(nxt, x, y), some("tu." + nxt, h), sampled(c, x, y), cl(2), None, A.add, None, some(c, h) + ["col2"])
            if k == 0 and not first:
                scan(T.y2[:], ["y2"], T.y0[:], T.y1[:], 0.0, A.add, A.min, ["y00", "y01", "y02", "y03", "y1", "tf.b", "tf.f", "tf.jt"], 4 * TW * CYC)
                tt(tf("q0"), ["tf.q0"], step("y2", 3, 4), sampled(c), A.min, ["y2"] + both(c))
                ts(tu("k2"), ["tu.k2"], tf("q0"), 4.0, cl(10), A.mult, A.add, ["tf.q0", "col10"])
                act(row(KS[0]), both(KS[0]), T.kw[:].indirect(tu("k2")), ["kw", "tu.k2"], scale=STEP1)
            for h, x, y in parts(True) if first or k > 0 else []:
                act(row(dm, 16 * x, 16 * y), some(dm, h), row(dst, 16 * x, 16 * y), some(dst, h), 16 * (y - x) * CYC, bias=-STEP1 * 2 ** (k + 1))

    KF = KS[1]

    def send(r, o, i, rk, wk, sem, lat):
        dst = T.cores[rank ^ STEP[r]]
        rid, pid = topo.addr(dst)[0:2]
        m = topo.mask(core, dst)
        n = len(topo.engines(core, dst))
        op("g", lambda: g.remote_dma(out_ap=o, in_ap=i, remote_sem=T.sem[sem], local_sem=T.sem.snt, pid=pid, routing_id=rid, dma_engine_mask=m),
           rk, wk, ISSUE, lat=lat, remote=(sem, n))

    sp = lambda r, x, a=0, b=TW: T.sp[:, TW * (4 * r + "dpla".index(x)) + a:TW * (4 * r + "dpla".index(x)) + b]

    def landed(r, x):
        p = [y for y in PARCELS if x in y][0]
        return T["l%s%d" % (p[0], r)][:, TW * p.index(x):TW * p.index(x) + TW]

    def finish(r):
        nxt = "tab1" if r else "tab0"
        kd, kp, kl, ka = ["sp%d%s" % (r, x) for x in "dpla"]
        tt(row("yk"), ["yk"], row(KF).indirect(tu(nxt)), row("kc"), A.max, both(KF) + both("tu." + nxt) + ["kc"], GAT)
        for h, x, y in parts(True):
            scan(row("ck", 16 * x, 16 * y), some("ck", h), row(KF, 16 * x, 16 * y), row("lc", 16 * x, 16 * y), -1024.0, A.max, A.add, some(KF, h) + ["lc"], 16 * (y - x) * CYC)
        tabs("ck", tu("root1"), ["tu.root1"], 5)
        tabs("ck", tu("root"), ["tu.root"], 4)
        tabs("ck", ti("k"), ["ti.k"], 3, 1024.0)
        ts(ti("d"), ["ti.d"], ti("k"), 511, None, A.bitwise_and, None, ["ti.k"])
        cp(sp(r, "d"), [kd], ti("d"), ["ti.d"])
        act(row("drow"), ["drow"], row("ends").indirect(sp(r, "d")), ["ends", "ends0", kd])
        scan(T.cum[:, 1:C + 1], ["cum"], row("yk"), row("kc"), -224.0 * STEP1, A.add, A.subtract, ["yk", "kc"])
        ke = pick("erow", T.cum[:, 0:C + 1], lambda a, b: tu("root1", a, b), ["cum", "cum0", "tu.root1"], OPT["HE"], 1024.0)
        act(row("srow"), ["srow"], T.cum[:, 0:C + 1].indirect(tu("root")), ["cum", "cum0", "tu.root"], scale=1024.0)
        tt(sampled("lcp"), ["lcp"], sampled("lc"), ti("d"), A.subtract, ["lc", "ti.d"])
        latch("erow", ke, "c2", "lcp")
        tabs("c2", sp(r, "p"), [kp], 8)
        op("v", lambda: g.vector.tensor_copy(row("cp").indirect(sp(r, "p")), row("code9")), ["code9", kp], ["cp"], SCA)
        tt(tf("en"), ["tf.en"], sampled("c2"), ti("d"), A.add, both("c2") + ["ti.d", ">cp"])
        latch("srow", ["srow", ">cp"], "c3")
        tt(tf("ln"), ["tf.ln"], tf("en"), sampled("c3"), A.subtract, both("c3") + ["tf.en"])
        cp(sp(r, "l"), [kl], tf("ln"), ["tf.ln"])
        latch("cp", ["cp"], "c4", "lc9", -2.0)
        tabs("c4", sp(r, "a"), [ka], 2, 512.0)
        for p in PARCELS:
            send(r, T["l%s%d" % (p[0], r)][:], sp(r, p[0], 0, TW * len(p)), ["sp%d%s" % (r, x) for x in p], ["l%d%s" % (r, x) for x in p], "a%s%d" % (p[0], r), 0.12 * len(p))
        ts(tu("last"), ["tu.last"], tf("en"), cl(8), None, A.add, None, ["tf.en", "col8"])

    def mm(dst, b, st, so, mv, a=0, z=C, rk=None):
        op("t", lambda: g.tensor.matmul_mx(T[dst][:, 512 * b:512 * b + z - a], T[st][:, so:so + 128], T[st + "s"][:, so:so + 128], T[mv][:, a:z], T[mv + "s"][:, a:z], True, True),
           [st, st + "s"] + (rk or [mv, mv + "s"]), [dst + str(b)], MMS * (z - a + 16) / (C + 16))

    def quant(tile, keys, w, q, a=0, wk=None):
        op("v", lambda: g.vector.quantize_mx(T[q][:, a:a + w], T[q + "s"][:, a:a + w], T[tile][:, 4 * a:4 * (a + w)]), keys, wk or [q, q + "s"], (14.5 + 1.06 * w) * CYC)

    def state_made(r):
        q, l = "qx%d" % r, "lq%d" % r
        send(r, T[l][:].bitcast(dt.uint8), T[q][:].bitcast(dt.uint8), [q], [l], "aq%d" % r, 3.8)
        send(r, T[l + "s"][:], T[q + "s"][:], [q + "s"], [l + "s"], "aq%d" % r, 1.0)
        mm("pb", 0, "qur", 0, q)
        act(row("sr"), ["sr"], T.pb[:, 0:C], ["pb0"], R4, scale=-1.0)
        for b in range(4):
            mm("pa", b, "qe", 128 * b, q)
        for b in range(4):
            mm("pb", b, "qe", 128 * b, l)

    def halves(x, y, h, c):
        t2(h, x, y, A.add)
        ts(tf(h), ["tf." + h], tf(h), 0.5, None, A.mult, None, ["tf." + h])
        t2(c, x, h, A.subtract)

    levels(True)
    cp(tu("m"), ["tu.m"], T.ml_s[:], ["ml_s"])
    cp(tf("f"), ["tf.f"], T.fl_s[:], ["fl_s"])
    cp(tf("m"), ["tf.m"], T.ml_s[:], ["ml_s"])
    act(row("fmr"), ["fmr"], row("ro0").indirect(tu("m")), both("ro0") + ["tu.m", ">ro7b"])
    latch("fmr", ["fmr"], "c8")
    tabs("c8", tf("fm"), ["tf.fm"], 2)
    halves("f", "fm", "hf", "cf")
    ts(tf("jt"), ["tf.jt"], tf("j16"), cl(0), None, A.add, None, ["tf.j16", "col0"])
    ts(step("y0", 3, 4), ["y03"], tf("j16"), 0.0, cl(11), A.mult, A.add, ["tf.j16", "col11"])
    t2("sn", "jt", "m", A.is_lt)
    ts(z1(5), ["z15"], tf("sn"), -float(C), float(C), A.mult, A.add, ["tf.sn"])
    ts(z1(6), ["z16"], tf("sn"), 2.0 * C, -float(C), A.mult, A.add, ["tf.sn"])
    quant("xin", ["xin"], C, "qx0")
    quant("uin", ["uin"], 128, "qu")
    cp(T.ofu[:], ["ofu"], T.ofi[:], ["ofi"])
    op("v", lambda: g.vector.tensor_copy(T.qur[:, 0:128].bitcast(dt.uint32), T.qu[:, 0:128].bitcast(dt.uint32).indirect(T.ofu[:, 0:8])), ["qu", "ofu"], ["qur"], gat(128))
    op("s", lambda: g.scalar.activation(T.qurs[:, 0:128], T.qus[:, 0:128].indirect(T.ofu[:, 0:8]), AF.Copy), ["qus", "ofu"], ["qurs"], gat(128))
    quant("et", ["et0", "et1", "et2", "et3"], 512, "qe")
    state_made(0)
    act(row("kc"), ["kc"], row("ramp"), ["ramp", ">ro7b"], R4, bias=-0.5)
    act(row("code9"), ["code9"], row("ramp"), ["ramp", ">kc"], R4, scale=2.0 ** -9)
    act(row("lc9"), ["lc9"], row("lc"), ["lc", ">kc"], R4, scale=2.0 ** -9)
    finish(0)
    iota(T.kw[:], ["kw"], [[1024, C], [1, 4]], -3 - 224 * 1024, 0, 4 * C, rk=[">l0a"])
    ts(tf("ple"), ["tf.ple"], sampled("c2"), -1.0, None, A.add, None, both("c2"))
    tt(tf("e1"), ["tf.e1"], tf("ple"), sampled("c3"), A.is_equal, ["tf.ple"] + both("c3"))
    t2("e1", "e1", "ln", A.mult)
    t2("e1", "e1", "ple", A.add)
    ts(tu("b"), ["tu.b"], tf("e1"), cl(8), None, A.add, None, ["tf.e1", "col8"])
    act(row("brow"), ["brow"], row("cp").indirect(tu("b")), ["cp", "tu.b"], scale=512.0)
    latch("brow", ["brow"], "c7")
    tabs("c7", tu("b"), ["tu.b"], 2)
    tabs("c7", tf("b"), ["tf.b"], 2)
    act(row("mrow"), ["mrow"], T.ramp[:].indirect(tu("m")), ["ramp", "tu.m", ">ro7b"])
    act(row("mbr"), ["mbr"], row("mrow").indirect(tu("b")), ["mrow", "tu.b"])
    latch("mbr", ["mbr"], "c8")
    tabs("c8", tf("mb"), ["tf.mb"], 2)
    halves("b", "mb", "hb", "cb")

    def store(eng, out, src, keys, lat=2.0):
        op(eng, lambda: Q[eng].dma_start(out, src), keys, [], 0.07, sem="outs", inc=16, lat=lat)

    marks = []
    for r in range(3):
        ks = "sp%da" % r
        last = r == 2
        marks.append(len(prog))
        act(T.rst[:, 1:C + 1], ["rst"], row("drow").indirect(sp(r, "a")), ["drow", ks], bias=-BIG / 2)
        act(T.rs2[:, 1:C + 1], ["rs2"], row("drow").indirect(sp(r, "a")), ["drow", ks])
        cp(row("sa"), both("sa"), row("sr").indirect(sp(r, "a")), ["sr", ks], GAT)
        scan(row("pm"), ["pm"], row("rst"), row("sa"), BIG, A.max, A.min, ["rst", "rst0"] + both("sa"))
        tt(row("neq"), ["neq"], row("pm").indirect(tu("last")), row("sr"), A.not_equal, ["pm", "tu.last", "sr"], GAT)
        tt(row("cand"), ["cand"], row("neq").indirect(sp(r, "a")), row("cp"), A.add, ["neq", ks, "cp"], GAT)
        scan(row("pm"), ["pm"], row("rs2"), row("cand"), 0.0, A.add, A.min, ["rs2", "rs20", "cand"])
        latch("sa", pick("sa", row("pm"), lambda a, b: tu("last", a, b), ["pm", "tu.last"], OPT["HL"], 512.0), "ck", c=R4)
        tabs("ck", tu("l"), ["tu.l"], 6)
        ts(ti("k"), ["ti.k"], sampled("ck"), cl(2), 1024.0, A.add, A.mult, both("ck") + ["col2"])
        ts(ti("e"), ["ti.e"], ti("k"), 1023, None, A.bitwise_and, None, ["ti.k"])
        for b in range(4):
            act(row("fh%d" % b), ["fh%d" % b], T.pa[:, 512 * b:512 * b + C], ["pa%d" % b], R4)
        for x, n in zip("dlpa", ["tdrow", "lenrow", "tprow", "ar"]):
            act(row(n), [n], T.ramp[:].indirect(landed(r, x)), ["ramp", "l%d%s" % (r, x)])
        for i, (n, h) in enumerate([("lenrow", 0), ("tdrow", TW), ("tprow", TW)]):
            latch("gr%d" % i, pick("gr%d" % i, row(n), lambda a, b: tu("l", a, b), [n, "tu.l"], h), "x%d" % i)
        for b in range(4):
            if b >= OPT["FTV"]:
                act(row("ft%d" % b), ["ft%d_0" % b], T.pb[:, 512 * b:512 * b + C], ["pb%d" % b], R4)
                continue
            for x in range(0, C, C // 4):
                cp(row("ft%d" % b, x, x + C // 4), ["ft%d_%d" % (b, x)], T.pb[:, 512 * b + x:512 * b + x + C // 4], ["pb%d" % b], C // 4 * CYC)
        ts(z0(4), ["z04"], sampled("x0"), cl(2), None, A.add, None, both("x0") + ["col2", "z0"])
        op("v", lambda: g.vector.reciprocal(z0(2), z0(4)), ["z04", "z0"], ["z02"], 0.19 + 6 * TW * CYC)
        tabs("x0", tf("hl"), ["tf.hl"], 9, 0.5)
        tt(tf("ng"), ["tf.ng"], ti("e"), ti("d"), A.is_lt, ["ti.e", "ti.d"])
        tt(tf("w"), ["tf.w"], ti("e"), ti("d"), A.subtract, ["ti.e", "ti.d"])
        t2("t1", "ng", "ln", A.mult)
        tt(z1(1), ["z11"], tf("w"), tf("t1"), A.add, ["tf.w", "tf.t1"])
        tt(z1(0), ["z10"], tf("hl"), sampled("x1"), A.subtract, both("x1") + ["tf.hl"])
        tt(z1(4), ["z14"], z1(1), sampled("x2"), A.add, both("x2") + ["z11"])
        scan(T.z2[:], ["z2"], T.z0[:], T.z1[:], 0.0, A.mult, A.add, ["z0", "z02", "z04"] + ["z1%d" % k for k in range(7)], 7 * TW * CYC)
        for k, x in ((5, "tpa"), (6, "tpb"), (4, "tp")):
            ts(tu(x), ["tu." + x], z2(k), cl(2), None, A.add, None, ["z2", "col2"])
        latch("trow", pick("trow", row("ar"), lambda a, b: tu("tp", a, b), ["ar", "tu.tp"], OPT["HT"] if last else TW), "c6")
        tabs("c6", tu("T"), ["tu.T"], 2)
        act(row("sfa"), ["sfa"], row("sr").indirect(landed(r, "a")), ["sr", "l%da" % r])
        act(row("sfa", C, 2 * C), ["sfb"], row("sfa"), ["sfa"], R4, scale=-1.0)
        cp(row("mu"), ["mu"], T.sfa[:].indirect(tu("tpa")), ["sfa", "sfb", "tu.tpa"], GAT)
        act(row("nu"), ["nu"], T.sfa[:].indirect(tu("tpb")), ["sfa", "sfb", "tu.tpb"])
        tt(row("sw"), ["sw"], row("mu").indirect(tu("m")), row("nu"), A.is_gt, ["mu", "nu", "tu.m"], GAT)
        latch("sw", ["sw"], "c9")
        tabs("c9", tf("sw"), ["tf.sw"], 7, -2.0)
        scan(T.v2[:], ["v2"], T.v0[:], T.v1[:], 0.0, A.mult, A.add, ["v0", "v1", "tf.cf", "tf.hf", "tf.sw"], 3 * TW * CYC)
        if not last:
            cp(tf("cf"), ["tf.cf"], step("v2", 1, 3), ["v2"])
            cp(tf("f"), ["tf.f"], step("v2", 2, 3), ["v2"])
        cp(tu("tab0"), ["tu.tab0"] + both("tu.tab0"), step("v2", 2, 3), ["v2"])
        latch("swb", pick("swb", row("sw"), lambda a, b: tu("b", a, b), ["sw", "tu.b"], TW if last else OPT["HB"]) + [">tu.tab0"], "c7")
        tabs("c7", tf("swb"), ["tf.swb"], 7, -2.0)
        t2("cb", "swb", "cb", A.mult)
        t2("b", "hb", "cb", A.add)
        cp(tu("b"), ["tu.b"], tf("b"), ["tf.b"])
        if not last:
            levels(False)
        for b in range(4):
            act(row("fs%d" % b), ["fs%d" % b], row("ft%d" % b).indirect(tu("T")), ["ft%d_%d" % (b, x) for x in range(0, C, C // 4)] + ["tu.T"])
        cuts = OPT["ZCUT"] if last else [0, TW]
        for h, (a, z) in enumerate(zip(cuts, cuts[1:])):
            n = 16 * (z - a)
            for b in range(4):
                tt(T.zt[:, 64 * a + b:64 * z:4], ["zt%d%d" % (h, b)], row("fh%d" % b).indirect(tu("tab0", a, z)), row("fs%d" % b, 16 * a, 16 * z), A.add,
                   ["fh%d" % b, "fs%d" % b, "tu.tab0"], gat(n))
            quant("zt", ["zt%d%d" % (h, b) for b in range(4)], n, "qz", 16 * a, ["qz%d" % h])
            for b in range(4):
                k = (b + 2 * h) % 4
                mm("pb", k, "wq", 128 * b, "qz", 16 * a, 16 * z, ["qz%d" % h])
                act(row("r2%d" % b, 16 * a, 16 * z), ["r2%d%d" % (h, b)], T.pb[:, 512 * k:512 * k + n], ["pb%d" % k], n * CYC, scale=0.015625)
        if last:
            quant("vin", ["vin", ">qz0"], 128, "qv")
        for h, (a, z) in enumerate(zip(OPT["XCUT"], OPT["XCUT"][1:]) if last else [(0, TW)]):
            n = 16 * (z - a)
            for b in range(4):
                out, src, rk = T.xt[:, 64 * a + b:64 * z:4], row("r2%d" % b).indirect(tu("b", a, z)), ["r20%d" % b, "r21%d" % b, "tu.b"]
                if h and b >= 4 - OPT["NL"]:
                    act(row("pp%d" % b, 0, n), ["pp%d" % b], src, rk, gat(n))
                    tt(out, ["xt%d%d" % (h, b)], row("pp%d" % b, 0, n), T.pa[:, 512 * b + 16 * a:512 * b + 16 * z], A.add, ["pp%d" % b, "pa%d" % b], n * CYC)
                else:
                    tt(out, ["xt%d%d" % (h, b)], src, row("fh%d" % b, 16 * a, 16 * z), A.add, rk + ["fh%d" % b], gat(n))
            keys = ["xt%d%d" % (h, b) for b in range(4)]
            if not last:
                quant("xt", keys, C, "qx%d" % (r + 1))
                continue
            q = "qx3%d" % h
            quant("xt", keys, n, "qx3", 16 * a, [q])
            mm("pb", h, "qv", 0, "qx3", 16 * a, 16 * z, [q])
            store("y", T.oc[:, 64 * a:64 * z], T.qx3[:, 16 * a:16 * z].bitcast(dt.uint8), [q], 1.8 + n / 400)
            act(row("sa", 16 * a, 16 * z), ["y%d_" % h] + both("sa"), T.pb[:, 512 * h:512 * h + n], ["pb%d" % h], n * CYC)
            store("s", T.y[:, 16 * a:16 * z], row("sa", 16 * a, 16 * z), ["y%d_" % h], 1.8 + n / 400)
        if last:
            break
        state_made(r + 1)
        finish(r + 1)
    act(row("nlr"), ["nlr"], T.ramp[:].indirect(tu("tab0")), ["ramp", "tu.tab0"], bias=224.0)
    store("y", T.nl[:], T.nlr[0:128:16, :], ["nlr"])
    for k in range(4):
        store("y", T.osc[4 * k:4 * k + 4, :], T.qx3s[32 * k:32 * k + 4, 0:C], ["qx30", "qx31"])

    n = len(prog)
    deps, kids = [set() for _ in range(n)], [[] for _ in range(n)]
    lw, rd = {}, {}
    for i, p in enumerate(prog):
        for k in p["r"]:
            if k[0] == ">":
                deps[i].add(lw[k[1:]])
            elif k in lw:
                deps[i].add(lw[k])
        for k in p["w"]:
            if k in lw:
                deps[i].add(lw[k])
            deps[i].update(rd.get(k, []))
        for k in p["r"]:
            rd.setdefault(k, []).append(i)
        for k in p["w"]:
            lw[k], rd[k] = i, []
        deps[i].discard(i)
        for d in deps[i]:
            kids[d].append(i)
    dl, far = [list(d) for d in deps], [bool(p["remote"]) for p in prog]
    lat, cost = [p["lat"] for p in prog], [[p["cs"][m] for p in prog] for m in GUESSES]

    def lay(rank_):
        at, done, left, tq, link = [0.0] * n, [0.0] * n, [len(x) for x in deps], {e: 0.0 for e in Q}, 0.0
        ready = {e: [] for e in Q}
        for i in range(n):
            if not left[i]:
                ready[prog[i]["eng"]].append((0.0, i))
        for _ in range(n):
            t0, e = min((max(tq[e], min(ready[e])[0]), e) for e in Q if ready[e])
            a, i = min((x for x in ready[e] if x[0] <= t0 + OPT["LOOK"]), key=lambda x: (rank_[x[1]], x[1]))
            soon = [x for x in ready[e] if rank_[x[1]] < rank_[i] and x[0] - t0 + cost[0][x[1]] < OPT["KAP"] * cost[0][i]]
            if soon:
                a, i = min(soon)
            ready[e].remove((a, i))
            at[i] = max(t0, a)
            tq[e] = at[i] + cost[0][i]
            done[i] = tq[e] + lat[i] + WAKES[0]
            if far[i]:
                link = max(link, tq[e] + STARTS[0]) + lat[i]
                done[i] = link + FARWAKE + WAKES[0]
            for k in kids[i]:
                left[k] -= 1
                if not left[k]:
                    ready[prog[k]["eng"]].append((max(done[d] for d in deps[k]), k))
        return at, done

    def clock_of(seq, m, old=None, since=0.0):
        c, wake, start, rate = cost[m], WAKES[m], STARTS[m], RATES[m]
        at, done, by, link, left = [0.0] * n, [-1.0] * n, [-1] * n, 0.0, n
        state = [[q, 0, 0.0] for q in seq.values()]
        for st in state if old else []:
            q, pos = st[0], 0
            while pos < len(q) and old[0][q[pos]] < since:
                i = q[pos]
                at[i], done[i], by[i] = old[0][i], old[1][i], old[2][i]
                if far[i]:
                    link = done[i] - FARWAKE - wake
                pos += 1
            if pos:
                st[1], st[2] = pos, at[q[pos - 1]] + c[q[pos - 1]]
                left -= pos
        while left:
            before = left
            for st in state:
                q, pos, t = st
                while pos < len(q):
                    i = q[pos]
                    t1, who = t, q[pos - 1] if pos else -1
                    for d in dl[i]:
                        x = done[d]
                        if x > t1:
                            t1, who = x, d
                        elif x < 0:
                            break
                    else:
                        at[i], by[i] = t1, who
                        t = t1 + c[i]
                        if far[i]:
                            link = max(link, t + start) + lat[i] * rate
                            done[i] = link + FARWAKE + wake
                        else:
                            done[i] = t + lat[i] + wake
                        pos += 1
                        left -= 1
                        continue
                    break
                st[1], st[2] = pos, t
            if left == before:
                return None
        return at, done, by

    if "seq" not in ORDER:
        span = [cost[0][i] + lat[i] + WAKES[0] + far[i] * (STARTS[0] + FARWAKE) for i in range(n)]
        prio = [0.0] * n
        for i in range(n - 1, -1, -1):
            prio[i] = span[i] + max([prio[k] for k in kids[i]] + [0.0])
        total = lambda runs: sum(max(x[1]) for x in runs)
        seed = [OPT["SEED"]]

        def draw(k):
            seed[0] = (seed[0] * 1103515245 + 12345) % 2 ** 31
            return (seed[0] >> 8) % k

        def laid(pr):
            at, done = lay([-x for x in pr])
            order = sorted(range(n), key=lambda i: (at[i], i))
            seq = {e: [i for i in order if prog[i]["eng"] == e] for e in Q}
            return max(done) + sum(max(clock_of(seq, m)[1]) for m in GUESSES[1:]), seq, at, order

        kept, pr = None, list(prio)
        for _ in range(OPT["PASS"] + 1):
            new = laid(pr)
            if kept is None or new[0] < kept[0]:
                kept, prio = new, list(pr)
            tail, behind = [0.0] * n, {}
            for i in reversed(new[3]):
                own = span[i] + max([tail[k] for k in kids[i]] + [0.0])
                tail[i] = max(own, cost[0][i] + behind.get(prog[i]["eng"], 0.0))
                behind[prog[i]["eng"]] = tail[i]
                pr[i] += OPT["ALPHA"] * (own - pr[i])
        kinds = {}
        for i, p in enumerate(prog):
            kinds.setdefault(p["w"][0].rstrip("0123456789") if p["w"] else "", []).append(i)
        kinds = list(kinds.values())
        for _ in range(OPT["KINDS"]):
            pr, more = list(prio), [-4.0, -2.0, -1.0, -0.4, 0.4, 1.0, 2.0, 4.0][draw(8)]
            for i in kinds[draw(len(kinds))]:
                pr[i] += more
            new = laid(pr)
            if new[0] <= kept[0]:
                kept, prio = new, pr
        OPT["MID"] = kept[0] / 3
        seq = {e: list(q) for e, q in kept[1].items()}
        runs = [clock_of(seq, m) for m in GUESSES]
        twin = marks[1] - marks[0]

        def chain_of(run):
            i, chain = run[1].index(max(run[1])), []
            while run[2][i] >= 0:
                chain.append(i)
                i = run[2][i]
            return chain, [i for i in chain if run[2][i] not in deps[i]]

        ends, chains = [max(x[1]) for x in runs], {}
        for it in range(OPT["TRIES"]):
            m = draw(len(runs))
            if m not in chains:
                chains[m] = chain_of(runs[m])
            at, (chain, pairs) = runs[m][0], chains[m]
            if draw(10) < 6:
                i = pairs[draw(len(pairs))]
                q = seq[prog[i]["eng"]]
                a, hop = q.index(i), [1, 1, 2, 3, 5, 9][draw(6)]
                a, b = (a, max(0, a - hop)) if draw(2) else (a - 1, min(len(q) - 1, a - 1 + hop))
            else:
                t, q = at[chain[draw(len(chain))]], seq["vs"[draw(2)]]
                a, b = 0, len(q)
                while a < b:
                    a, b = ((a + b) // 2 + 1, b) if at[q[(a + b) // 2]] < t else (a, (a + b) // 2)
                a = min(len(q) - 1, max(0, a + draw(9) - 6))
                b = min(len(q) - 1, max(0, a + draw(7) - 3))
            i, j = q[a], q[b]
            if a == b or any(x in deps[i] for x in q[b:a]) or any(i in deps[x] for x in q[a + 1:b + 1]):
                continue
            was = list(q)
            q.insert(b, q.pop(a))
            for lo, hi, shift in ((marks[0], marks[1], twin), (marks[1], marks[2], -twin)) if draw(10) < 8 else ():
                if lo <= i < hi and lo <= j < hi:
                    q.remove(i + shift)
                    q.insert(q.index(j + shift) + (b > a), i + shift)
            allow = -(OPT["HEAT"] * (1.0 - it / OPT["TRIES"]) + 0.01) * math.log((draw(9999) + 1) / 10000)
            k = next((x for x, y in zip(was, q) if x != y), q[-1])
            new, more = [], 0.0
            for m in GUESSES:
                run = clock_of(seq, m, runs[m], runs[m][0][k])
                more += max(run[1]) - ends[m] if run else 99.0
                if more > allow * (m + 2) / (len(runs) + 1) + 0.1 * (len(runs) - 1 - m):
                    break
                new.append(run)
            if len(new) == len(runs):
                runs, ends, chains = new, [max(x[1]) for x in new], {}
                if sum(ends) < kept[0]:
                    kept = (sum(ends), {e: list(z) for e, z in seq.items()}, runs[0][0])
            else:
                q[:] = was
        ORDER["seq"] = kept
    at = ORDER["seq"][2]
    place = {i: k for q in ORDER["seq"][1].values() for k, i in enumerate(q)}
    order = sorted(range(n), key=lambda i: (at[i], place[i]))
    OPT["EST"] = ORDER["seq"][0] / 3
    OPT["DBG"] = (prog, None, kids, at)

    cnt = {s: 0 for s in SEMAPHORES}
    known = {e: {} for e in Q}
    clock, lastw, readers = {}, {}, {}

    def need(eng, ds):
        most = {}
        for s, v in ds:
            most[s] = max(most.get(s, 0), v)
        own = CS.get(eng)
        for s in sorted(most, key=lambda x: (x == own, x)):
            if known[eng].get(s, 0) >= most[s]:
                continue
            Q[eng].wait_ge(T.sem[s], most[s])
            for x, y in clock[(s, most[s])].items():
                known[eng][x] = max(known[eng].get(x, 0), y)

    whole = {"aq%d" % i: 2 for i in range(3)}
    for i in order:
        p = prog[i]
        ds = []
        for k in p["r"]:
            if k in lastw:
                ds.append(lastw[k])
        if p["remote"]:
            need("g", ds)
            p["fn"]()
            sem, m = p["remote"]
            cnt["snt"] += m
            cnt[sem] += m
            me = (sem, m * whole.get(sem, 1))
            clock[me] = {sem: me[1]}
            for k in p["w"]:
                lastw[k] = me
            continue
        for k in p["w"]:
            if k in lastw:
                ds.append(lastw[k])
            ds += readers.get(k, [])
        need(p["eng"], ds)
        s = p["sem"] or CS[p["eng"]]
        cnt[s] += p["inc"]
        p["fn"]().then_inc(T.sem[s], p["inc"])
        me = (s, cnt[s])
        clock[me] = dict(known[p["eng"]])
        clock[me][s] = cnt[s]
        for k in p["r"]:
            readers.setdefault(k, []).append(me)
        for k in p["w"]:
            lastw[k] = me
            readers[k] = []
    for s in SEMAPHORES:
        if cnt[s] and known["g"].get(s, 0) < cnt[s]:
            g.wait_ge(T.sem[s], cnt[s])
